import numpy as np, ml_dtypes
CORES = [1,5,17,21,33,37,49,53]
N = 8
BF = ml_dtypes.bfloat16
def gentries(a):
    return np.ascontiguousarray(a.reshape(8, 16, -1).transpose(0, 2, 1)).reshape(8, -1)
def gtable(e):
    e = np.asarray(e); return np.ascontiguousarray(e.reshape(8, -1, 16).transpose(0, 2, 1)).reshape(128, -1).astype(np.int32)
def f(rng, *shape):
    return (rng.standard_normal(shape, dtype=np.float32) * np.exp2(rng.integers(-2, 3, shape[:-1] + (1,)))).astype(BF)
def wide(rng, *shape):
    v = f(rng, *shape).astype(np.float32); k = shape[:-2] + (1, shape[-1])
    return (v * np.exp2(rng.integers(-6, 7, k)) * (rng.random(k) > 0.0625)).astype(BF)
V, B, CAP, RO, HI, LO, M = 928, 48, 208, 5, 10, 5, 8192
FP = (N - 1) * B
def face(x, y, fs):
    p = np.zeros(4 * V, np.int64); p[x] = y; p[y] = x; p[fs] = 4 * V + np.arange(FP)
    return p
def mate(rng, a):
    a = rng.permutation(a); x, y = a[0::2].copy(), a[1::2].copy()
    for i in np.flatnonzero(x >> 2 == y >> 2):
        if x[i] >> 2 != y[i] >> 2: continue
        j = rng.choice(np.flatnonzero((x >> 2 != x[i] >> 2) & (y >> 2 != x[i] >> 2)))
        y[i], y[j] = int(y[j]), int(y[i])
    return x, y
def wire(rng, half=None, px=(), py=(), must=(), cell=0):
    px, py, must = np.array(px, np.int64), np.array(py, np.int64), np.array(must, np.int64)
    free = np.ones(4 * V, bool); free[px] = False; free[py] = False; free[must] = False
    a = np.flatnonzero(free); a = a[(a >> 2) >= cell]
    if half is None: fs = rng.permutation(a)[:FP - len(must)]
    else:
        h = half[a >> 2]; n = FP // 2 - len(must) // 2
        fs = np.concatenate([rng.permutation(a[h])[:n], rng.permutation(a[~h])[:n]])
    fs = np.concatenate([must[:1], rng.permutation(fs), must[1:]]); free[fs] = False; a = np.flatnonzero(free)
    if half is None: x, y = mate(rng, a)
    else:
        h = half[a >> 2]; c = (a >> 2) < cell
        x = np.concatenate([a[h & c], a[h & ~c]]); y = np.concatenate([rng.permutation(a[~h & c]), rng.permutation(a[~h & ~c])])
    return face(np.concatenate([x, px]), np.concatenate([y, py]), fs), fs
def seeds(rng, m):
    o = rng.permutation(V); st = np.sort(o[:m]); w = np.sort(o[m:]); give = np.zeros(V - m, bool)
    if m > 0:
        give[0] = True; give[1 + rng.permutation(V - m - 1)[:m - 1]] = True
    j = np.flatnonzero(~give); j = j[j > 0]
    px = np.concatenate([4 * rng.permutation(st) + 1, 4 * w[j - 1] + 1]); py = np.concatenate([4 * w[give], 4 * w[j]])
    free = np.ones(4 * V, bool); free[px] = False; free[py] = False
    s = np.flatnonzero(free); first = np.isin(s >> 2, st); a = s[first]; b = rng.permutation(s[~first])
    if m == 0: b = np.concatenate([np.zeros(1, np.int64), b[b != 0]])
    fs = rng.permutation(b[:FP]); b = b[FP:]; x, y = mate(rng, b[len(a):])
    return face(np.concatenate([px, a, x]), np.concatenate([py, b[:len(a)], y]), fs), fs, st
def knit(rng, px, py, fo, st):
    z = rng.integers(0, 2, (FP // 2, 1)); fs = (4 * fo[:, None] + 2 + np.concatenate([z, 1 - z], axis=1)).reshape(-1)
    free = np.ones(4 * V, bool); free[px] = False; free[py] = False; free[fs] = False
    s = np.flatnonzero(free); first = np.isin(s >> 2, st); a = s[first]; b = rng.permutation(s[~first]); x, y = mate(rng, b[len(a):])
    return face(np.concatenate([px, a, x]), np.concatenate([py, b[:len(a)], y]), fs), fs
def chain(rng, st, fo):
    m = len(st); w = np.setdiff1d(np.arange(V), st); give = np.zeros(V - m, bool); give[0] = True; give[1 + rng.permutation(V - m - 1)[:m - 1]] = True
    j = np.flatnonzero(~give)
    return knit(rng, np.concatenate([4 * rng.permutation(st) + 1, 4 * w[j - 1] + 1]), np.concatenate([4 * w[give], 4 * w[j]]), fo, st)
def blank():
    return np.zeros((N, 8, 4 * V), np.int64), np.zeros((N, 8, FP), np.int64), np.zeros((N, 8, V), np.int64), np.ones((N, 8, V), np.int64)
def mixed(rng):
    port, rim, t, d = blank()
    for r in range(N):
        k = rng.permutation(8)
        for g in range(8):
            if k[g] < 4:
                port[r, g], rim[r, g] = wire(rng); t[r, g] = rng.integers(0, 4, V); d[r, g] = 2 ** rng.integers(0, 3, V)
            else:
                half = np.zeros(V, bool); half[rng.permutation(V)[:V // 2]] = True
                port[r, g], rim[r, g] = wire(rng, half)
                t[r, g] = np.where(half, rng.integers(0, 2, V), rng.integers(2, 4, V)); d[r, g] = np.where(half, 2 ** rng.integers(0, 2, V), 2 ** rng.integers(0, 3, V))
    return port, rim, t, d
def limit(x, m):
    return np.clip(np.asarray(x).astype(np.float32), -m, m)
def gates(rng, q):
    z = np.std(q.reshape(N, 8, 16, V), axis=3, keepdims=True) * rng.uniform(0.4, 1.1, (N, 8, 1, 1))
    return np.clip(z, 0.0625, 4)
def sized(x):
    x = np.ascontiguousarray(np.reshape(x, (N, 128, V))).astype(np.float32)
    return np.where(np.abs(x) < np.float32(2.0 ** -40), np.float32(0), x).astype(BF)
def pack(q, v, h, t, d, port, rim):
    return {"q0": sized(q), "q1": sized(v),
            "th": np.ascontiguousarray(np.reshape(h, (N, 128, 1))).astype(np.float32), "t0": t.astype(np.int32), "d0": d.astype(np.int32),
            "port": np.stack([gtable(a) for a in port]), "rim": np.stack([gtable(a) for a in rim])}
def setup_inputs(rng):
    port, rim, t, d = mixed(rng); q = limit(f(rng, N, 128, V), 4); v = limit(0.25 * f(rng, N, 128, V).astype(np.float32), 1)
    return pack(q, v, gates(rng, q), t, d, port, rim)
def setup_inputs_spread(rng):
    port, rim, t, d = mixed(rng); q = limit(wide(rng, N, 128, V), 4); v = limit(0.25 * wide(rng, N, 128, V).astype(np.float32), 1)
    q = np.where(q == 0, np.float32(2.0 ** -12), q)
    h = np.clip(np.exp2(rng.uniform(-4, 2, (N, 8, 16, 1))), 0.0625, 4)
    t = np.minimum((4 * rng.random((N, 8, V)) ** 3).astype(np.int64), 3); d = 2 ** np.minimum((3 * rng.random((N, 8, V)) ** 0.5).astype(np.int64), 2)
    return pack(q, v, h, t, d, port, rim)
def setup_inputs_ends(rng):
    port, rim, t, d = blank(); t = 3 * rng.integers(0, 2, (N, 8, V)); d = 1 + 3 * rng.integers(0, 2, (N, 8, V))
    q = 8 * rng.integers(0, 2, (N, 8, 16, V)) - 4; v = 2 * rng.integers(0, 2, (N, 8, 16, V)) - 1
    h = np.where(rng.random((N, 8, 16, 1)) < 0.5, 0.0625, 4.0); half = np.arange(V) < V // 2
    for r in range(N):
        k = rng.permutation(8)
        if r == N - 1:
            i = int(np.flatnonzero(k == 4)[0]); k[i], k[7] = int(k[7]), 4
        for g in range(8):
            odd = (r + g) % 2 == 1
            px, py, must = ((), (), (0, 4 * V - 1)) if odd else ((0,), (4 * V - 1,), ())
            if k[g] < 4:
                low = rng.permutation(16) < (0, LO, LO + 1, HI - 1)[k[g]]
                h[r, g, :, 0] = np.where(low, 0.0625, 4.0); q[r, g] = np.where(low[:, None], q[r, g], np.where(half, -4, 4)[None, :])
                port[r, g], rim[r, g] = wire(rng, half, px, py, must)
            else:
                if k[g] == 4: h[r, g] = 0.0625
                port[r, g], rim[r, g] = wire(rng, None, px, py, must)
            late = (r + g) % 2 == (N + 6) % 2
            t[r, g, V - 2:] = (0, 3) if late else (3, 0); d[r, g, V - 2:] = (1, 4) if late else (4, 1)
    return pack(q, v, h, t, d, port, rim)
def setup_inputs_corners(rng):
    port, rim, t, d = blank(); most = (2 * V - FP) // 4 - 4
    for r in range(N):
        k = rng.permutation(np.array([1, CAP - 1, CAP, CAP, CAP + 1, CAP + 1, most])); k = np.concatenate([k[:5], np.zeros(1, np.int64), k[5:]])
        for g in range(8):
            port[r, g], rim[r, g], st = seeds(rng, int(k[g]))
            i = rng.integers(0, 3, V); t[r, g] = np.array([0, 2, 3])[i]; d[r, g] = np.array([4, 2, 1])[i]
            t[r, g, st] = 0; d[r, g, st] = 1
            if k[g] == 0: t[r, g] = 3; d[r, g] = 4
    q = limit(f(rng, N, 128, V), 4); v = limit(0.25 * f(rng, N, 128, V).astype(np.float32), 1)
    return pack(q, v, gates(rng, q), t, d, port, rim)
def setup_inputs_calm(rng):
    port, rim, t, d = blank(); e = np.arange(V); half = (e < CAP // 2) | ((e >= CAP) & (e < CAP + (V - CAP) // 2))
    q = np.zeros((N, 8, 16, V), np.float32); v = np.zeros((N, 8, 16, V), np.float32); h = np.zeros((N, 8, 16, 1), np.float32)
    kinds = ((LO, 3, 4), (LO, 2, 4), (LO, 0, 4), (HI, 0, 1), (HI, 1, 1), (HI - 1, 0, 2), (LO + 1, 3, 2), (HI - 1, 2, 2))
    for r in range(N):
        k = rng.permutation(8)
        for g in range(8):
            n, a, b = kinds[k[g]]; low = (rng.permutation(16) < n)[:, None]
            z = (0.5 + 2.5 * rng.random((16, 1))).astype(np.float32).astype(BF).astype(np.float32); sg = np.where(half, -1, 1)[None, :]
            any_ = 2 * rng.integers(0, 2, (16, V)) - 1
            q[r, g] = np.where(low, any_ * (1 + 2 * rng.random((16, V))), sg * z)
            v[r, g] = np.where(low, 2 * rng.random((16, V)) - 1, sg * rng.random((16, V)))
            h[r, g] = np.where(low, 0.0625, z); t[r, g] = a; d[r, g] = b
            port[r, g], rim[r, g] = wire(rng, half, (), (), (), CAP)
    return pack(q, v, h, t, d, port, rim)
def setup_inputs_knots(rng):
    port, rim, t, d = blank(); q = limit(f(rng, N, 128, V), 4).reshape(N, 8, 16, V); v = limit(0.25 * f(rng, N, 128, V).astype(np.float32), 1).reshape(N, 8, 16, V)
    h = gates(rng, q); tm = rng.permutation(16)[:2]; nt = np.setdiff1d(np.arange(16), tm); sg = 2 * rng.integers(0, 2, (N, 8, 2, V)) - 1
    q[:, :, tm] = sg * np.exp2(rng.integers(-40, -33, sg.shape).astype(np.float64)) * (1 + 0.0078125 * rng.integers(0, 128, sg.shape))
    v[:, :, tm] = sg * np.exp2(rng.integers(-40, -35, sg.shape).astype(np.float64))
    off = int(rng.integers(0, 2)); ne = (V - FP // 4) // 2; none = np.zeros(0, np.int64)
    for r in range(N):
        k = rng.permutation(4)
        for g in range(8):
            kind = int(k[g // 2])
            if (g + off) % 2 == 0:
                fo = rng.permutation(V)[:FP // 2]; st = np.sort(fo); port[r, g], rim[r, g] = chain(rng, st, fo)
                i = rng.integers(0, 3, V); t[r, g] = np.array([0, 2, 3])[i]; d[r, g] = np.array([4, 2, 1])[i]
                t[r, g, st] = rng.integers(0, 2, FP // 2); d[r, g, st] = 2 - t[r, g, st]
            elif kind == 0:
                fo = rng.permutation(V)[:FP // 2]; i = int(rng.integers(0, FP // 2)); st = fo[i:i + 1]; port[r, g], rim[r, g] = chain(rng, st, fo)
                t[r, g] = 3; d[r, g] = 4; t[r, g, st] = 0; d[r, g, st] = 1; q[r, g] = np.clip(q[r, g], -3, 3); h[r, g] = 4
            elif kind == 1:
                o = 1 + rng.permutation(V - 2); n = FP // 2; fo = o[:n]
                ea = np.concatenate([np.array([0]), o[n:n + 15]]); eb = np.concatenate([np.array([V - 1]), o[n + 15:n + 30]])
                px = (4 * ea[:, None] + np.arange(4)).reshape(-1); py = (4 * eb[:, None] + np.argsort(rng.random((16, 4)), axis=1)).reshape(-1)
                port[r, g], rim[r, g] = knit(rng, px, py, fo, none)
                t[r, g] = rng.integers(0, 4, V); d[r, g] = 2 ** rng.integers(0, 3, V); t[r, g, fo] = rng.integers(0, 2, n); d[r, g, fo] = 4
                t[r, g, ea] = 0; t[r, g, eb] = 0; d[r, g, ea] = 2 ** rng.integers(0, 3, 16); d[r, g, eb] = d[r, g, ea]
            else:
                up = kind == 2; e = np.arange(V); first = (e >= V - ne) if up else (e < ne); s = 1 if up else -1
                fo = rng.permutation(np.flatnonzero(~first))[:FP // 2]; port[r, g], rim[r, g] = knit(rng, none, none, fo, np.flatnonzero(first))
                t[r, g] = 0; d[r, g] = np.where(first, 2, 4)
                o = rng.permutation(nt); n = (LO, HI - 1)[(r + kind) % 2]; lo, ex = o[:n], o[n:]
                z = (1 + 0.9 * rng.random((len(ex), 1))).astype(np.float32).astype(BF).astype(np.float32)
                q[r, g][ex] = s * np.where(first[None, :], z, 2.0 ** -8 * (0.75 + 0.6 * rng.random((len(ex), V))))
                v[r, g][ex] = s * np.where(first[None, :], rng.random((len(ex), V)), 0); h[r, g][ex] = z
                q[r, g][lo] = (2 * rng.integers(0, 2, (n, V)) - 1) * (1 + 2 * rng.random((n, V))); h[r, g][lo] = 0.0625
    return pack(q, v, h, t, d, port, rim)
def check_inputs(d):
    bad = []
    for k, lo, hi in (("q0", -4, 4), ("q1", -1, 1), ("th", 0.0625, 4), ("t0", 0, 3), ("d0", 1, 4), ("port", 0, 4 * V + FP - 1), ("rim", 0, 4 * V - 1)):
        x = np.asarray(d[k]).astype(np.float64)
        if not np.all((x >= lo) & (x <= hi)): bad.append("range of " + k)
        if k in ("q0", "q1") and np.any((x != 0) & (np.abs(x) < 2.0 ** -40)): bad.append(k + " is under 2**-40 in size somewhere and not 0")
    if np.any(np.asarray(d["d0"]) == 3): bad.append("d0 is 3 somewhere")
    if bad: return bad
    p = np.stack([gentries(a) for a in d["port"]]).astype(np.int64); m = np.stack([gentries(a) for a in d["rim"]]).astype(np.int64)
    s = np.arange(4 * V); own = p < 4 * V; back = np.take_along_axis(p, np.where(own, p, 0), 2)
    if np.any(own & (back != s)): bad.append("port: facing slots don't face each other")
    if np.any(own & ((p >> 2) == (s >> 2))): bad.append("port: an element faces itself")
    if np.any(np.add.reduce((~own).astype(np.int64), axis=2) != FP) or np.any(np.take_along_axis(p, m, 2) != 4 * V + np.arange(FP)): bad.append("port and rim: foreign ports")
    return bad
def swap(x):
    y = np.zeros_like(x)
    for r in range(N):
        for d in range(1, N):
            s = (r + d) % N; gs = (np.arange(8) + (1 if r < s else 7)) % 8
            y[r][..., (d - 1) * B:d * B] = x[s][gs][..., (N - d - 1) * B:(N - d) * B]
    return y
def around(x, e):
    b = np.take_along_axis(x, e[:, :, None, :], 3) if x.ndim == 4 else np.take_along_axis(x, e, 2)
    return np.concatenate([x, swap(b)], axis=-1)
def overlap(x0, x1, a, b, tau):
    u = (b - a).astype(np.float32) * x0
    w = (np.float32(0.5) * ((b - tau) ** 2 - (a - tau) ** 2).astype(np.float32)) * x1
    return np.float32(0.03125) * (u + w)
def reference(q0, q1, th, t0, d0, port, rim):
    s0 = q0.astype(np.float32).reshape(N, 8, 16, V); s1 = q1.astype(np.float32).reshape(N, 8, 16, V); h = th.astype(np.float32).reshape(N, 8, 16, 1)
    t = t0.astype(np.int64); dt = d0.astype(np.int64)
    p = np.stack([gentries(a) for a in port]).astype(np.int64); m = np.stack([gentries(a) for a in rim]).astype(np.int64)
    col = np.where(p < 4 * V, p >> 2, p - 3 * V); e = m >> 2
    num = np.zeros((N, 8, V), np.int64) + np.arange(N)[:, None, None] * V + np.arange(V); nx = around(num, e)
    fm = np.zeros((N, 8, 16, 4 * V + FP), np.float32); inv = np.array([0, 1, 0.5, 0, 0.25], np.float32)
    for rnd in range(RO):
        key = M * (t + dt) + num; kn = np.take_along_axis(around(key, e), col, 2).reshape(N, 8, V, 4)
        can = np.all(key[..., None] < kn, axis=3); act = can & (np.add.accumulate(can.astype(np.int64), axis=2) <= CAP)
        x0, x1, tx = around(s0, e), around(s1, e), around(t, e)
        for r in range(N):
            for g in range(8):
                a = np.flatnonzero(act[r, g]); sl = 4 * a[:, None] + np.arange(4); c = p[r, g][sl]; n = col[r, g][sl]
                te = tx[r, g][a][:, None]; tn = tx[r, g][n]; de = dt[r, g][a]; tb = te + de[:, None]; ta = np.minimum(np.maximum(te, tn), tb)
                old = x0[r, g][:, a]
                ie = overlap(old[:, :, None], x1[r, g][:, a][:, :, None], ta, tb, te); ni = overlap(x0[r, g][:, n], x1[r, g][:, n], ta, tb, tn)
                left = nx[r, g][a][:, None] < nx[r, g][n]
                up = np.maximum(np.where(left, ie, ni), np.float32(0)); dn = np.minimum(np.where(left, ni, ie), np.float32(0))
                ph = np.float32(0.5) * (up * up + dn * dn); own = np.where(left, -ph, ph)
                new = old
                for i in range(4): new = new + (fm[r, g][:, sl[:, i]] + own[:, :, i])
                fm[r, g][:, sl] = 0
                fm[r, g][:, c] = fm[r, g][:, c] - own
                s0[r, g][:, a] = new; s1[r, g][:, a] = (new - old) * inv[de]
                cnt = np.add.reduce((np.abs(new) > h[r, g]).astype(np.int64), axis=0)
                t[r, g][a] = tb[:, 0]; dt[r, g][a] = np.where(cnt >= HI, 1, np.where(cnt <= LO, 4, 2))
        come = swap(fm[..., 4 * V:])
        for r in range(N):
            for g in range(8): fm[r, g][:, m[r, g]] = fm[r, g][:, m[r, g]] + come[r, g]
        fm[..., 4 * V:] = 0
    k = fm[..., :4 * V].reshape(N, 8, 16, V, 4)
    ym = ((k[..., 0] + k[..., 1]) + k[..., 2]) + k[..., 3]
    return {"y0": s0.reshape(N, 128, V), "y1": s1.reshape(N, 128, V), "ym": np.ascontiguousarray(ym).reshape(N, 128, V), "yt": np.concatenate([t, dt], axis=2).astype(np.float32)}

@@ -1,0 +1,584 @@
+from concourse.bass import DstId, RemoteDMATransfer
+from concourse.mybir import AluOpType as OP, ActivationFunctionType as AF
+
+N, V, B, CAP, RO = 8, 928, 48, 208, 5
+H = (N - 1) * B
+L = 4 * CAP
+EW = V + CAP + H
+MO = 2 * EW
+Z0 = 4 * EW
+MW = Z0 + 8
+SC = (V + CAP) // 4
+PC = V // 4
+AC, LC, EC, RC = CAP // 16, L // 16, V // 16, H // 16
+M1, M8, M128, BIG = 1.5 * 2.0 ** 23, 1.5 * 2.0 ** 26, 1.5 * 2.0 ** 30, 8192.0
+F, BF, I32, U16 = "float32", "bfloat16", "int32", "uint16"
+
+_SB = {
+    "qm": (MO + MW, F), "zw": (EW, BF), "tw": (EW, BF), "gw": (4 * V, BF), "st": (V + CAP, BF), "fail": (V, BF), "psb": (V, BF),
+    "lr": (2800, BF), "zl0": (H, BF), "zl1": (H, BF), "bl0": (2 * H, F), "bl1": (2 * H, F), "ml0": (H, F), "ml1": (H, F),
+    "zs": (H, BF), "bs": (2 * H, F), "ms": (H, F),
+    "pt": (PC, I32), "rm": (24, I32), "td": (128, I32), "tht": (4, F),
+    "xi": (160, I32), "xa": (160, I32), "xgi": (160, I32), "xb": (PC, I32), "col": (64, F), "coli": (8, I32),
+    "r16": (16, F), "r4": (4, F), "rk": (4, F), "br": (CAP, F), "bb": (CAP, BF),
+    "ti32": (160, F), "ti": (160, BF), "blk": (128, BF), "up": (128, BF), "ul": (128, BF), "sel": (2048, BF), "f4": (160, BF),
+    "tc": (160, BF), "tn": (160, BF), "ts": (160, BF), "tl": (160, BF), "td4": (160, BF), "te": (160, BF),
+    "ta": (160, BF), "tx": (160, BF), "t1": (160, BF), "dg": (512, BF), "dz": (128, BF), "tm": (640, BF),
+    "si": (PC, F), "cf": (PC, F), "w1": (PC, F), "w2": (PC, F),
+    "xf": (4 * SC, BF), "nbl": (PC, U16), "kk": (EC, F), "zb": (64, BF), "zf": (128, F),
+    "ri": (24, I32), "zrl": (24, U16), "brl": (48, U16), "mrl": (24, U16),
+    "can": (64, BF), "sm": (256, F), "ol": (EC, U16),
+    "al": (32, U16), "nl": (LC, U16), "il": (3 * LC, U16), "co": (6 * LC, BF), "cw": (16 * LC, F),
+    "qe": (2 * CAP, F), "q0n": (L, F), "q1n": (L, F), "car": (L, F), "ue": (L, F), "un": (L, F), "ss": (L, F),
+    "ff": (L, F), "mf": (L, F), "qn": (2 * CAP, F), "dq": (CAP, F), "cb": (2 * CAP, BF), "zu": (3 * CAP, BF),
+    "fl": (PC, U16), "mg": (4 * V, F), "yo": (V, F), "ytb": (256, F),
+}
+SCRATCH = {k: ("sbuf", [128, v[0]], v[1]) for k, v in _SB.items()}
+for _i in range(8):
+    SCRATCH["p%d" % _i] = ("psum", [128, 512], F)
+SEMAPHORES = (["cv", "ca", "ct", "cg", "zsent", "bsent", "msent", "zero", "lq"] + ["za%d" % i for i in range(RO + 1)]
+              + ["ba%d" % i for i in range(RO)] + ["ma%d" % i for i in range(1, RO + 1)] + ["d%d" % i for i in range(14)])
+
+
+def rank_program(g, core, T, topo):
+    r = T.rank_of(core)
+    if r is None:
+        return
+    o = B * r
+    nlo, nhi = B * r, H - B * r
+    hi0 = o + V
+    Q = {"v": g.vector, "a": g.scalar, "t": g.tensor, "s": g.sync, "g": g}
+    ops, acc, total, nd = [], {}, {}, [0]
+
+    def A(name, lo=0, hi=None, st=1):
+        hi = (512 if name not in _SB else _SB[name][0]) if hi is None else hi
+        if st == 1:
+            return (T[name][:, lo:hi], [(name, ((1 << (hi - lo)) - 1) << lo)], [])
+        m = 0
+        for c in range(lo, hi, st):
+            m |= 1 << c
+        return (T[name][:, lo:hi:st], [(name, m)], [])
+
+    def IND(w, off):
+        return (w[0].indirect(off[0]), w[1], off[1])
+
+    def add(q, fn, outs, ins, tok=None):
+        me = {"q": q, "fn": fn, "deps": [], "tok": tok, "need": False}
+        touch = [(x, True) for a in outs for x in a[1]] + [(x, False) for a in outs for x in a[2]]
+        touch += [(x, False) for a in ins if isinstance(a, tuple) for x in a[1] + a[2]]
+        for (name, m), wr in touch:
+            bank = name not in _SB
+            for (m2, wr2, op) in acc.get(name, []):
+                if op is me:
+                    continue
+                if bank and op["q"] != q:
+                    me["deps"].append(op)
+                elif (m & m2) and (wr or wr2) and not (q == "t" and op["q"] == "t"):
+                    me["deps"].append(op)
+        for (name, m), wr in touch:
+            bank = name not in _SB
+            old = acc.get(name, [])
+            if wr:
+                old = [x for x in old if (x[0] & ~m) and not (bank and x[2]["q"] != q)]
+            else:
+                old = [x for x in old if x[1] or x[2]["q"] != q or x[2]["tok"] is not None or (x[0] & ~m)]
+            acc[name] = old + [(m, wr, me)]
+        ops.append(me)
+        return me
+
+    def P(a):
+        return a[0] if isinstance(a, tuple) else a
+
+    def ts(out, x, s1, op0, s2=None, op1=None):
+        if op1 is None:
+            return add("v", lambda: g.vector.tensor_scalar(out[0], x[0], P(s1), None, op0), [out], [x, s1])
+        return add("v", lambda: g.vector.tensor_scalar(out[0], x[0], P(s1), P(s2), op0, op1), [out], [x, s1, s2])
+
+    def tt(out, x, y, op):
+        return add("v", lambda: g.vector.tensor_tensor(out[0], x[0], y[0], op), [out], [x, y])
+
+    def cp(out, x):
+        return add("v", lambda: g.vector.tensor_copy(out[0], x[0]), [out], [x])
+
+    def ms(out, c):
+        return add("v", lambda: g.vector.memset(out[0], c), [out], [])
+
+    def act(out, x, fn=AF.Copy, scale=1.0, bias=0.0):
+        return add("a", lambda: g.scalar.activation(out[0], x[0], fn, bias=bias, scale=P(scale)), [out], [x, scale])
+
+    def mm(out, lt, rhs, start=True, stop=True):
+        return add("t", lambda: g.tensor.matmul(out[0], lt[0], rhs[0], start, stop), [out], [lt, rhs])
+
+    def iota(out, step, n, base, ch):
+        return add("g", lambda: g.iota(out[0], [[step, n]], base, ch), [out], [])
+
+    def dma(q, out, x, sem=None):
+        if sem is None:
+            sem = "d%d" % nd[0]
+            nd[0] += 1
+        total[sem] = total.get(sem, 0) + 16
+        tok = [sem, total[sem]]
+        outs = [out] if isinstance(out, tuple) else []
+        return add(q, lambda: Q[q].dma_start(P(out), P(x)).then_inc(T.sem[sem], 16), outs, [x], tok=tok)
+
+    def plan(src, calls):
+        rs = T.rank_of(src)
+        peers = [T.cores[(rs + d) % N] for d in range(1, N)]
+        far = [c for c in peers if topo.chip(c) != topo.chip(src)]
+        near = [c for c in peers if c not in far]
+        eng = topo.engines(src, far[0])
+        res = []
+        if calls == 1:
+            spare, i, one = len(eng) - len(far), 0, {}
+            for n, c in enumerate(far):
+                k = 2 if n < spare else 1
+                one[c] = eng[i:i + k]
+                i += k
+            res.append(one)
+        else:
+            n1 = len(eng) // 2
+            for part in (far[:n1], far[n1:]):
+                k = len(eng) // len(part)
+                res.append({c: eng[n * k:(n + 1) * k] for n, c in enumerate(part)})
+        for n, c in enumerate(near):
+            rest = [e for e in topo.engines(src, c) if e not in eng]
+            k = len(rest) // len(near)
+            res[0][c] = rest[n * k:(n + 1) * k]
+        return res
+
+    def exchange(src, dst, w, sem, lsem, calls):
+        sent = []
+        for part in plan(core, calls):
+            tr = []
+            for c, es in part.items():
+                s = T.rank_of(c)
+                d = (s - r) % N
+                rid, pid, _ = topo.addr(c)
+                at = r if r < s else r - 1
+                tr.append(RemoteDMATransfer(dst_ids=[DstId(rid=rid, pnc=pid)], dma_engine_mask=sum(1 << e for e in es),
+                                            remote_sem=T.sem[sem], src=T[src][:, (d - 1) * w:d * w], dst=T[dst][:, at * w:(at + 1) * w]))
+            total[lsem] = total.get(lsem, 0) + sum(len(x) for x in part.values())
+            sent.append(add("g", lambda tr=tr: g.remote_dma_fused(tr, local_sem=T.sem[lsem]), [], [A(src)], tok=[lsem, 0]))
+        for x in sent:
+            x["tok"][1] = total[lsem]
+        total[sem] = sum(len(part.get(core, ())) for c in T.cores if c != core for part in plan(c, calls))
+        acc[dst] = []
+        add(None, None, [A(dst)], [], tok=[sem, total[sem]])
+
+    def C(i):
+        return A("col", i, i + 1)
+
+    ident, shup, shdn = A("ti", 16, 144), A("ti", 0, 128), A("ti", 32, 160)
+    Zw, Tw, Qw, Mw = A("zw"), A("tw"), A("qm", 0, MO), A("qm", MO, MO + MW)
+
+    def win(name, s):
+        return A(name, 16 - s, 144 - s)
+
+    dma("s", A("td", 0, EC), T.t0[:])
+    dma("a", A("td", 64, 64 + EC), T.d0[:])
+    dma("s", A("rm", 0, RC), T.rim[:])
+    dma("a", A("pt"), T.port[:])
+    dma("s", A("tht", 0, 1), T.th[:])
+    iota(A("coli", 0, 2), 0, 2, 0, 1)
+    iota(A("xi"), 1, 160, -16, -1)
+    iota(A("xb"), 1, PC, 0, 0)
+    a = dma("g", A("qm", o, o + V), T.q0[:], "lq")
+    b = dma("g", A("qm", EW + o, EW + o + V), T.q1[:], "lq")
+    a["tok"][1] = b["tok"][1]
+
+    ms(Zw, 8.0)
+    ts(A("coli", 2, 3), A("coli", 0, 1), 15, OP.bitwise_and)
+    ts(A("coli", 4, 5), A("coli", 0, 1), 3, OP.bitwise_and)
+    cp(C(0), A("coli", 2, 3))
+    cp(C(1), A("coli", 4, 5))
+    ts(A("xgi"), A("xi"), C(0), OP.add)
+    ts(A("r16"), A("xb", 0, 16), C(0), OP.is_equal)
+    ts(A("xa"), A("xgi"), 4, OP.arith_shift_right)
+    tt(C(2), C(0), C(1), OP.subtract)
+    ts(A("blk"), A("xa", 16, 144), 0.0, OP.is_equal)
+    for i in range(6):
+        act(A("sel", 128 * i, 128 * i + 128), A("blk"), scale=A("r16", i, i + 1))
+    for i in range(6, 16):
+        ts(A("sel", 128 * i, 128 * i + 128), A("blk"), A("r16", i, i + 1), OP.mult)
+    ts(A("zf", 0, EC), A("td", 0, EC), 8.0, OP.mult, -2.0, OP.add)
+    ts(A("zf", 64, 64 + EC), A("td", 64, 64 + EC), 9.0, OP.mult)
+    ts(A("ri", 0, RC), A("rm", 0, RC), 2, OP.arith_shift_right)
+    tt(A("zb", 0, EC), A("zf", 0, EC), A("zf", 64, 64 + EC), OP.add)
+    ts(A("zrl", 0, RC), A("ri", 0, RC), float(o), OP.add)
+
+    def spread_own(name, banks, eng):
+        for i in range(16):
+            mm(A(banks[i // 8], EC * (i % 8), EC * (i % 8 + 1)), A("sel", 128 * i, 128 * i + 128), A("zb", 0, EC))
+        eng[0](A(name, o, o + 8 * EC), A(banks[0], 0, 8 * EC))
+        eng[1](A(name, o + 8 * EC, o + V), A(banks[1], 0, 8 * EC))
+    cm = A("cf")
+    ts(A("w1"), A("pt"), float(4 * V), OP.max, 3.0, OP.mult)
+    ts(A("w2"), A("pt"), 4 * V + nhi - 0.5, OP.is_ge, -float(4 * (V + H)), OP.mult)
+    spread_own("zw", ("p0", "p1"), (act, cp))
+    act(A("zs"), IND(Zw, A("zrl", 0, RC)))
+    exchange("zs", "zl0", B, "za0", "zsent", 2)
+    for cc in range(3):
+        ts(A("brl", cc, 42, 6), A("ri", cc, RC, 3), float(o), OP.add)
+        ts(A("brl", 3 + cc, 42, 6), A("ri", cc, RC, 3), float(o + EW), OP.add)
+    ts(A("xa"), A("xi"), 127, OP.bitwise_and)
+    ts(A("r4"), A("xb", 0, 16, 4), C(2), OP.is_equal)
+    ts(A("rk"), A("xb", 0, 4), C(1), OP.is_equal)
+    ts(A("ti"), A("xa"), 0.0, OP.is_equal)
+    for u in range(4):
+        act(A("tm", 160 * u, 160 * u + 160), A("ti"), scale=A("r4", u, u + 1))
+    for base in (0, EW):
+        if o:
+            act(A("qm", base, base + o), A("sel", 0, o), scale=0.0)
+        act(A("qm", base + o + V, base + EW), A("sel", 0, EW - o - V), scale=0.0)
+    act(A("bs"), IND(Qw, A("brl", 0, 42)))
+    exchange("bs", "bl0", 2 * B, "ba0", "bsent", 2)
+    tt(A("w1"), A("w1"), A("pt"), OP.add)
+    ts(A("si"), A("xb"), 16.0, OP.mult, C(0), OP.add)
+    tt(A("w1"), A("w1"), A("w2"), OP.add)
+    ts(A("w2"), A("si"), float(4 * o - 1), OP.add)
+    ts(cm, A("w1"), 4 * o - 12 * V - 1.5, OP.add)
+    ts(C(3), C(2), 0.25, OP.mult, A("rk", 1, 2), OP.mult)
+    ts(A("xf", SC, SC + PC), cm, M128, OP.add, M128, OP.subtract)
+    tt(A("w1"), cm, A("w2"), OP.is_gt)
+    tt(A("xf", 2 * SC, 2 * SC + PC), cm, A("xf", SC, SC + PC), OP.subtract)
+    ts(A("xf", 0, PC), A("w1"), 8.0, OP.mult)
+    ts(C(11), A("rk", 3, 4), float(o), OP.mult, C(3), OP.add)
+    ts(C(12), A("rk", 3, 4), float(V + H), OP.mult, C(3), OP.add)
+    ms(A("xf", PC, SC), 8.0)
+    ts(A("xf", 3 * SC, 3 * SC + PC), A("xb"), A("rk", 0, 1), OP.mult, C(11), OP.add)
+    ts(C(13), A("rk", 2, 3), 8.0, OP.mult, C(12), OP.add)
+    ms(A("xf", SC + PC, 2 * SC), 5120.0)
+    ms(A("xf", 2 * SC + PC, 3 * SC), 4 * (V + H) - 5121.5)
+    ts(A("xf", 3 * SC + PC, 4 * SC), A("xb", 0, LC), A("rk", 0, 1), OP.mult, C(13), OP.add)
+    for k in range(4):
+        act(A("dg", 128 * k, 128 * k + 128), ident, scale=A("r16", k, k + 1))
+    for j, (c0, c1) in enumerate(((0, 120), (120, PC), (PC, SC))):
+        for u in range(4):
+            for f in (1, 2, 0, 3):
+                s = 160 * u + 16 - 4 * (f - u)
+                mm(A("p%d" % (2 + j), u, 4 * (c1 - c0), 4), A("tm", s, s + 128), A("xf", f * SC + c0, f * SC + c1), f == 1, f == 3)
+        act(A("st", 4 * c0, 4 * c1), A("p%d" % (2 + j), 0, 4 * (c1 - c0)))
+    ts(A("w2"), cm, 0.25, OP.mult, M1, OP.add)
+    tt(C(4), A("r16", 14, 15), A("r4", 0, 1), OP.subtract)
+    ts(C(5), A("r4", 0, 1), BIG, OP.mult)
+    ts(A("nbl"), A("w2"), M1, OP.subtract)
+    ts(A("dz"), ident, C(4), OP.mult)
+    ts(A("tx"), A("xgi"), 0.0, OP.is_equal, C(5), OP.mult)
+    ts(A("ul"), A("xi", 16, 144), -0.5, OP.is_lt)
+    ts(A("kk"), A("si", 0, EC), float(V), OP.add)
+    ms(A("can", 0, 2), 0.0)
+    ms(A("sm", 0, 2), 0.0)
+    tt(A("up"), A("ul"), A("blk"), OP.mult)
+    ts(C(7), A("r16", 12, 13), 4.0, OP.mult, A("r16", 13, 14), OP.add)
+    ts(A("xa"), A("xgi"), 2, OP.arith_shift_right)
+    tt(A("ul"), A("blk"), A("up"), OP.subtract)
+    act(A("ti32"), A("ti"))
+    act(A("td4"), A("ti"), scale=A("r4", 0, 1))
+
+    def lane_constants():
+        tt(C(6), A("r4", 1, 2), A("r4", 2, 3), OP.add)
+        tt(C(7), C(7), A("r16", 15, 16), OP.add)
+        ts(A("f4"), A("xa"), 0.0, OP.is_equal)
+        ts(A("tc"), A("xgi"), C(1), OP.is_equal, C(6), OP.mult)
+        ts(A("ta"), A("xgi"), 0.0, OP.is_equal, C(7), OP.mult)
+        ts(A("ts"), A("f4"), C(7), OP.mult, 4.0, OP.mult)
+        ts(C(8), C(1), -1.5, OP.add)
+        tt(A("tl"), A("tc"), A("ts"), OP.subtract)
+        act(A("te"), A("f4"), scale=A("r16", 14, 15))
+        act(A("tn"), A("tc"), scale=0.25)
+        act(C(9), C(1), AF.Identity, -1.0, float(Z0))
+        act(C(10), A("tht", 0, 1), scale=-1.0)
+        zc = MW // 8 + 3
+        act(A("qm", MO, MO + zc), A("sel", 0, zc), scale=0.0)
+        zs_ = [dma("s", A("qm", MO + c, min(MO + MW, MO + c + 736)), A("qm", MO, MO + min(736, MW - c)), "zero") for c in range(zc, MW, 736)]
+        for x in zs_:
+            x["tok"][1] = zs_[-1]["tok"][1]
+
+    parts = (("p0", 0, 384), ("p1", 384, 768), ("p4", 768, 848), ("p7", 848, V))
+    chunks = tuple(("va"[i % 2], 24 * i, 24 * i + 24, i // 4) for i in range(8)) + (("v", 192, 212, 2), ("a", 212, PC, 3))
+
+    def z_in(land, name, eng, banks=("p5", "p6")):
+        if nlo:
+            mm(A(banks[0], 0, nlo), shup, A(land, 0, nlo))
+        if nhi:
+            mm(A(banks[1], 0, nhi), shdn, A(land, nlo, H))
+        if nlo:
+            eng[0](A(name, 0, nlo), A(banks[0], 0, nlo))
+        if nhi:
+            eng[1 if nlo else 0](A(name, hi0, hi0 + nhi), A(banks[1], 0, nhi))
+
+    def halo_in(land, w, fields):
+        for f, at, bank in fields:
+            for p in range(N - 1):
+                mm(A(bank, B * p, B * p + B), A("ti32", 0, 128) if p < r else A("ti32", 32, 160), A(land, w * p + at, w * p + at + B))
+        for f, at, bank in fields:
+            base, st = ((0, 1), (EW, 1), (MO, 4))[f]
+            if nlo:
+                act(A("qm", base, base + st * nlo, st), A(bank, 0, nlo))
+            if nhi:
+                act(A("qm", base + st * hi0, base + st * (hi0 + nhi), st), A(bank, nlo, H))
+
+    def clocks(at):
+        for i in range(16):
+            mm(A("p2", 0, EC), win("t1", i), A("zw", o + EC * i, o + EC * (i + 1)), i == 0, i == 15)
+        ts(A("ytb", 128, 128 + EC), A("p2", 0, EC), M8, OP.add, M8, OP.subtract)
+        tt(A("ytb", 192, 192 + EC), A("ytb", 128, 128 + EC), A("p2", 0, EC), OP.subtract)
+        ts(A("ytb", 128, 128 + EC), A("ytb", 128, 128 + EC), -0.125, OP.mult, 2.0, OP.subtract)
+        tt(at, A("ytb", 128, 128 + EC), A("ytb", 192, 192 + EC), OP.subtract)
+
+    def W(i, n=1):
+        return A("cw", LC * i, LC * (i + n))
+
+    def CO(i):
+        return A("co", LC * i, LC * (i + 1))
+
+    def spread(i, bank):
+        for k in range(4):
+            for u in range(4):
+                s = 128 * (4 * u + k)
+                mm(A("p%d" % (bank + k // 2), CAP * (k % 2) + u, CAP * (k % 2 + 1), 4), A("sel", s, s + 128), CO(i))
+
+    def K(bank, k):
+        return A("p%d" % (bank + k // 2), CAP * (k % 2), CAP * (k % 2 + 1))
+
+    def lanes(t, bank, at):
+        for u in range(4):
+            mm(A(bank, at, at + LC), win(t, 4 * u), A("lr", u, CAP, 4), u == 0, u == 3)
+
+    for rnd in range(RO):
+        last = rnd == RO - 1
+        for bank, e0, e1 in parts:
+            mm(A(bank, 0, e1 - e0), ident, A("st", e0, e1), True, False)
+            mm(A(bank, 0, e1 - e0), A("dz"), A("zw", o + e0, o + e1), False, False)
+        act(A("lr", 0, CAP), A("st", V, V + CAP))
+        z_in("zl%d" % (rnd % 2), "zw", (cp, act))
+        for q, c0, c1, h in chunks:
+            (cp if q == "v" else act)(A("gw", 16 * c0, 16 * c1), IND(Zw, A("nbl", c0, c1)))
+        for q, c0, c1, h in chunks:
+            bank, e0, e1 = parts[h]
+            for k in range(4):
+                mm(A(bank, 4 * c0 - e0, 4 * c1 - e0), A("dg", 128 * k, 128 * k + 128), A("gw", 16 * c0 + k, 16 * c1, 4), False, 4 * c1 == e1 and k == 3)
+        for h, (bank, e0, e1) in enumerate(parts):
+            if h % 2 == 0:
+                ts(A("fail", e0, e1), A(bank, 0, e1 - e0), 4.0, OP.is_lt)
+            else:
+                act(A("fail", e0, e1), A(bank, 0, e1 - e0), AF.Relu, -1.0, 4.0)
+        for bank, e0, e1 in parts[::-1]:
+            act(A("psb", e0, e1), A(bank, 0, e1 - e0))
+        for i in range(16):
+            mm(A("p2", 0, EC), win("tx", i), A("fail", i, V, 16), i == 0, i == 15)
+        if rnd == 0:
+            lane_constants()
+        ts(A("can", 1, 1 + EC), A("p2", 0, EC), 0.5, OP.is_lt)
+        mm(A("p3", 0, EC), A("ul"), A("can", 1, 1 + EC), True, False)
+        mm(A("p3", 0, EC), A("up"), A("can", 0, EC), False, True)
+        tt(A("sm", 1, 1 + EC), A("p2", 0, EC), A("kk"), OP.min)
+        tt(A("sm", 64, 64 + EC), A("sm", 1, 1 + EC), A("sm", 0, EC), OP.subtract)
+        add("v", lambda: g.vector.tensor_tensor_scan(T.sm[:, 128:128 + EC], T.sm[:, 64:64 + EC], T.p3[:, 0:EC], -1.0, OP.add, OP.add),
+            [A("sm", 128, 128 + EC)], [A("sm", 64, 64 + EC), A("p3", 0, EC)])
+        cp(A("ol"), A("sm", 128, 128 + EC))
+        cp(IND(A("lr"), A("ol")), A("psb"))
+        halo_in("bl%d" % (rnd % 2), 2 * B, ((0, 0, "p5"), (1, B, "p6")))
+        lanes("td4", "p4", 0)
+        lanes("te", "p4", LC)
+        lanes("tl", "p4", 2 * LC)
+        for i in range(16):
+            mm(A("p3", 0, AC), win("ta", i), A("lr", i, CAP, 16), i == 0, i == 15)
+        lanes("tn", "p2", 0)
+        lanes("tc", "p5", 0)
+        lanes("ts", "p5", LC)
+        D, E = A("p4", 0, LC), A("p4", LC, 2 * LC)
+        ts(W(0, 2), A("p4", 0, 2 * LC), M8, OP.add, M8, OP.subtract)
+        ts(CO(0), A("p4", 2 * LC, 3 * LC), C(8), OP.is_lt, 0.5, OP.subtract)
+        tt(W(2), E, W(1), OP.subtract)
+        ts(W(3), W(0), -1.125, OP.mult, 0.5, OP.add)
+        tt(W(4), D, CO(0), OP.subtract)
+        ts(W(5), W(2), 2.0, OP.add)
+        tt(W(6), W(4), W(3), OP.add)
+        cp(A("al", 0, AC), A("p3", 0, AC))
+        ts(A("al", AC, 2 * AC), A("p3", 0, AC), float(EW), OP.add)
+        tt(W(7), W(6), W(5), OP.add)
+        ts(A("nl"), A("p2", 0, LC), M1, OP.add, M1, OP.subtract)
+        act(A("qe"), IND(Qw, A("al", 0, 2 * AC)))
+        if rnd:
+            act(W(13), W(6), AF.Relu, BIG, BIG)
+            act(W(14), W(6), AF.Relu, -BIG, BIG)
+        act(A("q0n"), IND(A("qm", 0, EW), A("nl")))
+        act(W(8), W(2), AF.Relu, -0.5, 0.25)
+        act(CO(4), W(1), AF.Identity, 1.0, 34.0)
+        act(CO(5), W(8), AF.Identity, 1.0, 0.25)
+        act(A("q1n"), IND(A("qm", EW, MO), A("nl")))
+        if last:
+            act(A("br"), IND(Zw, A("al", 0, AC)), AF.Identity, 0.125, M1)
+            act(A("bb"), A("br"), AF.Identity, 1.0, -M1)
+        tt(W(7), W(7), W(5), OP.min)
+        ts(A("il", 2 * LC, 3 * LC), A("p5", LC, 2 * LC), C(1), OP.add)
+        ts(W(10), W(7), 0.0, OP.max, -0.5, OP.mult)
+        tt(CO(1), W(10), CO(0), OP.mult)
+        tt(W(11), W(10), W(5), OP.add)
+        spread(1, 6)
+        tt(CO(2), W(11), CO(1), OP.mult)
+        tt(W(12), W(11), W(6), OP.add)
+        spread(2, 2)
+        tt(CO(3), W(12), CO(1), OP.mult)
+        spread(3, 0)
+        if rnd:
+            tt(W(13, 2), W(13, 2), A("p5", 0, 2 * LC), OP.add)
+            ts(A("il", 0, LC), W(13), Z0 - 1.5, OP.min, 1.5, OP.add)
+            ts(A("il", LC, 2 * LC), W(14), C(9), OP.min, C(1), OP.add)
+        spread(0, 4)
+        q0e, q1e = A("qe", 0, CAP), A("qe", CAP, 2 * CAP)
+        hs = [(2 * CAP * h, 2 * CAP * (h + 1)) for h in range(2)]
+        for h in range(2):
+            for k in (2 * h, 2 * h + 1):
+                tt(A("ue", CAP * k, CAP * k + CAP), q0e, K(6, k), OP.mult)
+            for k in (2 * h, 2 * h + 1):
+                tt(K(2, k), q1e, K(2, k), OP.mult)
+        for h in range(2):
+            tt(A("ue", *hs[h]), A("ue", *hs[h]), A("p%d" % (2 + h), 0, 2 * CAP), OP.add)
+        if last:
+            cp(IND(Tw, A("al", 0, AC)), A("bb"))
+        act(A("ue"), A("ue"), AF.Relu, 0.125)
+        if last:
+            act(A("zs"), IND(Tw, A("zrl", 0, RC)))
+            exchange("zs", "zl%d" % (RO % 2), B, "za%d" % RO, "zsent", 2)
+        act(A("ue"), A("ue"), AF.Square)
+        for h in range(2):
+            for k in (2 * h, 2 * h + 1):
+                tt(A("un", CAP * k, CAP * k + CAP), A("q0n", k, L, 4), K(6, k), OP.mult)
+            for k in (2 * h, 2 * h + 1):
+                tt(K(0, k), A("q1n", k, L, 4), K(0, k), OP.mult)
+            tt(A("un", *hs[h]), A("un", *hs[h]), A("p%d" % h, 0, 2 * CAP), OP.add)
+            act(A("un", *hs[h]), A("un", *hs[h]), AF.Relu, -0.125)
+            act(A("p%d" % (2 + h), 0, 2 * CAP), A("un", *hs[h]), AF.Square)
+        if rnd:
+            halo_in("ml%d" % (rnd % 2), B, ((2, 0, "p6"),))
+        for u in range(4):
+            mm(A("p7", u, CAP, 4), A("sel", 512 * u, 512 * u + 128), CO(4))
+            mm(A("p7", CAP + u, 2 * CAP, 4), A("sel", 512 * u, 512 * u + 128), CO(5))
+        if rnd:
+            act(A("car"), IND(Mw, A("il", LC, 2 * LC)))
+
+        def put_m():
+            if rnd:
+                tt(IND(Mw, A("il", 2 * LC, 3 * LC)), A("car"), A("ff"), OP.subtract)
+            else:
+                ts(IND(Mw, A("il", 2 * LC, 3 * LC)), A("ff"), -1.0, OP.mult, 0.0, OP.add)
+            act(A("ms"), IND(Mw, A("mrl", 0, RC)))
+            exchange("ms", "ml%d" % ((rnd + 1) % 2), B, "ma%d" % (rnd + 1), "msent", 2 if last else 1)
+        for h in range(2):
+            tt(A("ss", *hs[h]), A("ue", *hs[h]), A("p%d" % (2 + h), 0, 2 * CAP), OP.add)
+            for k in (2 * h, 2 * h + 1):
+                tt(A("ff", k, L, 4), A("ss", CAP * k, CAP * k + CAP), K(4, k), OP.mult)
+        src = "ff"
+        if rnd:
+            tt(A("mf"), IND(Mw, A("il", 0, LC)), A("ff"), OP.add)
+            src = "mf"
+        if last:
+            z_in("zl%d" % (RO % 2), "tw", (act, act), ("p0", "p2"))
+            for c in range(1):
+                act(A("gw", V * c, V * c + V), IND(Tw, A("nbl", EC * c, EC * c + EC)))
+            put_m()
+            for c in range(1, 3):
+                act(A("gw", V * c, V * c + V), IND(Tw, A("nbl", EC * c, EC * c + EC)))
+        acq, qn = A("p6", 0, CAP), A("qn", 0, CAP)
+        tt(acq, q0e, A(src, 0, L, 4), OP.add)
+        tt(acq, acq, A(src, 1, L, 4), OP.add)
+        tt(acq, acq, A(src, 2, L, 4), OP.add)
+        tt(qn, acq, A(src, 3, L, 4), OP.add)
+        ts(A("cb", 0, CAP), qn, A("tht", 0, 1), OP.is_gt)
+        ts(A("cb", CAP, 2 * CAP), qn, C(10), OP.is_lt)
+        mm(A("p1", 0, CAP), A("blk"), A("cb", 0, CAP), True, False)
+        mm(A("p1", 0, CAP), A("blk"), A("cb", CAP, 2 * CAP), False, True)
+
+        def put_z():
+            ts(A("zu", 0, CAP), A("p1", 0, CAP), 5.5, OP.is_ge, -18.0, OP.mult)
+            ts(A("zu", CAP, 2 * CAP), A("p1", 0, CAP), 9.5, OP.is_ge, -9.0, OP.mult)
+            tt(A("zu", 2 * CAP, 3 * CAP), A("zu", 0, CAP), A("p7", 0, CAP), OP.add)
+            tt(IND(Zw, A("al", 0, AC)), A("zu", 2 * CAP, 3 * CAP), A("zu", CAP, 2 * CAP), OP.add)
+
+        def put_q():
+            tt(A("qn", CAP, 2 * CAP), A("dq"), A("p7", CAP, 2 * CAP), OP.mult)
+            cp(IND(Qw, A("al", 0, 2 * AC)), A("qn"))
+
+        if not last:
+            put_z()
+            act(A("zs"), IND(Zw, A("zrl", 0, RC)))
+            exchange("zs", "zl%d" % ((rnd + 1) % 2), B, "za%d" % (rnd + 1), "zsent", 2)
+            tt(A("dq"), qn, q0e, OP.subtract)
+            put_q()
+            act(A("bs"), IND(Qw, A("brl", 0, 42)))
+            exchange("bs", "bl%d" % ((rnd + 1) % 2), 2 * B, "ba%d" % (rnd + 1), "bsent", 2)
+            if rnd == 0:
+                ts(C(14), A("r16", 0, 1), -1.0, OP.mult)
+                ts(A("mrl", 0, RC), A("rm", 0, RC), float(4 * o), OP.add)
+            put_m()
+            if rnd == 0:
+                ts(A("t1"), A("xgi"), 0.0, OP.is_equal, C(14), OP.mult)
+                ms(Tw, 0.0)
+            if rnd == RO - 2:
+                clocks(A("zb", 0, EC))
+                spread_own("tw", ("p3", "p4"), (act, act))
+        else:
+            tt(A("dq"), qn, q0e, OP.subtract)
+            put_q()
+            dma("s", T.y0[:], A("qm", o, o + V))
+            dma("s", T.y1[:], A("qm", EW + o, EW + o + V))
+            cp(A("gw", 3 * V, 4 * V), IND(Tw, A("nbl", 3 * EC, PC)))
+            put_z()
+
+    for u in range(4):
+        mm(A("p0", 0, PC), win("te", 4 * u), A("tw", o + u, o + V, 4), u == 0, False)
+    for h in range(2):
+        for i in range(16):
+            mm(A("p0", 2 * EC * h, 2 * EC * (h + 1)), win("t1", i), A("gw", 2 * V * h + i, 2 * V * (h + 1), 16), False, h == 1 and i == 15)
+    ts(A("w1"), A("p0", 0, PC), -0.5, OP.is_ge, BIG, OP.mult)
+    tt(A("w2"), A("w1"), cm, OP.add)
+    ts(A("fl"), A("w2"), Z0 - 1.5, OP.min, 1.5, OP.add)
+    clocks(A("ytb", 0, EC))
+    ts(A("ytb", 64, 64 + EC), A("ytb", 192, 192 + EC), 2.0, OP.add)
+    dma("s", T.yt[:, 0:V], A("ytb", 0, EC))
+    dma("s", T.yt[:, V:2 * V], A("ytb", 64, 64 + EC))
+    halo_in("ml%d" % (RO % 2), B, ((2, 0, "p6"),))
+    cuts = (0, 36, 76, 120, 164, 204, PC)
+    for c in range(6):
+        (cp if c == 0 else act)(A("mg", 16 * cuts[c], 16 * cuts[c + 1]), IND(Mw, A("fl", cuts[c], cuts[c + 1])))
+    for c in range(6):
+        s0, s1 = 16 * cuts[c], 16 * cuts[c + 1]
+        y = A("p%d" % (3 + c % 2), 0, (s1 - s0) // 4)
+        tt(y, A("mg", s0, s1, 4), A("mg", s0 + 1, s1, 4), OP.add)
+        tt(y, y, A("mg", s0 + 2, s1, 4), OP.add)
+        tt(A("yo", s0 // 4, s1 // 4), y, A("mg", s0 + 3, s1, 4), OP.add)
+        if c % 2:
+            dma("s", T.ym[:, 4 * cuts[c - 1]:4 * cuts[c + 1]], A("yo", 4 * cuts[c - 1], 4 * cuts[c + 1]))
+
+    for op in ops:
+        for d in op["deps"]:
+            d["need"] = True
+    cnt = {}
+    for op in ops:
+        if op["tok"] is None and op["need"]:
+            s = "c" + op["q"]
+            cnt[s] = cnt.get(s, 0) + 1
+            op["tok"] = [s, cnt[s]]
+            op["inc"] = True
+    seen = {q: {} for q in Q}
+    for op in ops:
+        q = op["q"]
+        if q is None:
+            continue
+        want = {}
+        for d in op["deps"]:
+            s, v = d["tok"]
+            want[s] = max(want.get(s, 0), v)
+        for s, v in want.items():
+            if seen[q].get(s, 0) < v:
+                Q[q].wait_ge(T.sem[s], v)
+                seen[q][s] = v
+        ins = op["fn"]()
+        if op.get("inc"):
+            ins.then_inc(T.sem[op["tok"][0]], 1)
+    total.update(cnt)
+    for s, v in total.items():
+        if seen["g"].get(s, 0) < v:
+            g.wait_ge(T.sem[s], v)

@@ -37,7 +37,7 @@ SCRATCH = {k: ("sbuf", [128, v[0]], v[1]) for k, v in _SB.items()}
 for _i in range(8):
     SCRATCH["p%d" % _i] = ("psum", [128, 512], F)
 SEMAPHORES = (["cv", "ca", "ct", "cg", "zsent", "bsent", "msent", "zero", "lq"] + ["za%d" % i for i in range(RO + 1)]
-              + ["ba%d" % i for i in range(RO)] + ["ma%d" % i for i in range(1, RO + 1)] + ["d%d" % i for i in range(14)])
+              + ["ba%d" % i for i in range(RO)] + ["bc%d" % i for i in range(RO + 1)] + ["ma%d" % i for i in range(1, RO + 1)] + ["d%d" % i for i in range(14)])
 
 
 def rank_program(g, core, T, topo):
@@ -48,7 +48,7 @@ def rank_program(g, core, T, topo):
     nlo, nhi = B * r, H - B * r
     hi0 = o + V
     Q = {"v": g.vector, "a": g.scalar, "t": g.tensor, "s": g.sync, "g": g}
-    ops, acc, total, nd = [], {}, {}, [0]
+    ops, acc, total, nd, order = [], {}, {}, [0], {}
 
     def A(name, lo=0, hi=None, st=1):
         hi = (512 if name not in _SB else _SB[name][0]) if hi is None else hi
@@ -146,9 +146,10 @@ def rank_program(g, core, T, topo):
             res[0][c] = rest[n * k:(n + 1) * k]
         return res
 
-    def exchange(src, dst, w, sem, lsem, calls):
-        sent = []
-        for part in plan(core, calls):
+    def exchange(src, dst, w, sem0, lsem, calls, sem1=None):
+        sent, sems = [], (sem0, sem1 or sem0)
+        for n, part in enumerate(plan(core, calls)):
+            sem = sems[n]
             tr = []
             for c, es in part.items():
                 s = T.rank_of(c)
@@ -161,9 +162,13 @@ def rank_program(g, core, T, topo):
             sent.append(add("g", lambda tr=tr: g.remote_dma_fused(tr, local_sem=T.sem[lsem]), [], [A(src)], tok=[lsem, 0]))
         for x in sent:
             x["tok"][1] = total[lsem]
-        total[sem] = sum(len(part.get(core, ())) for c in T.cores if c != core for part in plan(c, calls))
+        came = [(sems[n], s if s < r else s - 1, len(part[core])) for n in range(calls) for s, c in enumerate(T.cores) if c != core
+                for part in [plan(c, calls)[n]] if core in part]
         acc[dst] = []
-        add(None, None, [A(dst)], [], tok=[sem, total[sem]])
+        for sem in dict.fromkeys(sems):
+            total[sem] = sum(x[2] for x in came if x[0] == sem)
+            add(None, None, [A(dst, w * x[1], w * x[1] + w) for x in came if x[0] == sem], [], tok=[sem, total[sem]])
+        order[dst] = [[x[1] for x in came if x[0] == sem] for sem in dict.fromkeys(sems)]
 
     def C(i):
         return A("col", i, i + 1)
@@ -231,7 +236,7 @@ def rank_program(g, core, T, topo):
             act(A("qm", base, base + o), A("sel", 0, o), scale=0.0)
         act(A("qm", base + o + V, base + EW), A("sel", 0, EW - o - V), scale=0.0)
     act(A("bs"), IND(Qw, A("brl", 0, 42)))
-    exchange("bs", "bl0", 2 * B, "ba0", "bsent", 2)
+    exchange("bs", "bl0", 2 * B, "ba0", "bsent", 2, "bc0")
     tt(A("w1"), A("w1"), A("pt"), OP.add)
     ts(A("si"), A("xb"), 16.0, OP.mult, C(0), OP.add)
     tt(A("w1"), A("w1"), A("w2"), OP.add)
@@ -272,10 +277,11 @@ def rank_program(g, core, T, topo):
     ts(C(7), A("r16", 12, 13), 4.0, OP.mult, A("r16", 13, 14), OP.add)
     ts(A("xa"), A("xgi"), 2, OP.arith_shift_right)
     tt(A("ul"), A("blk"), A("up"), OP.subtract)
-    act(A("ti32"), A("ti"))
-    act(A("td4"), A("ti"), scale=A("r4", 0, 1))
 
     def lane_constants():
+        act(A("lr", 0, CAP), A("st", V, V + CAP))
+        act(A("ti32"), A("ti"))
+        act(A("td4"), A("ti"), scale=A("r4", 0, 1))
         tt(C(6), A("r4", 1, 2), A("r4", 2, 3), OP.add)
         tt(C(7), C(7), A("r16", 15, 16), OP.add)
         ts(A("f4"), A("xa"), 0.0, OP.is_equal)
@@ -308,9 +314,10 @@ def rank_program(g, core, T, topo):
             eng[1 if nlo else 0](A(name, hi0, hi0 + nhi), A(banks[1], 0, nhi))
 
     def halo_in(land, w, fields):
-        for f, at, bank in fields:
-            for p in range(N - 1):
-                mm(A(bank, B * p, B * p + B), A("ti32", 0, 128) if p < r else A("ti32", 32, 160), A(land, w * p + at, w * p + at + B))
+        for part in order[land]:
+            for f, at, bank in fields:
+                for p in part:
+                    mm(A(bank, B * p, B * p + B), A("ti32", 0, 128) if p < r else A("ti32", 32, 160), A(land, w * p + at, w * p + at + B))
         for f, at, bank in fields:
             base, st = ((0, 1), (EW, 1), (MO, 4))[f]
             if nlo:
@@ -345,13 +352,32 @@ def rank_program(g, core, T, topo):
         for u in range(4):
             mm(A(bank, at, at + LC), win(t, 4 * u), A("lr", u, CAP, 4), u == 0, u == 3)
 
+    MC = 36
+
+    def put_part(rnd, c0, c1):
+        to = IND(Mw, A("il", 2 * LC + c0, 2 * LC + c1))
+        if rnd:
+            tt(to, A("car", 16 * c0, 16 * c1), A("ff", 16 * c0, 16 * c1), OP.subtract)
+        else:
+            ts(to, A("ff", 16 * c0, 16 * c1), -1.0, OP.mult, 0.0, OP.add)
+
+    def send_m(rnd):
+        act(A("ms"), IND(Mw, A("mrl", 0, RC)))
+        if rnd == RO - 1:
+            exchange("ms", "ml%d" % (RO % 2), B, "ma%d" % RO, "msent", 2, "bc%d" % RO)
+        else:
+            exchange("ms", "ml%d" % ((rnd + 1) % 2), B, "ma%d" % (rnd + 1), "msent", 1)
+
     for rnd in range(RO):
         last = rnd == RO - 1
+        if rnd == 0:
+            z_in("zl0", "zw", (cp, act))
         for bank, e0, e1 in parts:
             mm(A(bank, 0, e1 - e0), ident, A("st", e0, e1), True, False)
             mm(A(bank, 0, e1 - e0), A("dz"), A("zw", o + e0, o + e1), False, False)
-        act(A("lr", 0, CAP), A("st", V, V + CAP))
-        z_in("zl%d" % (rnd % 2), "zw", (cp, act))
+        if rnd:
+            act(A("lr", 0, CAP), A("st", V, V + CAP))
+            z_in("zl%d" % (rnd % 2), "zw", (cp, act))
         for q, c0, c1, h in chunks:
             (cp if q == "v" else act)(A("gw", 16 * c0, 16 * c1), IND(Zw, A("nbl", c0, c1)))
         for q, c0, c1, h in chunks:
@@ -369,6 +395,9 @@ def rank_program(g, core, T, topo):
             mm(A("p2", 0, EC), win("tx", i), A("fail", i, V, 16), i == 0, i == 15)
         if rnd == 0:
             lane_constants()
+        else:
+            put_part(rnd - 1, MC, LC)
+            send_m(rnd - 1)
         ts(A("can", 1, 1 + EC), A("p2", 0, EC), 0.5, OP.is_lt)
         mm(A("p3", 0, EC), A("ul"), A("can", 1, 1 + EC), True, False)
         mm(A("p3", 0, EC), A("up"), A("can", 0, EC), False, True)
@@ -381,7 +410,7 @@ def rank_program(g, core, T, topo):
         halo_in("bl%d" % (rnd % 2), 2 * B, ((0, 0, "p5"), (1, B, "p6")))
         lanes("td4", "p4", 0)
         lanes("te", "p4", LC)
-        lanes("tl", "p4", 2 * LC)
+        lanes("tl", "p1", 0)
         for i in range(16):
             mm(A("p3", 0, AC), win("ta", i), A("lr", i, CAP, 16), i == 0, i == 15)
         lanes("tn", "p2", 0)
@@ -389,112 +418,118 @@ def rank_program(g, core, T, topo):
         lanes("ts", "p5", LC)
         D, E = A("p4", 0, LC), A("p4", LC, 2 * LC)
         ts(W(0, 2), A("p4", 0, 2 * LC), M8, OP.add, M8, OP.subtract)
-        ts(CO(0), A("p4", 2 * LC, 3 * LC), C(8), OP.is_lt, 0.5, OP.subtract)
+        ts(CO(0), A("p1", 0, LC), C(8), OP.is_lt, 0.5, OP.subtract)
         tt(W(2), E, W(1), OP.subtract)
         ts(W(3), W(0), -1.125, OP.mult, 0.5, OP.add)
         tt(W(4), D, CO(0), OP.subtract)
         ts(W(5), W(2), 2.0, OP.add)
         tt(W(6), W(4), W(3), OP.add)
-        cp(A("al", 0, AC), A("p3", 0, AC))
-        ts(A("al", AC, 2 * AC), A("p3", 0, AC), float(EW), OP.add)
         tt(W(7), W(6), W(5), OP.add)
+        cp(A("al", 0, AC), A("p3", 0, AC))
+        tt(W(7), W(7), W(5), OP.min)
+        ts(A("al", AC, 2 * AC), A("p3", 0, AC), float(EW), OP.add)
+        ts(W(10), W(7), 0.0, OP.max, -0.5, OP.mult)
         ts(A("nl"), A("p2", 0, LC), M1, OP.add, M1, OP.subtract)
-        act(A("qe"), IND(Qw, A("al", 0, 2 * AC)))
         if rnd:
             act(W(13), W(6), AF.Relu, BIG, BIG)
             act(W(14), W(6), AF.Relu, -BIG, BIG)
+        act(A("qe"), IND(Qw, A("al", 0, 2 * AC)))
         act(A("q0n"), IND(A("qm", 0, EW), A("nl")))
         act(W(8), W(2), AF.Relu, -0.5, 0.25)
         act(CO(4), W(1), AF.Identity, 1.0, 34.0)
         act(CO(5), W(8), AF.Identity, 1.0, 0.25)
-        act(A("q1n"), IND(A("qm", EW, MO), A("nl")))
         if last:
             act(A("br"), IND(Zw, A("al", 0, AC)), AF.Identity, 0.125, M1)
             act(A("bb"), A("br"), AF.Identity, 1.0, -M1)
-        tt(W(7), W(7), W(5), OP.min)
-        ts(A("il", 2 * LC, 3 * LC), A("p5", LC, 2 * LC), C(1), OP.add)
-        ts(W(10), W(7), 0.0, OP.max, -0.5, OP.mult)
+        act(A("q1n"), IND(A("qm", EW, MO), A("nl")))
         tt(CO(1), W(10), CO(0), OP.mult)
         tt(W(11), W(10), W(5), OP.add)
         spread(1, 6)
+        ts(A("il", 2 * LC, 3 * LC), A("p5", LC, 2 * LC), C(1), OP.add)
         tt(CO(2), W(11), CO(1), OP.mult)
         tt(W(12), W(11), W(6), OP.add)
         spread(2, 2)
-        tt(CO(3), W(12), CO(1), OP.mult)
-        spread(3, 0)
         if rnd:
             tt(W(13, 2), W(13, 2), A("p5", 0, 2 * LC), OP.add)
+        tt(CO(3), W(12), CO(1), OP.mult)
+        if rnd:
             ts(A("il", 0, LC), W(13), Z0 - 1.5, OP.min, 1.5, OP.add)
-            ts(A("il", LC, 2 * LC), W(14), C(9), OP.min, C(1), OP.add)
+        spread(3, 0)
         spread(0, 4)
+
+        def carried():
+            ts(A("il", LC, 2 * LC), W(14), C(9), OP.min, C(1), OP.add)
+            act(A("car"), IND(Mw, A("il", LC, 2 * LC)))
         q0e, q1e = A("qe", 0, CAP), A("qe", CAP, 2 * CAP)
         hs = [(2 * CAP * h, 2 * CAP * (h + 1)) for h in range(2)]
-        for h in range(2):
-            for k in (2 * h, 2 * h + 1):
-                tt(A("ue", CAP * k, CAP * k + CAP), q0e, K(6, k), OP.mult)
-            for k in (2 * h, 2 * h + 1):
-                tt(K(2, k), q1e, K(2, k), OP.mult)
-        for h in range(2):
-            tt(A("ue", *hs[h]), A("ue", *hs[h]), A("p%d" % (2 + h), 0, 2 * CAP), OP.add)
+
+        def side(u, x0, x1, bank, scale, sq):
+            def X(k):
+                return A(u, CAP * k, CAP * k + CAP)
+            for h in range(2):
+                for k in (2 * h, 2 * h + 1):
+                    tt(X(k), x0(k), K(6, k), OP.mult)
+                for k in (2 * h, 2 * h + 1):
+                    tt(K(bank, k), x1(k), K(bank, k), OP.mult)
+                for k in (2 * h, 2 * h + 1):
+                    tt(X(k), X(k), K(bank, k), OP.add)
+                act(A(u, *hs[h]), A(u, *hs[h]), AF.Relu, scale)
+                act(sq(h), A(u, *hs[h]), AF.Square)
+        side("ue", lambda k: q0e, lambda k: q1e, 2, 0.125, lambda h: A("ue", *hs[h]))
         if last:
             cp(IND(Tw, A("al", 0, AC)), A("bb"))
-        act(A("ue"), A("ue"), AF.Relu, 0.125)
-        if last:
             act(A("zs"), IND(Tw, A("zrl", 0, RC)))
             exchange("zs", "zl%d" % (RO % 2), B, "za%d" % RO, "zsent", 2)
-        act(A("ue"), A("ue"), AF.Square)
-        for h in range(2):
-            for k in (2 * h, 2 * h + 1):
-                tt(A("un", CAP * k, CAP * k + CAP), A("q0n", k, L, 4), K(6, k), OP.mult)
-            for k in (2 * h, 2 * h + 1):
-                tt(K(0, k), A("q1n", k, L, 4), K(0, k), OP.mult)
-            tt(A("un", *hs[h]), A("un", *hs[h]), A("p%d" % h, 0, 2 * CAP), OP.add)
-            act(A("un", *hs[h]), A("un", *hs[h]), AF.Relu, -0.125)
-            act(A("p%d" % (2 + h), 0, 2 * CAP), A("un", *hs[h]), AF.Square)
+        side("un", lambda k: A("q0n", k, L, 4), lambda k: A("q1n", k, L, 4), 0, -0.125, lambda h: A("p%d" % (2 + h), 0, 2 * CAP))
         if rnd:
             halo_in("ml%d" % (rnd % 2), B, ((2, 0, "p6"),))
         for u in range(4):
             mm(A("p7", u, CAP, 4), A("sel", 512 * u, 512 * u + 128), CO(4))
             mm(A("p7", CAP + u, 2 * CAP, 4), A("sel", 512 * u, 512 * u + 128), CO(5))
+        q0p = A("p6", CAP, 2 * CAP)
+        act(q0p, q0e)
         if rnd:
-            act(A("car"), IND(Mw, A("il", LC, 2 * LC)))
+            carried()
 
         def put_m():
-            if rnd:
-                tt(IND(Mw, A("il", 2 * LC, 3 * LC)), A("car"), A("ff"), OP.subtract)
-            else:
-                ts(IND(Mw, A("il", 2 * LC, 3 * LC)), A("ff"), -1.0, OP.mult, 0.0, OP.add)
-            act(A("ms"), IND(Mw, A("mrl", 0, RC)))
-            exchange("ms", "ml%d" % ((rnd + 1) % 2), B, "ma%d" % (rnd + 1), "msent", 2 if last else 1)
+            put_part(rnd, 0, LC if last else MC)
+            if last:
+                send_m(rnd)
         for h in range(2):
-            tt(A("ss", *hs[h]), A("ue", *hs[h]), A("p%d" % (2 + h), 0, 2 * CAP), OP.add)
+            for k in (2 * h, 2 * h + 1):
+                tt(A("ss", CAP * k, CAP * k + CAP), A("ue", CAP * k, CAP * k + CAP), K(2, k), OP.add)
             for k in (2 * h, 2 * h + 1):
                 tt(A("ff", k, L, 4), A("ss", CAP * k, CAP * k + CAP), K(4, k), OP.mult)
         src = "ff"
+        HC = CAP // 2
         if rnd:
-            tt(A("mf"), IND(Mw, A("il", 0, LC)), A("ff"), OP.add)
+            for h in range(2):
+                tt(A("mf", *hs[h]), IND(Mw, A("il", LC // 2 * h, LC // 2 * (h + 1))), A("ff", *hs[h]), OP.add)
             src = "mf"
         if last:
-            z_in("zl%d" % (RO % 2), "tw", (act, act), ("p0", "p2"))
-            for c in range(1):
-                act(A("gw", V * c, V * c + V), IND(Tw, A("nbl", EC * c, EC * c + EC)))
             put_m()
-            for c in range(1, 3):
+            z_in("zl%d" % (RO % 2), "tw", (act, act), ("p0", "p3"))
+            for c in range(3):
                 act(A("gw", V * c, V * c + V), IND(Tw, A("nbl", EC * c, EC * c + EC)))
-        acq, qn = A("p6", 0, CAP), A("qn", 0, CAP)
-        tt(acq, q0e, A(src, 0, L, 4), OP.add)
-        tt(acq, acq, A(src, 1, L, 4), OP.add)
-        tt(acq, acq, A(src, 2, L, 4), OP.add)
-        tt(qn, acq, A(src, 3, L, 4), OP.add)
-        ts(A("cb", 0, CAP), qn, A("tht", 0, 1), OP.is_gt)
-        ts(A("cb", CAP, 2 * CAP), qn, C(10), OP.is_lt)
-        mm(A("p1", 0, CAP), A("blk"), A("cb", 0, CAP), True, False)
-        mm(A("p1", 0, CAP), A("blk"), A("cb", CAP, 2 * CAP), False, True)
+        qn = A("qn", 0, CAP)
+        for k in range(4):
+            for h in range(2):
+                j0, j1 = HC * h, HC * (h + 1)
+                tt(A("qn" if k == 3 else "p6", j0, j1), A("p6", j0 + (0 if k else CAP), j1 + (0 if k else CAP)), A(src, 4 * j0 + k, 4 * j1, 4), OP.add)
+        for h in range(2):
+            j0, j1 = HC * h, HC * (h + 1)
+            ts(A("cb", j0, j1), A("qn", j0, j1), A("tht", 0, 1), OP.is_gt)
+            ts(A("cb", CAP + j0, CAP + j1), A("qn", j0, j1), C(10), OP.is_lt)
+            mm(A("p%d" % (1 + h), 0, HC), A("blk"), A("cb", j0, j1), True, False)
+            mm(A("p%d" % (1 + h), 0, HC), A("blk"), A("cb", CAP + j0, CAP + j1), False, True)
 
         def put_z():
-            ts(A("zu", 0, CAP), A("p1", 0, CAP), 5.5, OP.is_ge, -18.0, OP.mult)
-            ts(A("zu", CAP, 2 * CAP), A("p1", 0, CAP), 9.5, OP.is_ge, -9.0, OP.mult)
-            tt(A("zu", 2 * CAP, 3 * CAP), A("zu", 0, CAP), A("p7", 0, CAP), OP.add)
+            for h in range(2):
+                j0, j1 = HC * h, HC * (h + 1)
+                ts(A("zu", j0, j1), A("p%d" % (1 + h), 0, HC), 5.5, OP.is_ge, -18.0, OP.mult)
+                if h:
+                    tt(A("zu", 2 * CAP, 3 * CAP), A("zu", 0, CAP), A("p7", 0, CAP), OP.add)
+                ts(A("zu", CAP + j0, CAP + j1), A("p%d" % (1 + h), 0, HC), 9.5, OP.is_ge, -9.0, OP.mult)
             tt(IND(Zw, A("al", 0, AC)), A("zu", 2 * CAP, 3 * CAP), A("zu", CAP, 2 * CAP), OP.add)
 
         def put_q():
@@ -505,10 +540,10 @@ def rank_program(g, core, T, topo):
             put_z()
             act(A("zs"), IND(Zw, A("zrl", 0, RC)))
             exchange("zs", "zl%d" % ((rnd + 1) % 2), B, "za%d" % (rnd + 1), "zsent", 2)
-            tt(A("dq"), qn, q0e, OP.subtract)
+            tt(A("dq"), qn, q0p, OP.subtract)
             put_q()
             act(A("bs"), IND(Qw, A("brl", 0, 42)))
-            exchange("bs", "bl%d" % ((rnd + 1) % 2), 2 * B, "ba%d" % (rnd + 1), "bsent", 2)
+            exchange("bs", "bl%d" % ((rnd + 1) % 2), 2 * B, "ba%d" % (rnd + 1), "bsent", 2, "bc%d" % (rnd + 1))
             if rnd == 0:
                 ts(C(14), A("r16", 0, 1), -1.0, OP.mult)
                 ts(A("mrl", 0, RC), A("rm", 0, RC), float(4 * o), OP.add)
@@ -520,7 +555,7 @@ def rank_program(g, core, T, topo):
                 clocks(A("zb", 0, EC))
                 spread_own("tw", ("p3", "p4"), (act, act))
         else:
-            tt(A("dq"), qn, q0e, OP.subtract)
+            tt(A("dq"), qn, q0p, OP.subtract)
             put_q()
             dma("s", T.y0[:], A("qm", o, o + V))
             dma("s", T.y1[:], A("qm", EW + o, EW + o + V))
@@ -540,15 +575,16 @@ def rank_program(g, core, T, topo):
     dma("s", T.yt[:, 0:V], A("ytb", 0, EC))
     dma("s", T.yt[:, V:2 * V], A("ytb", 64, 64 + EC))
     halo_in("ml%d" % (RO % 2), B, ((2, 0, "p6"),))
-    cuts = (0, 36, 76, 120, 164, 204, PC)
+    cuts = (0, 40, 80, 124, 166, 200, PC)
     for c in range(6):
         (cp if c == 0 else act)(A("mg", 16 * cuts[c], 16 * cuts[c + 1]), IND(Mw, A("fl", cuts[c], cuts[c + 1])))
     for c in range(6):
         s0, s1 = 16 * cuts[c], 16 * cuts[c + 1]
-        y = A("p%d" % (3 + c % 2), 0, (s1 - s0) // 4)
-        tt(y, A("mg", s0, s1, 4), A("mg", s0 + 1, s1, 4), OP.add)
-        tt(y, y, A("mg", s0 + 2, s1, 4), OP.add)
-        tt(A("yo", s0 // 4, s1 // 4), y, A("mg", s0 + 3, s1, 4), OP.add)
+        two = ((s0, (s0 + s1) // 2), ((s0 + s1) // 2, s1))
+        for k in (1, 2, 3):
+            for a0, a1 in two:
+                y = A("p%d" % (3 + c % 2), (a0 - s0) // 4, (a1 - s0) // 4)
+                tt(A("yo", a0 // 4, a1 // 4) if k == 3 else y, A("mg", a0, a1, 4) if k == 1 else y, A("mg", a0 + k, a1, 4), OP.add)
         if c % 2:
             dma("s", T.ym[:, 4 * cuts[c - 1]:4 * cuts[c + 1]], A("yo", 4 * cuts[c - 1], 4 * cuts[c + 1]))
 

@@ -4,60 +4,58 @@ from concourse.mybir import AluOpType as OP, ActivationFunctionType as AF
 N, V, B, CAP, RO = 8, 928, 48, 208, 5
 H = (N - 1) * B
 L = 4 * CAP
-EW = V + CAP + H
-MO = 2 * EW
-Z0 = 4 * EW
-MW = Z0 + 8
-SC = (V + CAP) // 4
-PC = V // 4
-AC, LC, EC, RC = CAP // 16, L // 16, V // 16, H // 16
-M1, M8, M128, BIG = 1.5 * 2.0 ** 23, 1.5 * 2.0 ** 26, 1.5 * 2.0 ** 30, 8192.0
+O0 = 32
+H0 = O0 + V
+ZC = H0 + H
+AB, AS = ZC + 16, 224
+RW = AB + AS * RO
+MOFF = 4 * H0 - 8
+MZ = 4 * AB - MOFF - 8
+PC, EC, AC, LC, RC, TC = V // 4, V // 16, CAP // 16, L // 16, H // 16, (V + H) // 16
+M2, BIG, BIGM = 1.5 * 2.0 ** 24, 8192.0, 16384.0
+LATE = (3, 4)
 F, BF, I32, U16 = "float32", "bfloat16", "int32", "uint16"
+MASTERS = ("x1", "x2", "x4", "x16", "ti", "tiz", "nti", "tb4", "nb4", "tx", "dg", "tn", "tnb", "ta", "tlo", "tid", "tih", "tow", "tq", "tr",
+           "tco", "tt4", "tdt", "dz", "dz2", "ea", "es", "ed", "e4", "en", "dts", "ncb", "blk", "up", "ul", "tf", "tac", "tb2")
 
 _SB = {
-    "qm": (MO + MW, F), "zw": (EW, BF), "tw": (EW, BF), "gw": (4 * V, BF), "st": (V + CAP, BF), "fail": (V, BF), "psb": (V, BF),
-    "lr": (2800, BF), "zl0": (H, BF), "zl1": (H, BF), "bl0": (2 * H, F), "bl1": (2 * H, F), "ml0": (H, F), "ml1": (H, F),
-    "zs": (H, BF), "bs": (2 * H, F), "ms": (H, F),
-    "pt": (PC, I32), "rm": (24, I32), "td": (128, I32), "tht": (4, F),
-    "xi": (160, I32), "xa": (160, I32), "xgi": (160, I32), "xb": (PC, I32), "col": (64, F), "coli": (8, I32),
-    "r16": (16, F), "r4": (4, F), "rk": (4, F), "br": (CAP, F), "bb": (CAP, BF),
-    "ti32": (160, F), "ti": (160, BF), "blk": (128, BF), "up": (128, BF), "ul": (128, BF), "sel": (2048, BF), "f4": (160, BF),
-    "tc": (160, BF), "tn": (160, BF), "ts": (160, BF), "tl": (160, BF), "td4": (160, BF), "te": (160, BF),
-    "ta": (160, BF), "tx": (160, BF), "t1": (160, BF), "dg": (512, BF), "dz": (128, BF), "tm": (640, BF),
-    "si": (PC, F), "cf": (PC, F), "w1": (PC, F), "w2": (PC, F),
-    "xf": (4 * SC, BF), "nbl": (PC, U16), "kk": (EC, F), "zb": (64, BF), "zf": (128, F),
-    "ri": (24, I32), "zrl": (24, U16), "brl": (48, U16), "mrl": (24, U16),
-    "can": (64, BF), "sm": (256, F), "ol": (EC, U16),
-    "al": (32, U16), "nl": (LC, U16), "il": (3 * LC, U16), "co": (6 * LC, BF), "cw": (16 * LC, F),
-    "qe": (2 * CAP, F), "q0n": (L, F), "q1n": (L, F), "car": (L, F), "ue": (L, F), "un": (L, F), "ss": (L, F),
-    "ff": (L, F), "mf": (L, F), "qn": (2 * CAP, F), "dq": (CAP, F), "cb": (2 * CAP, BF), "zu": (3 * CAP, BF),
-    "fl": (PC, U16), "mg": (4 * V, F), "yo": (V, F), "ytb": (256, F),
+    "qq": (2 * RW, F), "mm": (4 * RW - MOFF, F), "zw": (RW, BF), "td": (ZC, I32), "qr": (2 * V, BF), "gw": (4 * V, BF),
+    "st": (V, BF), "fail": (V, BF), "psb": (V, BF), "lr": (2800, BF), "hz": (H, BF), "zh": (H, BF), "kz": (CAP, BF), "ze": (CAP, BF),
+    "zl0": (H, BF), "zl1": (H, BF), "bl0": (2 * H, F), "bl1": (2 * H, F), "ml0": (H, F), "ml1": (H, F),
+    "zs": (H, BF), "bs": (2 * H, F), "ms": (H, F), "mk": (H, BF), "mh": (H, F),
+    "pt": (PC, I32), "rm": (24, I32), "tht": (4, F), "xb": (PC, I32), "col": (64, F), "coli": (16, I32), "r16": (16, F), "r4": (4, F),
+    "tl": (3 * 80, I32), "ti32": (160, F), "sel": (2048, BF), "tm": (640, BF), "kc": (3 * LC, BF), "kr": (24, BF),
+    "si": (PC, F), "w1": (PC, I32), "w2": (PC, F), "xf": (4 * PC, BF), "nbl": (PC, U16), "kk": (EC, F),
+    "ri": (24, I32), "zrl": (24, U16), "brl": (48, U16), "mrl": (24, U16), "rnl": (24, U16), "rzl": (24, U16),
+    "can": (64, BF), "sm": (256, F), "ol": (EC, U16), "ql": (32, U16), "rl": (16, U16), "al": (16, U16), "nl": (3 * LC, U16), "zn": (L, BF),
+    "il": (2 * LC, U16), "co": (4 * LC, BF), "cw": (6 * LC, F), "fg": (2 * LC, BF), "rdt": (2 * CAP, F),
+    "qe": (2 * CAP, F), "qn": (2 * L, F), "ue": (L, F), "un": (L, F), "ss": (L, F), "ff": (L, F), "mf": (L, F), "cb": (2 * CAP, BF),
+    "fl": (PC, U16), "yl": (2 * EC, U16), "mg": (L + 4 * (V + H), F), "yo": (V, F), "yq": (2 * V, F), "ytb": (128, F),
 }
+for _m in MASTERS:
+    _SB[_m] = (160, BF)
 SCRATCH = {k: ("sbuf", [128, v[0]], v[1]) for k, v in _SB.items()}
 for _i in range(8):
     SCRATCH["p%d" % _i] = ("psum", [128, 512], F)
-SEMAPHORES = (["cv", "ca", "ct", "cg", "zsent", "bsent", "msent", "zero", "lq"] + ["za%d" % i for i in range(RO + 1)]
-              + ["ba%d" % i for i in range(RO)] + ["bc%d" % i for i in range(RO + 1)] + ["ma%d" % i for i in range(1, RO + 1)] + ["d%d" % i for i in range(14)])
+SEMAPHORES = (["cv", "ca", "ct", "cg", "zsent", "bsent", "msent", "ltd"] + ["za%d" % i for i in range(RO)] + ["zc%d" % i for i in range(RO)]
+              + ["ba%d" % i for i in range(RO)] + ["bc%d" % i for i in range(RO)] + ["ma%d" % i for i in range(1, RO + 1)] + ["d%d" % i for i in range(14)])
 
 
 def rank_program(g, core, T, topo):
     r = T.rank_of(core)
     if r is None:
         return
-    o = B * r
-    nlo, nhi = B * r, H - B * r
-    hi0 = o + V
+    nhi = B * (N - 1 - r)
     Q = {"v": g.vector, "a": g.scalar, "t": g.tensor, "s": g.sync, "g": g}
-    ops, acc, total, nd, order = [], {}, {}, [0], {}
+    ops, acc, total, nd = [], {}, {}, [0]
 
-    def A(name, lo=0, hi=None, st=1):
+    def A(name, lo=0, hi=None, st=1, rows=None):
         hi = (512 if name not in _SB else _SB[name][0]) if hi is None else hi
-        if st == 1:
-            return (T[name][:, lo:hi], [(name, ((1 << (hi - lo)) - 1) << lo)], [])
-        m = 0
-        for c in range(lo, hi, st):
-            m |= 1 << c
-        return (T[name][:, lo:hi:st], [(name, m)], [])
+        m = ((1 << (hi - lo)) - 1) << lo
+        if st > 1:
+            m = sum(1 << c for c in range(lo, hi, st))
+        ap = T[name][:, lo:hi:st] if st > 1 else T[name][:, lo:hi] if rows is None else T[name][rows::16, lo:hi]
+        return (ap, [(name, m)], [])
 
     def IND(w, off):
         return (w[0].indirect(off[0]), w[1], off[1])
@@ -69,7 +67,7 @@ def rank_program(g, core, T, topo):
         for (name, m), wr in touch:
             bank = name not in _SB
             for (m2, wr2, op) in acc.get(name, []):
-                if op is me:
+                if op is me or (tok is not None and op["tok"] is not None and op["tok"][0] == tok[0] == "ltd"):
                     continue
                 if bank and op["q"] != q:
                     me["deps"].append(op)
@@ -104,13 +102,15 @@ def rank_program(g, core, T, topo):
         return add("v", lambda: g.vector.memset(out[0], c), [out], [])
 
     def act(out, x, fn=AF.Copy, scale=1.0, bias=0.0):
-        return add("a", lambda: g.scalar.activation(out[0], x[0], fn, bias=bias, scale=P(scale)), [out], [x, scale])
+        return add("a", lambda: g.scalar.activation(out[0], x[0], fn, bias=P(bias), scale=P(scale)), [out], [x, scale, bias])
 
     def mm(out, lt, rhs, start=True, stop=True):
         return add("t", lambda: g.tensor.matmul(out[0], lt[0], rhs[0], start, stop), [out], [lt, rhs])
 
-    def iota(out, step, n, base, ch):
-        return add("g", lambda: g.iota(out[0], [[step, n]], base, ch), [out], [])
+    def iota(out, pattern, base, ch, small=False):
+        if small:
+            return add("g", lambda: g.iota(out[0], pattern, base, ch, allow_small_or_imprecise_dtypes=True), [out], [])
+        return add("g", lambda: g.iota(out[0], pattern, base, ch), [out], [])
 
     def dma(q, out, x, sem=None):
         if sem is None:
@@ -123,215 +123,308 @@ def rank_program(g, core, T, topo):
 
     def plan(src, calls):
         rs = T.rank_of(src)
-        peers = [T.cores[(rs + d) % N] for d in range(1, N)]
-        far = [c for c in peers if topo.chip(c) != topo.chip(src)]
-        near = [c for c in peers if c not in far]
-        eng = topo.engines(src, far[0])
+        peers = {d: T.cores[(rs + d) % N] for d in range(1, N)}
+        far = [d for d in peers if topo.chip(peers[d]) != topo.chip(src)]
+        near = [d for d in peers if d not in far]
+        eng = topo.engines(src, peers[far[0]])
         res = []
         if calls == 1:
             spare, i, one = len(eng) - len(far), 0, {}
-            for n, c in enumerate(far):
+            for n, d in enumerate(far):
                 k = 2 if n < spare else 1
-                one[c] = eng[i:i + k]
+                one[d] = eng[i:i + k]
                 i += k
             res.append(one)
         else:
-            n1 = len(eng) // 2
-            for part in (far[:n1], far[n1:]):
+            for part in ([d for d in far if d not in LATE], [d for d in far if d in LATE]):
                 k = len(eng) // len(part)
-                res.append({c: eng[n * k:(n + 1) * k] for n, c in enumerate(part)})
-        for n, c in enumerate(near):
-            rest = [e for e in topo.engines(src, c) if e not in eng]
+                res.append({d: eng[n * k:(n + 1) * k] for n, d in enumerate(part)})
+        for n, d in enumerate(near):
+            rest = [e for e in topo.engines(src, peers[d]) if e not in eng]
             k = len(rest) // len(near)
-            res[0][c] = rest[n * k:(n + 1) * k]
+            res[0][d] = rest[n * k:(n + 1) * k]
         return res
 
     def exchange(src, dst, w, sem0, lsem, calls, sem1=None):
         sent, sems = [], (sem0, sem1 or sem0)
         for n, part in enumerate(plan(core, calls)):
-            sem = sems[n]
             tr = []
-            for c, es in part.items():
-                s = T.rank_of(c)
-                d = (s - r) % N
-                rid, pid, _ = topo.addr(c)
-                at = r if r < s else r - 1
-                tr.append(RemoteDMATransfer(dst_ids=[DstId(rid=rid, pnc=pid)], dma_engine_mask=sum(1 << e for e in es),
-                                            remote_sem=T.sem[sem], src=T[src][:, (d - 1) * w:d * w], dst=T[dst][:, at * w:(at + 1) * w]))
+            for d, es in part.items():
+                rid, pid, _ = topo.addr(T.cores[(r + d) % N])
+                tr.append(RemoteDMATransfer(dst_ids=[DstId(rid=rid, pnc=pid)], dma_engine_mask=sum(1 << e for e in es), remote_sem=T.sem[sems[n]],
+                                            src=T[src][:, (d - 1) * w:d * w], dst=T[dst][:, (N - d - 1) * w:(N - d) * w]))
             total[lsem] = total.get(lsem, 0) + sum(len(x) for x in part.values())
-            sent.append(add("g", lambda tr=tr: g.remote_dma_fused(tr, local_sem=T.sem[lsem]), [], [A(src)], tok=[lsem, 0]))
+            sent.append(add("g", lambda tr=tr: g.remote_dma_fused(tr, local_sem=T.sem[lsem]), [], [A(src, (d - 1) * w, d * w) for d in part], tok=[lsem, 0]))
         for x in sent:
             x["tok"][1] = total[lsem]
-        came = [(sems[n], s if s < r else s - 1, len(part[core])) for n in range(calls) for s, c in enumerate(T.cores) if c != core
-                for part in [plan(c, calls)[n]] if core in part]
+        came = [(sems[n], d, len(part[N - d])) for n in range(calls) for d in range(1, N)
+                for part in [plan(T.cores[(r + d) % N], calls)[n]] if N - d in part]
         acc[dst] = []
         for sem in dict.fromkeys(sems):
             total[sem] = sum(x[2] for x in came if x[0] == sem)
-            add(None, None, [A(dst, w * x[1], w * x[1] + w) for x in came if x[0] == sem], [], tok=[sem, total[sem]])
-        order[dst] = [[x[1] for x in came if x[0] == sem] for sem in dict.fromkeys(sems)]
+            add(None, None, [A(dst, w * (x[1] - 1), w * x[1]) for x in came if x[0] == sem], [], tok=[sem, total[sem]])
 
     def C(i):
         return A("col", i, i + 1)
 
-    ident, shup, shdn = A("ti", 16, 144), A("ti", 0, 128), A("ti", 32, 160)
-    Zw, Tw, Qw, Mw = A("zw"), A("tw"), A("qm", 0, MO), A("qm", MO, MO + MW)
+    def R(i):
+        return A("r16", i, i + 1)
 
-    def win(name, s):
+    def R4(i):
+        return A("r4", i, i + 1)
+
+    def win(name, s=0):
         return A(name, 16 - s, 144 - s)
 
-    dma("s", A("td", 0, EC), T.t0[:])
-    dma("a", A("td", 64, 64 + EC), T.d0[:])
+    ident = win("ti")
+    own = (O0, O0 + V)
+    s0, s1 = B * (min(LATE) - 1), B * max(LATE)
+    l0, l1 = B * (N - 1 - max(LATE)), B * (N - min(LATE))
+    early = ((0, l0, 0), (l1, H, l0))
+    late = ((l0, l1, H - (l1 - l0)),)
+
+    def sides(c0, c1):
+        return [x for x in ((c0, min(c1, nhi), -16), (max(c0, nhi), c1, 16)) if x[0] < x[1]]
+
+    def Zw(rnd):
+        return A("zw", 0, AB + AS * rnd)
+
+    def Qw(rnd):
+        return A("qq", 0, 2 * (AB + AS * rnd))
+
+    def Mw(rnd):
+        return A("mm", 0, 4 * (AB + AS * rnd) - MOFF)
+
+    Zc = A("zw", 0, ZC)
+
+    def send_z(rnd, eng, w):
+        eng[0](A("zs", 0, s0), IND(w, A("zrl", 0, s0 // 16)))
+        eng[1](A("zs", s1, H), IND(w, A("zrl", s1 // 16, RC)))
+        eng[0](A("zs", s0, s1), IND(w, A("zrl", s0 // 16, s1 // 16)))
+        exchange("zs", "zl%d" % (rnd % 2), B, "za%d" % rnd, "zsent", 2, "zc%d" % rnd)
+
+    def list_q():
+        for i in range(8):
+            mm(A("p6", 0, 2 * RC), win("tq", 2 * i), A("zs", i, H, 8), i == 0, i == 7)
+        ts(A("brl", 0, 2 * RC), A("p6", 0, 2 * RC), ODD, OP.add)
+
+    def send_q(rnd, eng):
+        eng(A("bs"), IND(Qw(rnd), A("brl", 0, 2 * RC)))
+        exchange("bs", "bl%d" % (rnd % 2), 2 * B, "ba%d" % rnd, "bsent", 2, "bc%d" % rnd)
+
+    def rim_records():
+        mm(A("p7", 0, RC), ident, A("kr", 0, RC), True, False)
+        for i in range(16):
+            mm(A("p7", 0, RC), win("tr", i), A("zs", i, H, 16), False, i == 15)
+
+    def list_m():
+        ts(A("sm", 192, 192 + RC), A("p7", 0, RC), 4.0, OP.mult, -float(MOFF), OP.add)
+        ts(A("mrl", 0, RC), A("sm", 192, 192 + RC), 0.0, OP.max)
+
+    def send_m(rnd, eng, calls=1):
+        eng(A("ms"), IND(Mw(rnd), A("mrl", 0, RC)))
+        exchange("ms", "ml%d" % (rnd % 2), B, "ma%d" % rnd, "msent", calls)
+
+    def gather_z(eng, c0, c1):
+        eng(A("gw", 16 * c0, 16 * c1), IND(Zc, A("nbl", c0, c1)))
+
+    parts = (("p0", 0, 320), ("p1", 320, 640), ("p2", 640, 816), ("p3", 816, V))
+
+    def rows_own(dz):
+        for bank, e0, e1 in parts:
+            mm(A(bank, 0, e1 - e0), ident, A("st", e0, e1), True, False)
+            mm(A(bank, 0, e1 - e0), win(dz), A("zw", O0 + e0, O0 + e1), False, False)
+
+    def rows_near(bank, e0, e1):
+        for k in range(4):
+            mm(A(bank, 0, e1 - e0), win("dg", k), A("gw", 4 * e0 + k, 4 * e1, 4), False, k == 3)
+
+    def msum(out, names, bank):
+        for n, x in enumerate(names):
+            mm(A(bank, 0, 160), ident, A(x), n == 0, n == len(names) - 1)
+        act(A(out), A(bank, 0, 160))
+
+    def eq(out, x, c, k=None):
+        return ts(A(out), A(x), c, OP.is_equal) if k is None else ts(A(out), A(x), c, OP.is_equal, k, OP.mult)
+
+    def cyclic(out, x, c, n):
+        for lo, hi, s in ((16, 144, 0.0), (0, 16, n), (144, 160, -n)):
+            ts(A(out, lo, hi), A(x, lo, hi), s, OP.add, c, OP.is_equal)
+
+    PP, P16, PK, ODD, G16, G16K, G4, G41, G2, G1, MR, DT, KT, MC = (C(i) for i in range(14))
+
+    ms(A("td"), 0)
     dma("s", A("rm", 0, RC), T.rim[:])
     dma("a", A("pt"), T.port[:])
+    dma("s", A("qr", 0, V), T.q0[:])
+    dma("a", A("qr", V, 2 * V), T.q1[:])
+    iota(A("coli", 0, 2), [[0, 2]], 0, 1)
+    iota(A("xb"), [[1, PC]], 0, 0)
+    iota(A("x1"), [[1, 160]], -16, 0, True)
+    iota(A("x2"), [[1, 80], [0, 2]], -8, 0, True)
+    iota(A("x4"), [[1, 40], [0, 4]], -4, 0, True)
+    iota(A("x16"), [[1, 10], [0, 16]], -1, 0, True)
+    ltd = [dma("s", A("td", *own, rows=4), T.t0[:], "ltd"), dma("a", A("td", *own, rows=1), T.d0[:], "ltd")]
+    for i, m in enumerate((15, 3, 1, 112)):
+        ts(A("coli", 2 + 2 * i, 3 + 2 * i), A("coli", 0, 1), m, OP.bitwise_and)
+    ts(C(14), A("coli", 2, 3), float(TC), OP.mult, float(O0), OP.add)
+    cp(A("col", 0, 5), A("coli", 0, 10, 2))
+    ts(A("tl", 0, TC), A("xb", 0, TC), C(14), OP.add)
+    ts(A("r16"), A("xb", 0, 16), P16, OP.is_equal)
+    ts(A("tl", 80, 80 + TC), A("tl", 0, TC), 4064, OP.bitwise_and)
+    ts(A("tl", 160, 160 + TC), A("tl", 0, TC), 31, OP.bitwise_and)
+    ltd += [dma("sa"[i % 2], A("td", O0, ZC, rows=row), A("tl", at, at + TC), "ltd") for i, (row, at) in enumerate(((2, 80), (3, 160), (8, 80), (12, 160)))]
+    for x in ltd:
+        x["tok"][1] = total["ltd"]
     dma("s", A("tht", 0, 1), T.th[:])
-    iota(A("coli", 0, 2), 0, 2, 0, 1)
-    iota(A("xi"), 1, 160, -16, -1)
-    iota(A("xb"), 1, PC, 0, 0)
-    a = dma("g", A("qm", o, o + V), T.q0[:], "lq")
-    b = dma("g", A("qm", EW + o, EW + o + V), T.q1[:], "lq")
-    a["tok"][1] = b["tok"][1]
 
-    ms(Zw, 8.0)
-    ts(A("coli", 2, 3), A("coli", 0, 1), 15, OP.bitwise_and)
-    ts(A("coli", 4, 5), A("coli", 0, 1), 3, OP.bitwise_and)
-    cp(C(0), A("coli", 2, 3))
-    cp(C(1), A("coli", 4, 5))
-    ts(A("xgi"), A("xi"), C(0), OP.add)
-    ts(A("r16"), A("xb", 0, 16), C(0), OP.is_equal)
-    ts(A("xa"), A("xgi"), 4, OP.arith_shift_right)
-    tt(C(2), C(0), C(1), OP.subtract)
-    ts(A("blk"), A("xa", 16, 144), 0.0, OP.is_equal)
-    for i in range(6):
-        act(A("sel", 128 * i, 128 * i + 128), A("blk"), scale=A("r16", i, i + 1))
-    for i in range(6, 16):
-        ts(A("sel", 128 * i, 128 * i + 128), A("blk"), A("r16", i, i + 1), OP.mult)
-    ts(A("zf", 0, EC), A("td", 0, EC), 8.0, OP.mult, -2.0, OP.add)
-    ts(A("zf", 64, 64 + EC), A("td", 64, 64 + EC), 9.0, OP.mult)
+    def aff(out, x, scale, bias=0.0):
+        return act(out, x, AF.Identity, scale, bias)
+    aff(C(15), PK, -1.0, P16)
+    aff(MR, R(2), 1.0, R(3))
+    aff(DT, R(0), 2.0, R(1))
+    aff(MC, R(8), 1.0, R(12))
+    aff(G2, G16, 0.5)
+    aff(C(16), MR, 2.0)
+    aff(KT, DT, 1.0, R(4))
+    aff(G1, G16, 0.0625)
+    aff(C(17), R(2), 8.0, G16)
+    aff(C(18), R(3), 4.0, R(2))
+    aff(G4, G16, 0.25)
+    aff(C(17), R(3), 12.0, C(17))
+    aff(C(18), R(4), -1.0, C(18))
+    aff(G41, G16, 0.25, 1.0)
+    aff(C(17), R(4), 4.0, C(17))
+    aff(C(20), KT, -1.0)
+    aff(G16K, G16, 1.0, PK)
+    cyclic("ti", "x1", PP, 128.0)
     ts(A("ri", 0, RC), A("rm", 0, RC), 2, OP.arith_shift_right)
-    tt(A("zb", 0, EC), A("zf", 0, EC), A("zf", 64, 64 + EC), OP.add)
-    ts(A("zrl", 0, RC), A("ri", 0, RC), float(o), OP.add)
-
-    def spread_own(name, banks, eng):
-        for i in range(16):
-            mm(A(banks[i // 8], EC * (i % 8), EC * (i % 8 + 1)), A("sel", 128 * i, 128 * i + 128), A("zb", 0, EC))
-        eng[0](A(name, o, o + 8 * EC), A(banks[0], 0, 8 * EC))
-        eng[1](A(name, o + 8 * EC, o + V), A(banks[1], 0, 8 * EC))
-    cm = A("cf")
-    ts(A("w1"), A("pt"), float(4 * V), OP.max, 3.0, OP.mult)
-    ts(A("w2"), A("pt"), 4 * V + nhi - 0.5, OP.is_ge, -float(4 * (V + H)), OP.mult)
-    spread_own("zw", ("p0", "p1"), (act, cp))
-    act(A("zs"), IND(Zw, A("zrl", 0, RC)))
-    exchange("zs", "zl0", B, "za0", "zsent", 2)
-    for cc in range(3):
-        ts(A("brl", cc, 42, 6), A("ri", cc, RC, 3), float(o), OP.add)
-        ts(A("brl", 3 + cc, 42, 6), A("ri", cc, RC, 3), float(o + EW), OP.add)
-    ts(A("xa"), A("xi"), 127, OP.bitwise_and)
-    ts(A("r4"), A("xb", 0, 16, 4), C(2), OP.is_equal)
-    ts(A("rk"), A("xb", 0, 4), C(1), OP.is_equal)
-    ts(A("ti"), A("xa"), 0.0, OP.is_equal)
+    ts(A("r4"), A("xb", 0, 16, 4), C(15), OP.is_equal)
+    ts(A("zrl", 0, RC), A("ri", 0, RC), float(O0), OP.add)
+    ts(A("w1"), A("pt"), 2, OP.arith_shift_right)
+    ts(A("p4", 0, PC), A("pt"), 4 * V - 0.5, OP.is_ge, -BIG, OP.mult)
+    ts(A("si"), A("xb"), 16.0, OP.mult, P16, OP.add)
+    ts(A("p5", 0, PC), A("pt"), 4 * V + nhi - 0.5, OP.is_ge, BIG, OP.mult)
+    tt(A("w2"), A("w1"), A("p4", 0, PC), OP.add)
     for u in range(4):
-        act(A("tm", 160 * u, 160 * u + 160), A("ti"), scale=A("r4", u, u + 1))
-    for base in (0, EW):
-        if o:
-            act(A("qm", base, base + o), A("sel", 0, o), scale=0.0)
-        act(A("qm", base + o + V, base + EW), A("sel", 0, EW - o - V), scale=0.0)
-    act(A("bs"), IND(Qw, A("brl", 0, 42)))
-    exchange("bs", "bl0", 2 * B, "ba0", "bsent", 2, "bc0")
-    tt(A("w1"), A("w1"), A("pt"), OP.add)
-    ts(A("si"), A("xb"), 16.0, OP.mult, C(0), OP.add)
-    tt(A("w1"), A("w1"), A("w2"), OP.add)
-    ts(A("w2"), A("si"), float(4 * o - 1), OP.add)
-    ts(cm, A("w1"), 4 * o - 12 * V - 1.5, OP.add)
-    ts(C(3), C(2), 0.25, OP.mult, A("rk", 1, 2), OP.mult)
-    ts(A("xf", SC, SC + PC), cm, M128, OP.add, M128, OP.subtract)
-    tt(A("w1"), cm, A("w2"), OP.is_gt)
-    tt(A("xf", 2 * SC, 2 * SC + PC), cm, A("xf", SC, SC + PC), OP.subtract)
-    ts(A("xf", 0, PC), A("w1"), 8.0, OP.mult)
-    ts(C(11), A("rk", 3, 4), float(o), OP.mult, C(3), OP.add)
-    ts(C(12), A("rk", 3, 4), float(V + H), OP.mult, C(3), OP.add)
-    ms(A("xf", PC, SC), 8.0)
-    ts(A("xf", 3 * SC, 3 * SC + PC), A("xb"), A("rk", 0, 1), OP.mult, C(11), OP.add)
-    ts(C(13), A("rk", 2, 3), 8.0, OP.mult, C(12), OP.add)
-    ms(A("xf", SC + PC, 2 * SC), 5120.0)
-    ms(A("xf", 2 * SC + PC, 3 * SC), 4 * (V + H) - 5121.5)
-    ts(A("xf", 3 * SC + PC, 4 * SC), A("xb", 0, LC), A("rk", 0, 1), OP.mult, C(13), OP.add)
-    for k in range(4):
-        act(A("dg", 128 * k, 128 * k + 128), ident, scale=A("r16", k, k + 1))
-    for j, (c0, c1) in enumerate(((0, 120), (120, PC), (PC, SC))):
+        act(A("tm", 160 * u, 160 * u + 160), A("ti"), scale=R4(u))
+    ts(A("w1"), A("pt"), 3, OP.bitwise_and)
+    tt(A("p5", 0, PC), A("si"), A("p5", 0, PC), OP.add)
+    ts(A("nbl"), A("w2"), float(O0), OP.add, 0.0, OP.max)
+    tt(A("xf", 3 * PC, 4 * PC), A("w1"), A("p4", 0, PC), OP.add)
+    tt(A("xf", 0, PC), A("pt"), A("p5", 0, PC), OP.is_gt)
+    eq("tq", "x2", G2, C(16))
+    eq("blk", "x16", G1)
+    ts(A("xf", 3 * PC, 4 * PC), A("xf", 3 * PC, 4 * PC), 0.0, OP.max)
+    ts(A("xf", PC, 2 * PC), A("xf", 0, PC), -32.0, OP.mult)
+    ts(A("xf", 2 * PC, 3 * PC), A("xf", 0, PC), 128.0, OP.mult)
+    act(A("qq", 2 * O0, 2 * H0, 2), A("qr", 0, V))
+    act(A("qq", 2 * O0 + 1, 2 * H0, 2), A("qr", V, 2 * V))
+    act(A("qq", 0, 2 * O0), A("qr", 0, 2 * O0), scale=0.0)
+
+    def static_rows(j):
         for u in range(4):
-            for f in (1, 2, 0, 3):
-                s = 160 * u + 16 - 4 * (f - u)
-                mm(A("p%d" % (2 + j), u, 4 * (c1 - c0), 4), A("tm", s, s + 128), A("xf", f * SC + c0, f * SC + c1), f == 1, f == 3)
-        act(A("st", 4 * c0, 4 * c1), A("p%d" % (2 + j), 0, 4 * (c1 - c0)))
-    ts(A("w2"), cm, 0.25, OP.mult, M1, OP.add)
-    tt(C(4), A("r16", 14, 15), A("r4", 0, 1), OP.subtract)
-    ts(C(5), A("r4", 0, 1), BIG, OP.mult)
-    ts(A("nbl"), A("w2"), M1, OP.subtract)
-    ts(A("dz"), ident, C(4), OP.mult)
-    ts(A("tx"), A("xgi"), 0.0, OP.is_equal, C(5), OP.mult)
-    ts(A("ul"), A("xi", 16, 144), -0.5, OP.is_lt)
-    ts(A("kk"), A("si", 0, EC), float(V), OP.add)
-    ms(A("can", 0, 2), 0.0)
-    ms(A("sm", 0, 2), 0.0)
-    tt(A("up"), A("ul"), A("blk"), OP.mult)
-    ts(C(7), A("r16", 12, 13), 4.0, OP.mult, A("r16", 13, 14), OP.add)
-    ts(A("xa"), A("xgi"), 2, OP.arith_shift_right)
-    tt(A("ul"), A("blk"), A("up"), OP.subtract)
+            for f, row in enumerate((0, 8, 12, 12)):
+                s = 160 * u + 16 - (row - 4 * u)
+                mm(A("p%d" % (2 + j), u, 2 * PC, 4), A("tm", s, s + 128), A("xf", f * PC + j * PC // 2, f * PC + (j + 1) * PC // 2), f == 0, f == 3)
+    static_rows(0)
+    ms(A("zw", 0, O0), -100.0)
+    ts(C(19), KT, 1.0, OP.min)
+    ts(C(21), MC, R(4), OP.add, -1.0, OP.mult)
+    send_z(0, (cp, cp), A("td"))
+    for out, step, ch, op in (("up", -1, 1, OP.is_gt), ("ul", 1, -1, OP.is_ge)):
+        add("g", lambda out=out, step=step, ch=ch, op=op: g.affine_select(win(out)[0], win("blk")[0], [[step, 128]], op, 0.0, 0, ch), [win(out)], [win("blk")])
+    eq("e4", "x4", G4, C(20))
+    eq("dz2", "x4", G41, R(4))
+    ts(A("en"), A("ti"), C(21), OP.mult)
+    eq("ea", "x1", G16, KT)
+    eq("es", "x1", C(17), C(18))
+    list_q()
+    static_rows(1)
+    cp(A("zw", O0, ZC), A("td", O0, ZC))
+    act(A("st", 0, 2 * PC), A("p2", 0, 2 * PC))
+    send_q(0, act)
+    msum("dz", ("e4", "dz2", "en"), "p5")
+    msum("dg", ("ea", "es"), "p4")
+    ts(A("tiz"), A("ti"), C(19), OP.mult)
+    ts(C(22), R4(0), BIG, OP.mult)
+    ts(C(23), R4(0), -1.0, OP.mult, 1.0, OP.add)
+    ts(C(24), R4(1), -8.0, OP.mult, R(1), OP.add)
+    cp(A("st", 2 * PC, V), A("p3", 0, 2 * PC))
+    for c0, c1, at in early + late:
+        ts(A("hz", at, at + c1 - c0), A("zw", H0 + c0, H0 + c1), MR, OP.mult)
+        i = at // 16 + (c0 == l0)
+        cp(A("rzl", i, i + (c1 - c0) // 16), A("rm", c0 // 16, c1 // 16))
+    gather_z(act, 0, 70)
+    gather_z(act, 70, 136)
+    gather_z(cp, 136, 190)
+    gather_z(cp, 190, PC)
 
-    def lane_constants():
-        act(A("lr", 0, CAP), A("st", V, V + CAP))
-        act(A("ti32"), A("ti"))
-        act(A("td4"), A("ti"), scale=A("r4", 0, 1))
-        tt(C(6), A("r4", 1, 2), A("r4", 2, 3), OP.add)
-        tt(C(7), C(7), A("r16", 15, 16), OP.add)
-        ts(A("f4"), A("xa"), 0.0, OP.is_equal)
-        ts(A("tc"), A("xgi"), C(1), OP.is_equal, C(6), OP.mult)
-        ts(A("ta"), A("xgi"), 0.0, OP.is_equal, C(7), OP.mult)
-        ts(A("ts"), A("f4"), C(7), OP.mult, 4.0, OP.mult)
-        ts(C(8), C(1), -1.5, OP.add)
-        tt(A("tl"), A("tc"), A("ts"), OP.subtract)
-        act(A("te"), A("f4"), scale=A("r16", 14, 15))
-        act(A("tn"), A("tc"), scale=0.25)
-        act(C(9), C(1), AF.Identity, -1.0, float(Z0))
-        act(C(10), A("tht", 0, 1), scale=-1.0)
-        zc = MW // 8 + 3
-        act(A("qm", MO, MO + zc), A("sel", 0, zc), scale=0.0)
-        zs_ = [dma("s", A("qm", MO + c, min(MO + MW, MO + c + 736)), A("qm", MO, MO + min(736, MW - c)), "zero") for c in range(zc, MW, 736)]
-        for x in zs_:
-            x["tok"][1] = zs_[-1]["tok"][1]
-
-    parts = (("p0", 0, 384), ("p1", 384, 768), ("p4", 768, 848), ("p7", 848, V))
-    chunks = tuple(("va"[i % 2], 24 * i, 24 * i + 24, i // 4) for i in range(8)) + (("v", 192, 212, 2), ("a", 212, PC, 3))
-
-    def z_in(land, name, eng, banks=("p5", "p6")):
-        if nlo:
-            mm(A(banks[0], 0, nlo), shup, A(land, 0, nlo))
-        if nhi:
-            mm(A(banks[1], 0, nhi), shdn, A(land, nlo, H))
-        if nlo:
-            eng[0](A(name, 0, nlo), A(banks[0], 0, nlo))
-        if nhi:
-            eng[1 if nlo else 0](A(name, hi0, hi0 + nhi), A(banks[1], 0, nhi))
-
-    def halo_in(land, w, fields):
-        for part in order[land]:
-            for f, at, bank in fields:
-                for p in part:
-                    mm(A(bank, B * p, B * p + B), A("ti32", 0, 128) if p < r else A("ti32", 32, 160), A(land, w * p + at, w * p + at + B))
-        for f, at, bank in fields:
-            base, st = ((0, 1), (EW, 1), (MO, 4))[f]
-            if nlo:
-                act(A("qm", base, base + st * nlo, st), A(bank, 0, nlo))
-            if nhi:
-                act(A("qm", base + st * hi0, base + st * (hi0 + nhi), st), A(bank, nlo, H))
-
-    def clocks(at):
-        for i in range(16):
-            mm(A("p2", 0, EC), win("t1", i), A("zw", o + EC * i, o + EC * (i + 1)), i == 0, i == 15)
-        ts(A("ytb", 128, 128 + EC), A("p2", 0, EC), M8, OP.add, M8, OP.subtract)
-        tt(A("ytb", 192, 192 + EC), A("ytb", 128, 128 + EC), A("p2", 0, EC), OP.subtract)
-        ts(A("ytb", 128, 128 + EC), A("ytb", 128, 128 + EC), -0.125, OP.mult, 2.0, OP.subtract)
-        tt(at, A("ytb", 128, 128 + EC), A("ytb", 192, 192 + EC), OP.subtract)
+    def lane_constants(part):
+        if part == 0:
+            act(A("lr", 0, CAP), A("zw", H0, H0 + CAP), AF.Identity, MR, C(24))
+            eq("tx", "x1", G16, C(22))
+            ts(A("kk"), A("si", 0, EC), float(V), OP.add)
+            ms(A("can", 0, 2), 0.0)
+            ms(A("sm", 0, 2), 0.0)
+            ts(C(25), R4(2), 2.0, OP.mult)
+            eq("tn", "x1", G16K, R4(1))
+            ts(C(26), R4(3), 0.5, OP.mult, C(25), OP.add)
+            eq("e4", "x4", G4, DT)
+            eq("tlo", "x1", G16K, R4(3))
+            eq("tih", "x1", G16K, C(26))
+            ms(A("kc", 0, LC), -0.75)
+        elif part == 1:
+            ts(C(27), R(0), 6.0, OP.mult)
+            tt(C(28), R(0), R(1), OP.add)
+            eq("tr", "x1", G16, MR)
+            ts(C(27), R(1), 11.0, OP.mult, C(27), OP.add)
+            ts(C(29), C(28), BIG, OP.mult, -BIG, OP.add)
+            ts(C(30), C(28), 3.0 - BIG, OP.mult, BIG, OP.add)
+            ts(C(27), R(2), float(AB - H0), OP.mult, C(27), OP.add)
+            tt(C(29), C(29), R(1), OP.add)
+            tt(C(30), C(30), DT, OP.subtract)
+        elif part == 2:
+            msum("ta", ("tn", "e4"), "p6")
+            act(A("ti32"), A("ti"))
+            for i in range(16):
+                act(A("sel", 128 * i, 128 * i + 128), win("blk"), scale=R(i))
+        elif part == 3:
+            eq("tco", "x1", G16, MC)
+            eq("ncb", "x2", G2, -1.0)
+        elif part == 4:
+            act(A("kz"), A("zw", H0, H0 + CAP), AF.Identity, MR, C(27))
+            act(A("ed"), A("ti"), scale=MC)
+            act(A("dts"), A("blk"), scale=DT)
+            act(C(31), A("tht", 0, 1), scale=-1.0)
+        elif part == 5:
+            ts(C(32), MR, 4.0, OP.mult)
+            ts(C(33), R(2), float(AS), OP.mult)
+            ts(A("ri", 0, RC), A("rm", 0, RC), 3, OP.bitwise_and)
+            ms(A("kc", LC, 2 * LC), 0.0)
+            ms(A("mm", 0, 8), 0.0)
+            eq("tow", "x4", G4, C(32))
+            ts(A("kr", 0, RC), A("ri", 0, RC), 0.25, OP.mult)
+            ts(A("kc", 2 * LC, 3 * LC), A("kc", LC, 2 * LC), PK, OP.add)
+        elif part == 6:
+            act(A("tid"), A("tih"), scale=2.0)
+            act(A("nti"), A("ti"), scale=-1.0)
+        elif part == 7:
+            cyclic("nb4", "x16", G1, 8.0)
+            eq("tt4", "x1", G16, R(4))
+            eq("tdt", "x1", G16, DT)
+            ts(A("rnl", 0, RC), A("rm", 0, RC), float(L), OP.add)
+            tt(C(42), G4, PK, OP.add)
+            ms(A("mm", MZ, MZ + 8), 0.0)
+            eq("tac", "x4", C(42), -BIGM)
+        else:
+            act(A("tb4"), A("nb4"), scale=R(4))
+            act(A("tb2"), A("blk"), scale=R(2))
+            act(A("nb4"), A("tb4"), scale=-1.0)
+            act(A("tnb"), A("tn"), scale=-BIGM)
+            act(A("col", 34, 38), A("r4"), scale=-1.0)
+            act(A("col", 38, 42), A("r4"), scale=CAP - 0.5)
+            msum("tf", ("tid", "tnb"), "p6")
 
     def W(i, n=1):
         return A("cw", LC * i, LC * (i + n))
@@ -348,245 +441,280 @@ def rank_program(g, core, T, topo):
     def K(bank, k):
         return A("p%d" % (bank + k // 2), CAP * (k % 2), CAP * (k % 2 + 1))
 
-    def lanes(t, bank, at):
+    def lanes(t, bank, at, start=True, stop=True):
         for u in range(4):
-            mm(A(bank, at, at + LC), win(t, 4 * u), A("lr", u, CAP, 4), u == 0, u == 3)
+            mm(A(bank, at, at + LC), win(t, 4 * u), A("lr", u, CAP, 4), start and u == 0, stop and u == 3)
 
-    MC = 36
-
-    def put_part(rnd, c0, c1):
-        to = IND(Mw, A("il", 2 * LC + c0, 2 * LC + c1))
+    def put_m(rnd):
+        to = A("mm", 4 * (AB + AS * rnd) - MOFF, 4 * (AB + AS * rnd) - MOFF + L)
         if rnd:
-            tt(to, A("car", 16 * c0, 16 * c1), A("ff", 16 * c0, 16 * c1), OP.subtract)
+            tt(to, IND(Mw(rnd), A("il", LC, 2 * LC)), A("ff"), OP.subtract)
         else:
-            ts(to, A("ff", 16 * c0, 16 * c1), -1.0, OP.mult, 0.0, OP.add)
+            ts(to, A("ff"), -1.0, OP.mult)
 
-    def send_m(rnd):
-        act(A("ms"), IND(Mw, A("mrl", 0, RC)))
-        if rnd == RO - 1:
-            exchange("ms", "ml%d" % (RO % 2), B, "ma%d" % RO, "msent", 2, "bc%d" % RO)
-        else:
-            exchange("ms", "ml%d" % ((rnd + 1) % 2), B, "ma%d" % (rnd + 1), "msent", 1)
-
+    HC = CAP // 2
+    hs = [(2 * CAP * h, 2 * CAP * (h + 1)) for h in range(2)]
     for rnd in range(RO):
         last = rnd == RO - 1
+        zl, bl, ml = ("%s%d" % (x, rnd % 2) for x in ("zl", "bl", "ml"))
+        rec = AB + AS * rnd
+        rows_own("dz")
+        ins = []
+        for bank, pieces in (("p4", early), ("p5", late)):
+            a0, a1 = pieces[0][2], pieces[-1][2] + pieces[-1][1] - pieces[-1][0]
+            mm(A(bank, 0, a1 - a0), ident, A("hz", a0, a1), True, False)
+            ins.append((bank, a0, a1, [(x0, x1, at + x0 - c0 - a0, s) for c0, c1, at in pieces for x0, x1, s in sides(c0, c1)]))
+        for bank, a0, a1, todo in ins:
+            for n, (x0, x1, at, s) in enumerate(todo):
+                mm(A(bank, at, at + x1 - x0), win("tiz", s), A(zl, x0, x1), False, n == len(todo) - 1)
+            (cp if a0 else act)(A("zh", a0, a1), A(bank, 0, a1 - a0))
+            cp(IND(A("gw"), A("rzl", a0 // 16 + (a0 > 0), a1 // 16 + (a0 > 0))), A("zh", a0, a1))
         if rnd == 0:
-            z_in("zl0", "zw", (cp, act))
-        for bank, e0, e1 in parts:
-            mm(A(bank, 0, e1 - e0), ident, A("st", e0, e1), True, False)
-            mm(A(bank, 0, e1 - e0), A("dz"), A("zw", o + e0, o + e1), False, False)
-        if rnd:
-            act(A("lr", 0, CAP), A("st", V, V + CAP))
-            z_in("zl%d" % (rnd % 2), "zw", (cp, act))
-        for q, c0, c1, h in chunks:
-            (cp if q == "v" else act)(A("gw", 16 * c0, 16 * c1), IND(Zw, A("nbl", c0, c1)))
-        for q, c0, c1, h in chunks:
-            bank, e0, e1 = parts[h]
-            for k in range(4):
-                mm(A(bank, 4 * c0 - e0, 4 * c1 - e0), A("dg", 128 * k, 128 * k + 128), A("gw", 16 * c0 + k, 16 * c1, 4), False, 4 * c1 == e1 and k == 3)
-        for h, (bank, e0, e1) in enumerate(parts):
-            if h % 2 == 0:
-                ts(A("fail", e0, e1), A(bank, 0, e1 - e0), 4.0, OP.is_lt)
-            else:
-                act(A("fail", e0, e1), A(bank, 0, e1 - e0), AF.Relu, -1.0, 4.0)
-        for bank, e0, e1 in parts[::-1]:
-            act(A("psb", e0, e1), A(bank, 0, e1 - e0))
-        for i in range(16):
-            mm(A("p2", 0, EC), win("tx", i), A("fail", i, V, 16), i == 0, i == 15)
-        if rnd == 0:
-            lane_constants()
+            lane_constants(0)
         else:
-            put_part(rnd - 1, MC, LC)
-            send_m(rnd - 1)
-        ts(A("can", 1, 1 + EC), A("p2", 0, EC), 0.5, OP.is_lt)
-        mm(A("p3", 0, EC), A("ul"), A("can", 1, 1 + EC), True, False)
-        mm(A("p3", 0, EC), A("up"), A("can", 0, EC), False, True)
-        tt(A("sm", 1, 1 + EC), A("p2", 0, EC), A("kk"), OP.min)
-        tt(A("sm", 64, 64 + EC), A("sm", 1, 1 + EC), A("sm", 0, EC), OP.subtract)
-        add("v", lambda: g.vector.tensor_tensor_scan(T.sm[:, 128:128 + EC], T.sm[:, 64:64 + EC], T.p3[:, 0:EC], -1.0, OP.add, OP.add),
-            [A("sm", 128, 128 + EC)], [A("sm", 64, 64 + EC), A("p3", 0, EC)])
-        cp(A("ol"), A("sm", 128, 128 + EC))
-        cp(IND(A("lr"), A("ol")), A("psb"))
-        halo_in("bl%d" % (rnd % 2), 2 * B, ((0, 0, "p5"), (1, B, "p6")))
-        lanes("td4", "p4", 0)
-        lanes("te", "p4", LC)
-        lanes("tl", "p1", 0)
+            act(A("lr", 0, CAP), A("zw", H0, H0 + CAP), AF.Identity, MR, C(24))
+            act(A("kz"), A("kz"), AF.Identity, 1.0, C(33))
+            put_m(rnd - 1)
+            list_m()
+        for bank, e0, e1 in parts:
+            rows_near(bank, e0, e1)
+            ts(A("fail", e0, e1), A(bank, 0, e1 - e0), 0.5, OP.is_lt)
+            act(A("psb", e0, e1), A(bank, 0, e1 - e0), AF.Copy, C(23))
         for i in range(16):
-            mm(A("p3", 0, AC), win("ta", i), A("lr", i, CAP, 16), i == 0, i == 15)
-        lanes("tn", "p2", 0)
-        lanes("tc", "p5", 0)
-        lanes("ts", "p5", LC)
-        D, E = A("p4", 0, LC), A("p4", LC, 2 * LC)
-        ts(W(0, 2), A("p4", 0, 2 * LC), M8, OP.add, M8, OP.subtract)
-        ts(CO(0), A("p1", 0, LC), C(8), OP.is_lt, 0.5, OP.subtract)
-        tt(W(2), E, W(1), OP.subtract)
-        ts(W(3), W(0), -1.125, OP.mult, 0.5, OP.add)
-        tt(W(4), D, CO(0), OP.subtract)
-        ts(W(5), W(2), 2.0, OP.add)
-        tt(W(6), W(4), W(3), OP.add)
-        tt(W(7), W(6), W(5), OP.add)
-        cp(A("al", 0, AC), A("p3", 0, AC))
-        tt(W(7), W(7), W(5), OP.min)
-        ts(A("al", AC, 2 * AC), A("p3", 0, AC), float(EW), OP.add)
-        ts(W(10), W(7), 0.0, OP.max, -0.5, OP.mult)
-        ts(A("nl"), A("p2", 0, LC), M1, OP.add, M1, OP.subtract)
+            mm(A("p6", 0, EC), win("tx", i), A("fail", i, V, 16), i == 0, i == 15)
+        if rnd < 2:
+            lane_constants(1 + 6 * rnd)
+        ts(A("can", 1, 1 + EC), A("p6", 0, EC), 0.5, OP.is_lt)
+        mm(A("p7", 0, EC), win("ul"), A("can", 1, 1 + EC), True, False)
+        mm(A("p7", 0, EC), win("up"), A("can", 0, EC), False, True)
+        tt(A("sm", 1, 1 + EC), A("p6", 0, EC), A("kk"), OP.min)
+        tt(A("sm", 64, 64 + EC), A("sm", 1, 1 + EC), A("sm", 0, EC), OP.subtract)
+        add("v", lambda: g.vector.tensor_tensor_scan(T.sm[:, 128:128 + EC], T.sm[:, 64:64 + EC], T.p7[:, 0:EC], -1.0, OP.add, OP.add),
+            [A("sm", 128, 128 + EC)], [A("sm", 64, 64 + EC), A("p7", 0, EC)])
+        cp(A("ol"), A("sm", 128, 128 + EC))
+        tt(IND(A("lr"), A("ol")), A("psb"), A("zw", *own), OP.add)
+        if rnd < 3:
+            lane_constants((2, 6, 8)[rnd])
         if rnd:
-            act(W(13), W(6), AF.Relu, BIG, BIG)
-            act(W(14), W(6), AF.Relu, -BIG, BIG)
-        act(A("qe"), IND(Qw, A("al", 0, 2 * AC)))
-        act(A("q0n"), IND(A("qm", 0, EW), A("nl")))
-        act(W(8), W(2), AF.Relu, -0.5, 0.25)
-        act(CO(4), W(1), AF.Identity, 1.0, 34.0)
-        act(CO(5), W(8), AF.Identity, 1.0, 0.25)
+            send_m(rnd, act)
         if last:
-            act(A("br"), IND(Zw, A("al", 0, AC)), AF.Identity, 0.125, M1)
-            act(A("bb"), A("br"), AF.Identity, 1.0, -M1)
-        act(A("q1n"), IND(A("qm", EW, MO), A("nl")))
-        tt(CO(1), W(10), CO(0), OP.mult)
-        tt(W(11), W(10), W(5), OP.add)
-        spread(1, 6)
-        ts(A("il", 2 * LC, 3 * LC), A("p5", LC, 2 * LC), C(1), OP.add)
-        tt(CO(2), W(11), CO(1), OP.mult)
-        tt(W(12), W(11), W(6), OP.add)
-        spread(2, 2)
+            for j in range(2):
+                e0, e1 = V // 2 * j, V // 2 * (j + 1)
+                mm(A("p%d" % j, 0, V // 2), ident, A("psb", e0, e1), True, False)
+                mm(A("p%d" % j, 0, V // 2), ident, A("zw", O0 + e0, O0 + e1), False, True)
+                act(A("fail", e0, e1), A("p%d" % j, 0, V // 2), AF.Relu, 1.0, R4(1))
+            for u in range(4):
+                act(A("xf", 64 * u, 64 * u + EC), A("sm", 128, 128 + EC), AF.Relu, C(34 + u), C(38 + u))
+        for bank, (c0, c1, at) in zip(("p4", "p5", "p6"), early + late):
+            for x0, x1, s in sides(c0, c1):
+                mm(A(bank, 2 * (x0 - c0), 2 * (x1 - c0)), win("ti32", s), A(bl, 2 * x0, 2 * x1))
+            act(A("qq", 2 * (H0 + c0), 2 * (H0 + c1)), A(bank, 0, 2 * (c1 - c0)))
+        mm(A("p2", 0, LC), ident, A("kc", 0, LC), True, False)
         if rnd:
-            tt(W(13, 2), W(13, 2), A("p5", 0, 2 * LC), OP.add)
-        tt(CO(3), W(12), CO(1), OP.mult)
+            mm(A("p3", 0, 2 * LC), ident, A("kc", LC, 3 * LC), True, False)
+        else:
+            lane_constants(3)
+        for i in range(8):
+            mm(A("p1", 0, 2 * AC), win("tq", 2 * i), A("lr", i, CAP, 8), i == 0, i == 7)
+        lanes("tn", "p0", 0)
+        lanes("ta", "p0", LC)
+        lanes("tlo", "p7", 0)
+        lanes("tih", "p2", 0, False)
+        nn, aa = A("p0", 0, LC), A("p0", LC, 2 * LC)
+        ts(A("ql", 0, 2 * AC), A("p1", 0, 2 * AC), ODD, OP.add)
+        act(A("qe"), IND(Qw(rnd), A("ql", 0, 2 * AC)))
+        ts(W(0, 2), A("p0", 0, 2 * LC), 0.0, OP.max, -0.5, OP.mult)
+        ts(CO(0), A("p7", 0, LC), 127.5, OP.is_lt, 0.5, OP.subtract)
+        tt(W(2), W(1), W(0), OP.subtract)
+        ts(A("nl", 0, LC), A("p2", 0, LC), M2, OP.add, M2, OP.subtract)
+        tt(CO(1), W(2), CO(0), OP.mult)
+        tt(W(3), W(2), aa, OP.add)
+        spread(1, 4)
+        tt(W(4), W(3), nn, OP.subtract)
+        tt(CO(3), W(3), CO(1), OP.mult)
+        tt(CO(2), W(4), CO(1), OP.mult)
+        spread(2, 6)
+        ts(A("nl", LC, 2 * LC), A("nl", 0, LC), 1.0, OP.add)
+        act(A("qn", 0, L), IND(Qw(rnd), A("nl", 0, LC)))
         if rnd:
-            ts(A("il", 0, LC), W(13), Z0 - 1.5, OP.min, 1.5, OP.add)
+            lanes("tn", "p1", 64)
+            lanes("tid", "p3", 0, False, False)
+            lanes("tow", "p3", LC, False, False)
+        for i in range(16):
+            mm(A("p2", 128, 128 + AC), win("tr", i), A("lr", i, CAP, 16), i == 0, i == 15)
+        if rnd:
+            act(A("fg", 0, LC), A("p1", 64, 64 + LC), AF.Relu, BIGM, BIGM)
+            act(A("fg", LC, 2 * LC), A("p1", 64, 64 + LC), AF.Relu, -BIGM, BIGM)
+        act(A("qn", L, 2 * L), IND(Qw(rnd), A("nl", LC, 2 * LC)))
+        if rnd:
+            mm(A("p3", 0, 2 * LC), win("nti"), A("fg"), False, True)
         spread(3, 0)
-        spread(0, 4)
+        q0e, q1e = A("qe", 0, 2 * CAP, 2), A("qe", 1, 2 * CAP, 2)
 
-        def carried():
-            ts(A("il", LC, 2 * LC), W(14), C(9), OP.min, C(1), OP.add)
-            act(A("car"), IND(Mw, A("il", LC, 2 * LC)))
-        q0e, q1e = A("qe", 0, CAP), A("qe", CAP, 2 * CAP)
-        hs = [(2 * CAP * h, 2 * CAP * (h + 1)) for h in range(2)]
-
-        def side(u, x0, x1, bank, scale, sq):
+        def side(u, x0, x1, bank, scale, sq, between):
             def X(k):
                 return A(u, CAP * k, CAP * k + CAP)
             for h in range(2):
                 for k in (2 * h, 2 * h + 1):
-                    tt(X(k), x0(k), K(6, k), OP.mult)
+                    tt(X(k), x0(k), K(4, k), OP.mult)
                 for k in (2 * h, 2 * h + 1):
                     tt(K(bank, k), x1(k), K(bank, k), OP.mult)
+                between(h)
                 for k in (2 * h, 2 * h + 1):
                     tt(X(k), X(k), K(bank, k), OP.add)
                 act(A(u, *hs[h]), A(u, *hs[h]), AF.Relu, scale)
                 act(sq(h), A(u, *hs[h]), AF.Square)
-        side("ue", lambda k: q0e, lambda k: q1e, 2, 0.125, lambda h: A("ue", *hs[h]))
-        if last:
-            cp(IND(Tw, A("al", 0, AC)), A("bb"))
-            act(A("zs"), IND(Tw, A("zrl", 0, RC)))
-            exchange("zs", "zl%d" % (RO % 2), B, "za%d" % RO, "zsent", 2)
-        side("un", lambda k: A("q0n", k, L, 4), lambda k: A("q1n", k, L, 4), 0, -0.125, lambda h: A("p%d" % (2 + h), 0, 2 * CAP))
-        if rnd:
-            halo_in("ml%d" % (rnd % 2), B, ((2, 0, "p6"),))
-        for u in range(4):
-            mm(A("p7", u, CAP, 4), A("sel", 512 * u, 512 * u + 128), CO(4))
-            mm(A("p7", CAP + u, 2 * CAP, 4), A("sel", 512 * u, 512 * u + 128), CO(5))
-        q0p = A("p6", CAP, 2 * CAP)
-        act(q0p, q0e)
-        if rnd:
-            carried()
 
-        def put_m():
-            put_part(rnd, 0, LC if last else MC)
-            if last:
-                send_m(rnd)
+        def lists(h):
+            if h == 1:
+                cp(A("rl", 0, AC), A("p2", 128, 128 + AC))
+                if rnd:
+                    ts(A("il"), A("p3", 0, 2 * LC), -float(MOFF), OP.add, 0.0, OP.max)
+                if last:
+                    ts(W(0), A("p2", 0, LC), M2, OP.add, M2, OP.subtract)
+                    ts(A("nl", 2 * LC, 3 * LC), A("nl", 0, LC), 0.5, OP.mult)
+                    tt(W(0), A("p2", 0, LC), W(0), OP.subtract)
+                    act(W(1), W(0), scale=0.5)
+                spread(0, 2)
+        side("ue", lambda k: q0e, lambda k: q1e, 6, 0.125, lambda h: A("ue", *hs[h]), lists)
+        act(A("ze"), IND(Zw(rnd), A("rl", 0, AC)))
+        if rnd == 0:
+            lane_constants(4)
+        side("un", lambda k: A("qn", k, L, 4), lambda k: A("qn", L + k, 2 * L, 4), 0, -0.125, lambda h: A("p%d" % (6 + h), 0, 2 * CAP), lambda h: None)
+        for i in range(16):
+            mm(A("p0", 0, AC), win("tco", i), A("ze", i, CAP, 16), i == 0, i == 15)
+        zu = A("zw", rec, rec + CAP)
+
+        def rows_new(bank, j0, j1, stop):
+            mm(A(bank, 0, j1 - j0), ident, A("kz", j0, j1), True, False)
+            mm(A(bank, 0, j1 - j0), win("ea", 4), A("ze", j0, j1), False, False)
+            mm(A(bank, 0, j1 - j0), win("ed"), A("ze", j0, j1), False, stop)
+        if last:
+            rows_new("p5", 0, CAP, True)
+            act(zu, A("p5", 0, CAP))
+        if rnd:
+            for x0, x1, s in sides(0, H):
+                mm(A("p4", 128 + x0, 128 + x1), win("ti32", s), A(ml, x0, x1))
+            act(A("mm", 8, 8 + 4 * H, 4), A("p4", 128, 128 + H))
+        mm(A("p1", 0, CAP), win("dts"), A("ze"))
+        q0p = A("p1", CAP, 2 * CAP)
+        act(q0p, q0e)
+        act(A("rdt", 0, CAP), A("p1", 0, CAP), AF.Relu, -0.5, 1.25)
+        for h in range(2):
+            rows_new("p%d" % (4 + h), HC * h, HC * h + HC, False)
         for h in range(2):
             for k in (2 * h, 2 * h + 1):
-                tt(A("ss", CAP * k, CAP * k + CAP), A("ue", CAP * k, CAP * k + CAP), K(2, k), OP.add)
+                tt(A("ss", CAP * k, CAP * k + CAP), A("ue", CAP * k, CAP * k + CAP), K(6, k), OP.add)
+            if h == 0:
+                cp(A("al", 0, AC), A("p0", 0, AC))
+                if last:
+                    for u in range(4):
+                        mm(A("p0", 128, 128 + PC), win("tf", 4 * u), A("fail", u, V, 4), u == 0, False)
+                    for u in range(4):
+                        mm(A("p0", 128 + u, 128 + PC, 4), win("tac"), A("xf", 64 * u, 64 * u + EC), False, u == 3)
             for k in (2 * h, 2 * h + 1):
-                tt(A("ff", k, L, 4), A("ss", CAP * k, CAP * k + CAP), K(4, k), OP.mult)
+                tt(A("ff", k, L, 4), A("ss", CAP * k, CAP * k + CAP), K(2, k), OP.mult)
+            if h == 0 and last:
+                cp(IND(Zc, A("al", 0, AC)), zu)
+                act(A("zs"), IND(Zc, A("zrl", 0, RC)))
+            if h == 1 and last:
+                ts(A("fl"), A("p0", 128, 128 + PC), -float(MOFF + MZ), OP.add, 0.0, OP.max)
+        act(A("rdt", CAP, 2 * CAP), A("rdt", 0, CAP), AF.Identity, 1.0, 0.25)
+        if last:
+            mm(A("p6", 0, H), win("nb4"), A("zs"), True, False)
+            todo = sides(0, H)
+            for n, (x0, x1, s) in enumerate(todo):
+                mm(A("p6", x0, x1), win("tb4", s), A(zl, x0, x1), False, n == len(todo) - 1)
+            rim_records()
+            put_m(rnd)
+            list_m()
+            ts(A("mk"), A("p6", 0, H), -0.5, OP.is_lt)
+            send_m(RO, lambda out, x: tt(out, x, A("mk"), OP.mult), 2)
+            act(A("zn"), IND(Zw(rnd), A("nl", 2 * LC, 3 * LC)))
+            for c0, c1 in ((0, 80), (80, 160), (160, PC)):
+                act(A("mg", L + 16 * c0, L + 16 * c1), IND(A("mm", MZ, 4 * rec - MOFF), A("fl", c0, c1)))
+            for i in range(16):
+                mm(A("p0", 0, LC), win("tco", i), A("zn", i, L, 16), i == 0, i == 15)
+            for i in range(16):
+                mm(A("p7", 0, EC), win("tr", i), A("zw", O0 + i, H0, 16), i == 0, i == 15)
+            mm(A("p6", 0, H), win("tb2"), A("zs"))
         src = "ff"
-        HC = CAP // 2
         if rnd:
             for h in range(2):
-                tt(A("mf", *hs[h]), IND(Mw, A("il", LC // 2 * h, LC // 2 * (h + 1))), A("ff", *hs[h]), OP.add)
+                tt(A("mf", *hs[h]), IND(Mw(rnd), A("il", LC // 2 * h, LC // 2 * (h + 1))), A("ff", *hs[h]), OP.add)
             src = "mf"
-        if last:
-            put_m()
-            z_in("zl%d" % (RO % 2), "tw", (act, act), ("p0", "p3"))
-            for c in range(3):
-                act(A("gw", V * c, V * c + V), IND(Tw, A("nbl", EC * c, EC * c + EC)))
-        qn = A("qn", 0, CAP)
+
+        def q0n(j0, j1):
+            return A("qq", 2 * (rec + j0), 2 * (rec + j1), 2)
         for k in range(4):
             for h in range(2):
                 j0, j1 = HC * h, HC * (h + 1)
-                tt(A("qn" if k == 3 else "p6", j0, j1), A("p6", j0 + (0 if k else CAP), j1 + (0 if k else CAP)), A(src, 4 * j0 + k, 4 * j1, 4), OP.add)
+                tt(q0n(j0, j1) if k == 3 else A("p1", j0, j1), A("p1", j0 + (0 if k else CAP), j1 + (0 if k else CAP)), A(src, 4 * j0 + k, 4 * j1, 4), OP.add)
         for h in range(2):
             j0, j1 = HC * h, HC * (h + 1)
-            ts(A("cb", j0, j1), A("qn", j0, j1), A("tht", 0, 1), OP.is_gt)
-            ts(A("cb", CAP + j0, CAP + j1), A("qn", j0, j1), C(10), OP.is_lt)
-            mm(A("p%d" % (1 + h), 0, HC), A("blk"), A("cb", j0, j1), True, False)
-            mm(A("p%d" % (1 + h), 0, HC), A("blk"), A("cb", CAP + j0, CAP + j1), False, True)
+            ts(A("cb", j0, j1), q0n(j0, j1), A("tht", 0, 1), OP.is_gt)
+            ts(A("cb", CAP + j0, CAP + j1), q0n(j0, j1), C(31), OP.is_lt)
+            mm(A("p%d" % (4 + h), 0, HC), win("ncb"), A("cb", j0, j1), False, False)
+            mm(A("p%d" % (4 + h), 0, HC), win("ncb"), A("cb", CAP + j0, CAP + j1), False, True)
 
         def put_z():
             for h in range(2):
-                j0, j1 = HC * h, HC * (h + 1)
-                ts(A("zu", j0, j1), A("p%d" % (1 + h), 0, HC), 5.5, OP.is_ge, -18.0, OP.mult)
-                if h:
-                    tt(A("zu", 2 * CAP, 3 * CAP), A("zu", 0, CAP), A("p7", 0, CAP), OP.add)
-                ts(A("zu", CAP + j0, CAP + j1), A("p%d" % (1 + h), 0, HC), 9.5, OP.is_ge, -9.0, OP.mult)
-            tt(IND(Zw, A("al", 0, AC)), A("zu", 2 * CAP, 3 * CAP), A("zu", CAP, 2 * CAP), OP.add)
+                ts(A("zw", rec + HC * h, rec + HC * h + HC), A("p%d" % (4 + h), 0, HC), C(29), OP.max, C(30), OP.min)
+            cp(IND(Zc, A("al", 0, AC)), zu)
 
         def put_q():
-            tt(A("qn", CAP, 2 * CAP), A("dq"), A("p7", CAP, 2 * CAP), OP.mult)
-            cp(IND(Qw, A("al", 0, 2 * AC)), A("qn"))
+            tt(A("p1", 0, CAP), q0n(0, CAP), q0p, OP.subtract)
+            tt(A("qq", 2 * rec + 1, 2 * (rec + CAP), 2), A("rdt", CAP, 2 * CAP), A("p1", 0, CAP), OP.mult)
 
         if not last:
             put_z()
-            act(A("zs"), IND(Zw, A("zrl", 0, RC)))
-            exchange("zs", "zl%d" % ((rnd + 1) % 2), B, "za%d" % (rnd + 1), "zsent", 2)
-            tt(A("dq"), qn, q0p, OP.subtract)
+            send_z(rnd + 1, (act, cp), Zc)
+            gather_z(act, 0, 60)
             put_q()
-            act(A("bs"), IND(Qw, A("brl", 0, 42)))
-            exchange("bs", "bl%d" % ((rnd + 1) % 2), 2 * B, "ba%d" % (rnd + 1), "bsent", 2, "bc%d" % (rnd + 1))
+            list_q()
+            send_q(rnd + 1, cp)
+            gather_z(act, 60, 110)
+            gather_z(act, 110, 146)
+            gather_z(cp, 146, 190)
+            gather_z(cp, 190, PC)
             if rnd == 0:
-                ts(C(14), A("r16", 0, 1), -1.0, OP.mult)
-                ts(A("mrl", 0, RC), A("rm", 0, RC), float(4 * o), OP.add)
-            put_m()
-            if rnd == 0:
-                ts(A("t1"), A("xgi"), 0.0, OP.is_equal, C(14), OP.mult)
-                ms(Tw, 0.0)
-            if rnd == RO - 2:
-                clocks(A("zb", 0, EC))
-                spread_own("tw", ("p3", "p4"), (act, act))
-        else:
-            tt(A("dq"), qn, q0p, OP.subtract)
-            put_q()
-            dma("s", T.y0[:], A("qm", o, o + V))
-            dma("s", T.y1[:], A("qm", EW + o, EW + o + V))
-            cp(A("gw", 3 * V, 4 * V), IND(Tw, A("nbl", 3 * EC, PC)))
-            put_z()
+                lane_constants(5)
+            rim_records()
 
-    for u in range(4):
-        mm(A("p0", 0, PC), win("te", 4 * u), A("tw", o + u, o + V, 4), u == 0, False)
-    for h in range(2):
+    ml = "ml%d" % (RO % 2)
+    tt(W(0), W(1), A("p0", 0, LC), OP.add)
+    ts(A("yl", 0, EC), A("p7", 0, EC), 2.0, OP.mult)
+    ts(W(0), W(0), 4.0, OP.mult, L + 1.5 - 4 * O0, OP.add)
+    ts(A("yl", EC, 2 * EC), A("p7", 0, EC), 2.0, OP.mult, 1.0, OP.add)
+    tt(W(0), W(0), A("si", 0, LC), OP.max)
+    put_q()
+    cp(A("il", 0, LC), W(0))
+    put_z()
+    cp(IND(A("mg"), A("il", 0, LC)), A("mm", 4 * rec - MOFF, 4 * rec - MOFF + L))
+    ts(A("mk"), A("p6", 0, H), AB + AS * (RO - 1) - 0.5, OP.is_lt)
+    for x0, x1, s in sides(0, H):
+        mm(A("p2", x0, x1), win("ti32", s), A(ml, x0, x1))
+    for j, t in enumerate(("tt4", "tdt")):
         for i in range(16):
-            mm(A("p0", 2 * EC * h, 2 * EC * (h + 1)), win("t1", i), A("gw", 2 * V * h + i, 2 * V * (h + 1), 16), False, h == 1 and i == 15)
-    ts(A("w1"), A("p0", 0, PC), -0.5, OP.is_ge, BIG, OP.mult)
-    tt(A("w2"), A("w1"), cm, OP.add)
-    ts(A("fl"), A("w2"), Z0 - 1.5, OP.min, 1.5, OP.add)
-    clocks(A("ytb", 0, EC))
-    ts(A("ytb", 64, 64 + EC), A("ytb", 192, 192 + EC), 2.0, OP.add)
-    dma("s", T.yt[:, 0:V], A("ytb", 0, EC))
-    dma("s", T.yt[:, V:2 * V], A("ytb", 64, 64 + EC))
-    halo_in("ml%d" % (RO % 2), B, ((2, 0, "p6"),))
-    cuts = (0, 40, 80, 124, 166, 200, PC)
+            mm(A("p7", 64 * (j + 1), 64 * (j + 1) + EC), win(t, i), A("zw", O0 + EC * i, O0 + EC * (i + 1)), i == 0, i == 15)
+    for j in range(2):
+        act(A("yq", V * j, V * j + V), IND(Qw(RO), A("yl", EC * j, EC * j + EC)))
+        dma("s", (T.y0, T.y1)[j][:], A("yq", V * j, V * j + V))
+    for j in range(2):
+        act(A("ytb", 64 * j, 64 * j + EC), A("p7", 64 * (j + 1), 64 * (j + 1) + EC))
+        dma("s", T.yt[:, V * j:V * (j + 1)], A("ytb", 64 * j, 64 * j + EC))
+    tt(A("mh"), A("mk"), A("p2", 0, H), OP.mult)
+    cp(IND(A("mg"), A("rnl", 0, RC)), A("mh"))
+    cuts = (0, 100, 200, 400, 600, 764, V)
     for c in range(6):
-        (cp if c == 0 else act)(A("mg", 16 * cuts[c], 16 * cuts[c + 1]), IND(Mw, A("fl", cuts[c], cuts[c + 1])))
-    for c in range(6):
-        s0, s1 = 16 * cuts[c], 16 * cuts[c + 1]
-        two = ((s0, (s0 + s1) // 2), ((s0 + s1) // 2, s1))
+        act(A("p%d" % c, 0, cuts[c + 1] - cuts[c]), A("mg", L + 4 * cuts[c], L + 4 * cuts[c + 1], 4))
+    for c in range(0, 6, 2):
         for k in (1, 2, 3):
-            for a0, a1 in two:
-                y = A("p%d" % (3 + c % 2), (a0 - s0) // 4, (a1 - s0) // 4)
-                tt(A("yo", a0 // 4, a1 // 4) if k == 3 else y, A("mg", a0, a1, 4) if k == 1 else y, A("mg", a0 + k, a1, 4), OP.add)
-        if c % 2:
-            dma("s", T.ym[:, 4 * cuts[c - 1]:4 * cuts[c + 1]], A("yo", 4 * cuts[c - 1], 4 * cuts[c + 1]))
+            for h in range(2):
+                e0, e1 = cuts[c + h], cuts[c + h + 1]
+                y = A("p%d" % (c + h), 0, e1 - e0)
+                tt(A("yo", e0, e1) if k == 3 else y, y, A("mg", L + 4 * e0 + k, L + 4 * e1, 4), OP.add)
+        dma("sa"[c // 2 % 2], T.ym[:, cuts[c]:cuts[c + 2]], A("yo", cuts[c], cuts[c + 2]))
 
     for op in ops:
         for d in op["deps"]:

@@ -6,39 +6,40 @@ H = (N - 1) * B
 L = 4 * CAP
 O0 = 32
 H0 = O0 + V
-ZC = H0 + H
+ZC = H0 + CAP
 AB, AS = ZC + 16, 224
 RW = AB + AS * RO
-MOFF = 4 * H0 - 8
-MZ = 4 * AB - MOFF - 8
-PC, EC, AC, LC, RC, TC = V // 4, V // 16, CAP // 16, L // 16, H // 16, (V + H) // 16
-M2, BIG, BIGM = 1.5 * 2.0 ** 24, 8192.0, 16384.0
+FB = 2 * RW
+MOFF = 4 * AB - 8
+PC, EC, AC, LC, RC, TC = V // 4, V // 16, CAP // 16, L // 16, H // 16, (V + CAP) // 16
+M1, BIG, BIGM = 1.5 * 2.0 ** 23, 8192.0, 16384.0
 LATE = (3, 4)
+OPT = {"q": "xim", "m": "dma", "ms": "mid", "mc": 2, "pe": "aqsn", "v": "02qs3cn4r", "e": 1, "soon0": 0, "halves": 0, "afail": 1}
 F, BF, I32, U16 = "float32", "bfloat16", "int32", "uint16"
-MASTERS = ("x1", "x2", "x4", "x16", "ti", "tiz", "nti", "tb4", "nb4", "tx", "dg", "tn", "tnb", "ta", "tlo", "tid", "tih", "tow", "tq", "tr",
-           "tco", "tt4", "tdt", "dz", "dz2", "ea", "es", "ed", "e4", "en", "dts", "ncb", "blk", "up", "ul", "tf", "tac", "tb2")
+MASTERS = ("x1", "x2", "x4", "x16", "ti", "tiz", "nti", "tx", "dg", "tn", "tnb", "ta", "tlo", "tid", "tih", "tow", "tq", "tr",
+           "tco", "tt4", "tdt", "dz", "dz2", "ea", "es", "ed", "e4", "en", "dts", "ncb", "blk", "up", "ul", "tf", "tac", "tpw", "dzl")
 
 _SB = {
-    "qq": (2 * RW, F), "mm": (4 * RW - MOFF, F), "zw": (RW, BF), "td": (ZC, I32), "qr": (2 * V, BF), "gw": (4 * V, BF),
-    "st": (V, BF), "fail": (V, BF), "psb": (V, BF), "lr": (2800, BF), "hz": (H, BF), "zh": (H, BF), "kz": (CAP, BF), "ze": (CAP, BF),
+    "qq": (RW + FB + H, F), "mm": (4 * (FB + H) - MOFF, F), "zw": (RW, BF), "td": (128, I32), "tb": (288, BF), "qr": (2 * V, BF), "gw": (4 * V, BF),
+    "st": (V, BF), "fail": (V, BF), "psb": (V, BF), "pz": (V, BF), "zq": (H0, BF), "lr": (2800, BF), "hz": (H, BF), "zh": (H, BF), "kz": (CAP, BF), "ze": (2 * CAP, BF),
     "zl0": (H, BF), "zl1": (H, BF), "bl0": (2 * H, F), "bl1": (2 * H, F), "ml0": (H, F), "ml1": (H, F),
-    "zs": (H, BF), "bs": (2 * H, F), "ms": (H, F), "mk": (H, BF), "mh": (H, F),
+    "zs": (H, BF), "bs": (2 * H, F), "ms": (H, F), "mo": (H, F), "mh": (H, F),
     "pt": (PC, I32), "rm": (24, I32), "tht": (4, F), "xb": (PC, I32), "col": (64, F), "coli": (16, I32), "r16": (16, F), "r4": (4, F),
     "tl": (3 * 80, I32), "ti32": (160, F), "sel": (2048, BF), "tm": (640, BF), "kc": (3 * LC, BF), "kr": (24, BF),
     "si": (PC, F), "w1": (PC, I32), "w2": (PC, F), "xf": (4 * PC, BF), "nbl": (PC, U16), "kk": (EC, F),
     "ri": (24, I32), "zrl": (24, U16), "brl": (48, U16), "mrl": (24, U16), "rnl": (24, U16), "rzl": (24, U16),
-    "can": (64, BF), "sm": (256, F), "ol": (EC, U16), "ql": (32, U16), "rl": (16, U16), "al": (16, U16), "nl": (3 * LC, U16), "zn": (L, BF),
+    "can": (64, BF), "sm": (256, F), "ol": (EC, U16), "ql": (32, U16), "rl": (32, U16), "al": (16, U16), "nl": (LC, U16), "pw": (H0 + CAP, BF), "pe": (CAP, BF),
     "il": (2 * LC, U16), "co": (4 * LC, BF), "cw": (6 * LC, F), "fg": (2 * LC, BF), "rdt": (2 * CAP, F),
-    "qe": (2 * CAP, F), "qn": (2 * L, F), "ue": (L, F), "un": (L, F), "ss": (L, F), "ff": (L, F), "mf": (L, F), "cb": (2 * CAP, BF),
-    "fl": (PC, U16), "yl": (2 * EC, U16), "mg": (L + 4 * (V + H), F), "yo": (V, F), "yq": (2 * V, F), "ytb": (128, F),
+    "qe": (2 * CAP, F), "qn": (2 * L, F), "ue": (L, F), "un": (L, F), "ss": (L, F), "ff": (8 + L, F), "mf": (8 + L, F), "cb": (2 * CAP, BF),
+    "fl": (PC, U16), "yl": (EC, U16), "mg": (L + 4 * V + H, F), "yo": (V, F), "yq": (2 * V, F), "ytb": (128, F),
 }
 for _m in MASTERS:
     _SB[_m] = (160, BF)
 SCRATCH = {k: ("sbuf", [128, v[0]], v[1]) for k, v in _SB.items()}
 for _i in range(8):
     SCRATCH["p%d" % _i] = ("psum", [128, 512], F)
-SEMAPHORES = (["cv", "ca", "ct", "cg", "zsent", "bsent", "msent", "ltd"] + ["za%d" % i for i in range(RO)] + ["zc%d" % i for i in range(RO)]
-              + ["ba%d" % i for i in range(RO)] + ["bc%d" % i for i in range(RO)] + ["ma%d" % i for i in range(1, RO + 1)] + ["d%d" % i for i in range(14)])
+SEMAPHORES = (["cv", "ca", "ct", "cg", "zsent", "bsent", "msent", "ltd", "hq", "hm"] + ["za%d" % i for i in range(RO)] + ["zc%d" % i for i in range(RO)]
+              + ["ba%d" % i for i in range(RO)] + ["bc%d" % i for i in range(RO)] + ["ma%d" % i for i in range(1, RO + 1)] + ["d%d" % i for i in range(15)])
 
 
 def rank_program(g, core, T, topo):
@@ -67,7 +68,7 @@ def rank_program(g, core, T, topo):
         for (name, m), wr in touch:
             bank = name not in _SB
             for (m2, wr2, op) in acc.get(name, []):
-                if op is me or (tok is not None and op["tok"] is not None and op["tok"][0] == tok[0] == "ltd"):
+                if op is me or (tok is not None and op["tok"] is not None and op["tok"][0] == tok[0] and tok[0] in ("ltd", "hq", "hm")):
                     continue
                 if bank and op["q"] != q:
                     me["deps"].append(op)
@@ -186,14 +187,24 @@ def rank_program(g, core, T, topo):
     def sides(c0, c1):
         return [x for x in ((c0, min(c1, nhi), -16), (max(c0, nhi), c1, 16)) if x[0] < x[1]]
 
+    def shift(out, land, w, sem, c0=0, c1=H, c2=0, c3=0):
+        moves = []
+        for x0, x1, s in sides(c0, c1) + sides(c2, c3):
+            for p0, p1 in ((0, 112), (112, 128)) if s < 0 else ((16, 128), (0, 16)):
+                q0 = (p0 - s) % 128
+                to, fro = A(out, w * x0, w * x1), A(land, w * x0, w * x1)
+                moves.append(dma("s", (T[out][p0:p1, w * x0:w * x1],) + to[1:], (T[land][q0:q0 + p1 - p0, w * x0:w * x1],) + fro[1:], sem))
+        for x in moves:
+            x["tok"][1] = total[sem]
+
     def Zw(rnd):
         return A("zw", 0, AB + AS * rnd)
 
-    def Qw(rnd):
-        return A("qq", 0, 2 * (AB + AS * rnd))
+    def Qw(rnd, f=None):
+        return A("qq", RW * (f or 0), RW * (1 if f is None else f) + AB + AS * rnd)
 
-    def Mw(rnd):
-        return A("mm", 0, 4 * (AB + AS * rnd) - MOFF)
+    def Mw(rnd=None):
+        return A("mm") if rnd is None else A("mm", 0, 4 * (AB + AS * rnd) - MOFF)
 
     Zc = A("zw", 0, ZC)
 
@@ -206,19 +217,19 @@ def rank_program(g, core, T, topo):
     def list_q():
         for i in range(8):
             mm(A("p6", 0, 2 * RC), win("tq", 2 * i), A("zs", i, H, 8), i == 0, i == 7)
-        ts(A("brl", 0, 2 * RC), A("p6", 0, 2 * RC), ODD, OP.add)
+        ts(A("brl", 0, 2 * RC), A("p6", 0, 2 * RC), C(16), OP.add)
 
     def send_q(rnd, eng):
         eng(A("bs"), IND(Qw(rnd), A("brl", 0, 2 * RC)))
         exchange("bs", "bl%d" % (rnd % 2), 2 * B, "ba%d" % rnd, "bsent", 2, "bc%d" % rnd)
 
-    def rim_records():
-        mm(A("p7", 0, RC), ident, A("kr", 0, RC), True, False)
+    def rim_records(bank="p7"):
+        mm(A(bank, 0, RC), ident, A("kr", 0, RC), True, False)
         for i in range(16):
-            mm(A("p7", 0, RC), win("tr", i), A("zs", i, H, 16), False, i == 15)
+            mm(A(bank, 0, RC), win("tr", i), A("zs", i, H, 16), False, i == 15)
 
-    def list_m():
-        ts(A("sm", 192, 192 + RC), A("p7", 0, RC), 4.0, OP.mult, -float(MOFF), OP.add)
+    def list_m(off=-MOFF, bank="p7"):
+        ts(A("sm", 192, 192 + RC), A(bank, 0, RC), 4.0, OP.mult, float(off), OP.add)
         ts(A("mrl", 0, RC), A("sm", 192, 192 + RC), 0.0, OP.max)
 
     def send_m(rnd, eng, calls=1):
@@ -228,15 +239,17 @@ def rank_program(g, core, T, topo):
     def gather_z(eng, c0, c1):
         eng(A("gw", 16 * c0, 16 * c1), IND(Zc, A("nbl", c0, c1)))
 
-    parts = (("p0", 0, 320), ("p1", 320, 640), ("p2", 640, 816), ("p3", 816, V))
+    parts = (("p0", 0, 320), ("p1", 320, 480), ("p2", 480, 784), ("p3", 784, V))
+    if not OPT["halves"]:
+        parts = (("p0", 0, 320), ("p1", 320, 640), ("p2", 640, 832), ("p3", 832, V))
 
     def rows_own(dz):
         for bank, e0, e1 in parts:
             mm(A(bank, 0, e1 - e0), ident, A("st", e0, e1), True, False)
             mm(A(bank, 0, e1 - e0), win(dz), A("zw", O0 + e0, O0 + e1), False, False)
 
-    def rows_near(bank, e0, e1):
-        for k in range(4):
+    def rows_near(bank, e0, e1, ports=range(4)):
+        for k in ports:
             mm(A(bank, 0, e1 - e0), win("dg", k), A("gw", 4 * e0 + k, 4 * e1, 4), False, k == 3)
 
     def msum(out, names, bank):
@@ -253,18 +266,18 @@ def rank_program(g, core, T, topo):
 
     PP, P16, PK, ODD, G16, G16K, G4, G41, G2, G1, MR, DT, KT, MC = (C(i) for i in range(14))
 
-    ms(A("td"), 0)
+    ms(A("zw", O0, ZC), 0.0)
+    dma("s", A("td", 0, EC), T.t0[:])
+    dma("a", A("td", 64, 64 + EC), T.d0[:])
     dma("s", A("rm", 0, RC), T.rim[:])
     dma("a", A("pt"), T.port[:])
-    dma("s", A("qr", 0, V), T.q0[:])
-    dma("a", A("qr", V, 2 * V), T.q1[:])
     iota(A("coli", 0, 2), [[0, 2]], 0, 1)
     iota(A("xb"), [[1, PC]], 0, 0)
     iota(A("x1"), [[1, 160]], -16, 0, True)
     iota(A("x2"), [[1, 80], [0, 2]], -8, 0, True)
     iota(A("x4"), [[1, 40], [0, 4]], -4, 0, True)
     iota(A("x16"), [[1, 10], [0, 16]], -1, 0, True)
-    ltd = [dma("s", A("td", *own, rows=4), T.t0[:], "ltd"), dma("a", A("td", *own, rows=1), T.d0[:], "ltd")]
+    ms(A("zw", 0, O0), -100.0)
     for i, m in enumerate((15, 3, 1, 112)):
         ts(A("coli", 2 + 2 * i, 3 + 2 * i), A("coli", 0, 1), m, OP.bitwise_and)
     ts(C(14), A("coli", 2, 3), float(TC), OP.mult, float(O0), OP.add)
@@ -273,9 +286,17 @@ def rank_program(g, core, T, topo):
     ts(A("r16"), A("xb", 0, 16), P16, OP.is_equal)
     ts(A("tl", 80, 80 + TC), A("tl", 0, TC), 4064, OP.bitwise_and)
     ts(A("tl", 160, 160 + TC), A("tl", 0, TC), 31, OP.bitwise_and)
-    ltd += [dma("sa"[i % 2], A("td", O0, ZC, rows=row), A("tl", at, at + TC), "ltd") for i, (row, at) in enumerate(((2, 80), (3, 160), (8, 80), (12, 160)))]
+    cp(A("tb", 0, TC), A("tl", 80, 80 + TC))
+    cp(A("tb", 80, 80 + TC), A("tl", 160, 160 + TC))
+    ltd = [dma("s", A("zw", O0, ZC, rows=row), A("tb", at, at + TC), "ltd") for row, at in ((2, 0), (3, 80), (8, 0), (12, 80))]
+    cyclic("ti", "x1", PP, 128.0)
+    cp(A("tb", 160, 160 + EC), A("td", 0, EC))
+    cp(A("tb", 224, 224 + EC), A("td", 64, 64 + EC))
+    ltd += [dma("s", A("zw", *own, rows=row), A("tb", at, at + EC), "ltd") for row, at in ((4, 160), (1, 224))]
     for x in ltd:
         x["tok"][1] = total["ltd"]
+    dma("s", A("qr", 0, V), T.q0[:])
+    dma("s", A("qr", V, 2 * V), T.q1[:])
     dma("s", A("tht", 0, 1), T.th[:])
 
     def aff(out, x, scale, bias=0.0):
@@ -285,7 +306,7 @@ def rank_program(g, core, T, topo):
     aff(DT, R(0), 2.0, R(1))
     aff(MC, R(8), 1.0, R(12))
     aff(G2, G16, 0.5)
-    aff(C(16), MR, 2.0)
+    aff(C(16), ODD, float(RW))
     aff(KT, DT, 1.0, R(4))
     aff(G1, G16, 0.0625)
     aff(C(17), R(2), 8.0, G16)
@@ -297,7 +318,6 @@ def rank_program(g, core, T, topo):
     aff(C(17), R(4), 4.0, C(17))
     aff(C(20), KT, -1.0)
     aff(G16K, G16, 1.0, PK)
-    cyclic("ti", "x1", PP, 128.0)
     ts(A("ri", 0, RC), A("rm", 0, RC), 2, OP.arith_shift_right)
     ts(A("r4"), A("xb", 0, 16, 4), C(15), OP.is_equal)
     ts(A("zrl", 0, RC), A("ri", 0, RC), float(O0), OP.add)
@@ -308,72 +328,76 @@ def rank_program(g, core, T, topo):
     tt(A("w2"), A("w1"), A("p4", 0, PC), OP.add)
     for u in range(4):
         act(A("tm", 160 * u, 160 * u + 160), A("ti"), scale=R4(u))
+    eq("tq", "x2", G2, MR)
+    eq("blk", "x16", G1)
+    send_z(0, (act, act), Zc)
+    for out, step, ch, op in (("up", -1, 1, OP.is_gt), ("ul", 1, -1, OP.is_ge)):
+        add("g", lambda out=out, step=step, ch=ch, op=op: g.affine_select(win(out)[0], win("blk")[0], [[step, 128]], op, 0.0, 0, ch), [win(out)], [win("blk")])
     ts(A("w1"), A("pt"), 3, OP.bitwise_and)
-    tt(A("p5", 0, PC), A("si"), A("p5", 0, PC), OP.add)
     ts(A("nbl"), A("w2"), float(O0), OP.add, 0.0, OP.max)
+    tt(A("p5", 0, PC), A("si"), A("p5", 0, PC), OP.add)
     tt(A("xf", 3 * PC, 4 * PC), A("w1"), A("p4", 0, PC), OP.add)
     tt(A("xf", 0, PC), A("pt"), A("p5", 0, PC), OP.is_gt)
-    eq("tq", "x2", G2, C(16))
-    eq("blk", "x16", G1)
+    list_q()
+    act(A("qq", 0, 2 * RW, RW), A("r16", 0, 2), scale=0.0)
+    aff(C(44), R(2), float(FB - O0))
+    act(A("qq", O0, H0), A("qr", 0, V))
+    act(A("qq", RW + O0, RW + H0), A("qr", V, 2 * V))
+    send_q(0, act)
     ts(A("xf", 3 * PC, 4 * PC), A("xf", 3 * PC, 4 * PC), 0.0, OP.max)
     ts(A("xf", PC, 2 * PC), A("xf", 0, PC), -32.0, OP.mult)
-    ts(A("xf", 2 * PC, 3 * PC), A("xf", 0, PC), 128.0, OP.mult)
-    act(A("qq", 2 * O0, 2 * H0, 2), A("qr", 0, V))
-    act(A("qq", 2 * O0 + 1, 2 * H0, 2), A("qr", V, 2 * V))
-    act(A("qq", 0, 2 * O0), A("qr", 0, 2 * O0), scale=0.0)
+    ts(A("p5", 0, PC), A("xf", 0, PC), 128.0, OP.mult)
+    tt(A("xf", 2 * PC, 3 * PC), A("xf", 3 * PC, 4 * PC), A("p5", 0, PC), OP.add)
 
     def static_rows(j):
         for u in range(4):
-            for f, row in enumerate((0, 8, 12, 12)):
+            for f, row in enumerate((0, 8, 12)):
                 s = 160 * u + 16 - (row - 4 * u)
-                mm(A("p%d" % (2 + j), u, 2 * PC, 4), A("tm", s, s + 128), A("xf", f * PC + j * PC // 2, f * PC + (j + 1) * PC // 2), f == 0, f == 3)
+                mm(A("p%d" % (2 + j), u, 2 * PC, 4), A("tm", s, s + 128), A("xf", f * PC + j * PC // 2, f * PC + (j + 1) * PC // 2), f == 0, f == 2)
     static_rows(0)
-    ms(A("zw", 0, O0), -100.0)
+    static_rows(1)
+    gather_z(act, 0, 50)
     ts(C(19), KT, 1.0, OP.min)
     ts(C(21), MC, R(4), OP.add, -1.0, OP.mult)
-    send_z(0, (cp, cp), A("td"))
-    for out, step, ch, op in (("up", -1, 1, OP.is_gt), ("ul", 1, -1, OP.is_ge)):
-        add("g", lambda out=out, step=step, ch=ch, op=op: g.affine_select(win(out)[0], win("blk")[0], [[step, 128]], op, 0.0, 0, ch), [win(out)], [win("blk")])
     eq("e4", "x4", G4, C(20))
     eq("dz2", "x4", G41, R(4))
     ts(A("en"), A("ti"), C(21), OP.mult)
     eq("ea", "x1", G16, KT)
     eq("es", "x1", C(17), C(18))
-    list_q()
-    static_rows(1)
-    cp(A("zw", O0, ZC), A("td", O0, ZC))
-    act(A("st", 0, 2 * PC), A("p2", 0, 2 * PC))
-    send_q(0, act)
-    msum("dz", ("e4", "dz2", "en"), "p5")
-    msum("dg", ("ea", "es"), "p4")
     ts(A("tiz"), A("ti"), C(19), OP.mult)
     ts(C(22), R4(0), BIG, OP.mult)
     ts(C(23), R4(0), -1.0, OP.mult, 1.0, OP.add)
     ts(C(24), R4(1), -8.0, OP.mult, R(1), OP.add)
-    cp(A("st", 2 * PC, V), A("p3", 0, 2 * PC))
     for c0, c1, at in early + late:
-        ts(A("hz", at, at + c1 - c0), A("zw", H0 + c0, H0 + c1), MR, OP.mult)
+        ts(A("hz", at, at + c1 - c0), A("zw", O0 + c0, O0 + c1), MR, OP.mult, C(44), OP.add)
         i = at // 16 + (c0 == l0)
         cp(A("rzl", i, i + (c1 - c0) // 16), A("rm", c0 // 16, c1 // 16))
-    gather_z(act, 0, 70)
-    gather_z(act, 70, 136)
-    gather_z(cp, 136, 190)
-    gather_z(cp, 190, PC)
+    cp(A("st", 0, 2 * PC), A("p2", 0, 2 * PC))
+    gather_z(cp, 104, 170)
+    cp(A("st", 2 * PC, V), A("p3", 0, 2 * PC))
+    msum("dz", ("e4", "dz2", "en"), "p5")
+    msum("dg", ("ea", "es"), "p4")
+    gather_z(act, 50, 104)
+    gather_z(cp, 170, PC)
 
     def lane_constants(part):
         if part == 0:
             act(A("lr", 0, CAP), A("zw", H0, H0 + CAP), AF.Identity, MR, C(24))
+            act(A("ti32"), A("ti"))
+            for f in range(2):
+                act(A("qq", RW * f + H0, RW * f + ZC), A("qr", 0, CAP), scale=0.0)
+            for i in range(6):
+                act(A("sel", 128 * i, 128 * i + 128), win("blk"), scale=R(i))
             eq("tx", "x1", G16, C(22))
             ts(A("kk"), A("si", 0, EC), float(V), OP.add)
             ms(A("can", 0, 2), 0.0)
             ms(A("sm", 0, 2), 0.0)
-            ts(C(25), R4(2), 2.0, OP.mult)
             eq("tn", "x1", G16K, R4(1))
-            ts(C(26), R4(3), 0.5, OP.mult, C(25), OP.add)
+            ts(C(26), R4(3), 0.25, OP.mult, R4(2), OP.add)
             eq("e4", "x4", G4, DT)
             eq("tlo", "x1", G16K, R4(3))
             eq("tih", "x1", G16K, C(26))
-            ms(A("kc", 0, LC), -0.75)
+            ms(A("kc", 0, LC), -0.375)
         elif part == 1:
             ts(C(27), R(0), 6.0, OP.mult)
             tt(C(28), R(0), R(1), OP.add)
@@ -384,47 +408,64 @@ def rank_program(g, core, T, topo):
             ts(C(27), R(2), float(AB - H0), OP.mult, C(27), OP.add)
             tt(C(29), C(29), R(1), OP.add)
             tt(C(30), C(30), DT, OP.subtract)
+            for i in range(6, 12):
+                ts(A("sel", 128 * i, 128 * i + 128), win("blk"), R(i), OP.mult)
         elif part == 2:
-            msum("ta", ("tn", "e4"), "p6")
-            act(A("ti32"), A("ti"))
-            for i in range(16):
+            msum("ta", ("tn", "e4"), "p0")
+            for i in range(12, 16):
                 act(A("sel", 128 * i, 128 * i + 128), win("blk"), scale=R(i))
+        elif part == 10:
+            lane_constants(4)
         elif part == 3:
             eq("tco", "x1", G16, MC)
             eq("ncb", "x2", G2, -1.0)
+            ts(A("ri", 0, RC), A("rm", 0, RC), 3, OP.bitwise_and)
+            ts(C(33), R(2), float(AS), OP.mult)
+            ts(A("kr", 0, RC), A("ri", 0, RC), 0.25, OP.mult)
         elif part == 4:
             act(A("kz"), A("zw", H0, H0 + CAP), AF.Identity, MR, C(27))
             act(A("ed"), A("ti"), scale=MC)
             act(A("dts"), A("blk"), scale=DT)
             act(C(31), A("tht", 0, 1), scale=-1.0)
+            act(A("mm", 0, 8), A("r16", 0, 8), scale=0.0)
         elif part == 5:
             ts(C(32), MR, 4.0, OP.mult)
-            ts(C(33), R(2), float(AS), OP.mult)
-            ts(A("ri", 0, RC), A("rm", 0, RC), 3, OP.bitwise_and)
             ms(A("kc", LC, 2 * LC), 0.0)
-            ms(A("mm", 0, 8), 0.0)
             eq("tow", "x4", G4, C(32))
-            ts(A("kr", 0, RC), A("ri", 0, RC), 0.25, OP.mult)
             ts(A("kc", 2 * LC, 3 * LC), A("kc", LC, 2 * LC), PK, OP.add)
+            ts(A("w1"), A("pt"), 4064, OP.bitwise_and)
+        elif part == 9:
+            ts(A("w1"), A("pt"), 31, OP.bitwise_and)
+            tt(C(43), R4(0), R4(1), OP.add)
+            cp(A("xf", PC, 2 * PC), A("w1"))
+            eq("tpw", "x1", G16K, C(43))
+            ms(A("pw", H0, H0 + CAP), -100.0)
         elif part == 6:
-            act(A("tid"), A("tih"), scale=2.0)
+            act(A("tid"), A("tih"), scale=4.0)
             act(A("nti"), A("ti"), scale=-1.0)
+            act(A("tnb"), A("tn"), scale=-BIGM)
+            act(A("col", 34, 38), A("r4"), scale=-1.0)
+            act(A("col", 38, 42), A("r4"), scale=CAP - 0.5)
+            act(A("en"), A("en"), scale=-1.0)
+        elif part == 11:
+            msum("tf", ("tid", "tnb"), "p6")
+            msum("dzl", ("dz", "en"), "p7")
         elif part == 7:
-            cyclic("nb4", "x16", G1, 8.0)
             eq("tt4", "x1", G16, R(4))
             eq("tdt", "x1", G16, DT)
             ts(A("rnl", 0, RC), A("rm", 0, RC), float(L), OP.add)
             tt(C(42), G4, PK, OP.add)
-            ms(A("mm", MZ, MZ + 8), 0.0)
-            eq("tac", "x4", C(42), -BIGM)
+            ms(A("ff", 0, 8), 0.0)
+            eq("tac", "x4", C(42), -4 * BIGM)
+            ts(A("xf", 0, PC), A("w1"), float(L), OP.add)
         else:
-            act(A("tb4"), A("nb4"), scale=R(4))
-            act(A("tb2"), A("blk"), scale=R(2))
-            act(A("nb4"), A("tb4"), scale=-1.0)
-            act(A("tnb"), A("tn"), scale=-BIGM)
-            act(A("col", 34, 38), A("r4"), scale=-1.0)
-            act(A("col", 38, 42), A("r4"), scale=CAP - 0.5)
-            msum("tf", ("tid", "tnb"), "p6")
+            for j in range(2):
+                for u in range(4):
+                    for f in range(2):
+                        s = 160 * u + 16 - 4 * (f - u)
+                        mm(A("p%d" % (6 + j), u, 2 * PC, 4), A("tm", s, s + 128), A("xf", f * PC + j * PC // 2, f * PC + (j + 1) * PC // 2), f == 0, f == 1)
+                act(A("pw", O0 + 2 * PC * j, O0 + 2 * PC * (j + 1)), A("p%d" % (6 + j), 0, 2 * PC))
+
 
     def W(i, n=1):
         return A("cw", LC * i, LC * (i + n))
@@ -432,25 +473,27 @@ def rank_program(g, core, T, topo):
     def CO(i):
         return A("co", LC * i, LC * (i + 1))
 
-    def spread(i, bank):
-        for k in range(4):
+    def K(i, k, u=0, st=1):
+        bank, at = ((4 + k, 0), (4 + k, 0), (4 + k, CAP), (k // 2, CAP * (k % 2)), (2 + k // 2, CAP * (k % 2)))[i]
+        return A("p%d" % bank, at + u, at + CAP, st)
+
+    def spread(i, ports=range(4)):
+        for k in ports:
             for u in range(4):
                 s = 128 * (4 * u + k)
-                mm(A("p%d" % (bank + k // 2), CAP * (k % 2) + u, CAP * (k % 2 + 1), 4), A("sel", s, s + 128), CO(i))
+                mm(K(i, k, u, 4), A("sel", s, s + 128), CO(i))
 
-    def K(bank, k):
-        return A("p%d" % (bank + k // 2), CAP * (k % 2), CAP * (k % 2 + 1))
-
-    def lanes(t, bank, at, start=True, stop=True):
+    def lanes(t, bank, at, start=True, stop=True, rows="lr"):
         for u in range(4):
-            mm(A(bank, at, at + LC), win(t, 4 * u), A("lr", u, CAP, 4), start and u == 0, stop and u == 3)
+            mm(A(bank, at, at + LC), win(t, 4 * u), A(rows, u, CAP, 4), start and u == 0, stop and u == 3)
 
-    def put_m(rnd):
-        to = A("mm", 4 * (AB + AS * rnd) - MOFF, 4 * (AB + AS * rnd) - MOFF + L)
+    def put_m(rnd, c0=0, c1=LC):
+        at = 4 * (AB + AS * rnd) - MOFF
+        to, f = A("mm", at + 16 * c0, at + 16 * c1) if rnd < RO - 1 else A("un"), A("ff", 8 + 16 * c0, 8 + 16 * c1)
         if rnd:
-            tt(to, IND(Mw(rnd), A("il", LC, 2 * LC)), A("ff"), OP.subtract)
+            tt(to, IND(Mw(rnd), A("il", LC + c0, LC + c1)), f, OP.subtract)
         else:
-            ts(to, A("ff"), -1.0, OP.mult)
+            ts(to, f, -1.0, OP.mult)
 
     HC = CAP // 2
     hs = [(2 * CAP * h, 2 * CAP * (h + 1)) for h in range(2)]
@@ -458,7 +501,7 @@ def rank_program(g, core, T, topo):
         last = rnd == RO - 1
         zl, bl, ml = ("%s%d" % (x, rnd % 2) for x in ("zl", "bl", "ml"))
         rec = AB + AS * rnd
-        rows_own("dz")
+        rows_own("dzl" if last else "dz")
         ins = []
         for bank, pieces in (("p4", early), ("p5", late)):
             a0, a1 = pieces[0][2], pieces[-1][2] + pieces[-1][1] - pieces[-1][0]
@@ -476,180 +519,280 @@ def rank_program(g, core, T, topo):
             act(A("kz"), A("kz"), AF.Identity, 1.0, C(33))
             put_m(rnd - 1)
             list_m()
-        for bank, e0, e1 in parts:
-            rows_near(bank, e0, e1)
-            ts(A("fail", e0, e1), A(bank, 0, e1 - e0), 0.5, OP.is_lt)
-            act(A("psb", e0, e1), A(bank, 0, e1 - e0), AF.Copy, C(23))
-        for i in range(16):
-            mm(A("p6", 0, EC), win("tx", i), A("fail", i, V, 16), i == 0, i == 15)
-        if rnd < 2:
-            lane_constants(1 + 6 * rnd)
-        ts(A("can", 1, 1 + EC), A("p6", 0, EC), 0.5, OP.is_lt)
-        mm(A("p7", 0, EC), win("ul"), A("can", 1, 1 + EC), True, False)
-        mm(A("p7", 0, EC), win("up"), A("can", 0, EC), False, True)
-        tt(A("sm", 1, 1 + EC), A("p6", 0, EC), A("kk"), OP.min)
-        tt(A("sm", 64, 64 + EC), A("sm", 1, 1 + EC), A("sm", 0, EC), OP.subtract)
-        add("v", lambda: g.vector.tensor_tensor_scan(T.sm[:, 128:128 + EC], T.sm[:, 64:64 + EC], T.p7[:, 0:EC], -1.0, OP.add, OP.add),
-            [A("sm", 128, 128 + EC)], [A("sm", 64, 64 + EC), A("p7", 0, EC)])
-        cp(A("ol"), A("sm", 128, 128 + EC))
-        tt(IND(A("lr"), A("ol")), A("psb"), A("zw", *own), OP.add)
-        if rnd < 3:
-            lane_constants((2, 6, 8)[rnd])
-        if rnd:
-            send_m(rnd, act)
         if last:
-            for j in range(2):
-                e0, e1 = V // 2 * j, V // 2 * (j + 1)
-                mm(A("p%d" % j, 0, V // 2), ident, A("psb", e0, e1), True, False)
-                mm(A("p%d" % j, 0, V // 2), ident, A("zw", O0 + e0, O0 + e1), False, True)
-                act(A("fail", e0, e1), A("p%d" % j, 0, V // 2), AF.Relu, 1.0, R4(1))
+            act(A("zq", *own), A("zw", *own), scale=R4(0))
+
+        def failing(n):
+            bank, e0, e1 = parts[n]
+            act(A("fail", e0, e1), A(bank, 0, e1 - e0), AF.Relu, -1.0, 1.0)
+
+        def rows_out(n):
+            bank, e0, e1 = parts[n]
+            act(A("psb", e0, e1), A(bank, 0, e1 - e0), AF.Copy, C(23))
+
+        def rows_ym(n):
+            bank, e0, e1 = parts[n]
+            act(A("pz", e0, e1), A(bank, 0, e1 - e0), AF.Relu, 1.0, R4(1))
+
+        def count(bank, c0, c1):
+            for i in range(16):
+                mm(A(bank, c0, c1), win("tx", i), A("fail", 16 * c0 + i, 16 * c1, 16), i == 0, i == 15)
+
+        def ranks(bank, c0, c1):
+            mm(A(bank, c0, c1), win("ul"), A("can", 1 + c0, 1 + c1), True, False)
+            mm(A(bank, c0, c1), win("up"), A("can", c0, c1), False, True)
+
+        def to_front(cnt, bank, c0, c1):
+            tt(A("sm", 1 + c0, 1 + c1), A(cnt, c0, c1), A("kk", c0, c1), OP.min)
+            tt(A("sm", 64 + c0, 64 + c1), A("sm", 1 + c0, 1 + c1), A("sm", c0, c1), OP.subtract)
+            out, d0, d1, ini = A("sm", 128 + c0, 128 + c1), A("sm", 64 + c0, 64 + c1), A(bank, c0, c1), A("sm", 127 + c0, 128 + c0) if c0 else -1.0
+            add("v", lambda: g.vector.tensor_tensor_scan(out[0], d0[0], d1[0], P(ini), OP.add, OP.add), [out], [d0, d1, ini])
+            cp(A("ol", c0, c1), out)
+            tt(IND(A("lr"), A("ol", c0, c1)), A("psb", 16 * c0, 16 * c1), A("zq" if last else "zw", O0 + 16 * c0, O0 + 16 * c1), OP.add)
+        mid = parts[2][1] // 16
+        if not OPT["halves"]:
+            for n in range(4):
+                rows_near(*parts[n])
+                if OPT["afail"] and n != 2:
+                    failing(n)
+                else:
+                    ts(A("fail", *parts[n][1:]), A(parts[n][0], 0, parts[n][2] - parts[n][1]), 0.5, OP.is_lt)
+                if n == 0 or not OPT["afail"]:
+                    rows_out(n)
+            for n in range(1, 4):
+                if OPT["afail"]:
+                    rows_out(n)
+            count("p6", 0, EC)
+            if not last:
+                lane_constants((1, 5, 7, 9)[rnd])
+            ts(A("can", 1, 1 + EC), A("p6", 0, EC), 0.5, OP.is_lt)
+            ranks("p7", 0, EC)
+            to_front("p6", "p7", 0, EC)
+            if last:
+                for n in (2, 3, 0, 1):
+                    rows_ym(n)
+        else:
+            for n in range(2):
+                rows_near(*parts[n])
+                failing(n)
+            rows_near(*parts[2], ports=(0,))
+            rows_out(0)
+            rows_out(1)
+            if rnd and OPT["ms"] == "early":
+                send_m(rnd, act, OPT["mc"])
+            count("p6", 0, mid)
+            rows_near(*parts[2], ports=(1,))
+            if not last:
+                lane_constants((1, 5, 7, 9)[rnd])
+            ts(A("can", 1, 1 + mid), A("p6", 0, mid), 0.5, OP.is_lt)
+            ranks("p7", 0, mid)
+            rows_near(*parts[2], ports=(2, 3))
+            failing(2)
+            rows_near(*parts[3])
+            failing(3)
+            to_front("p6", "p7", 0, mid)
+            count("p5", mid, EC)
+            rows_out(2)
+            if last:
+                rows_ym(0)
+            act(A("can", 1 + mid, 1 + EC), A("p5", mid, EC), AF.Relu, -1.0, 1.0)
+            ranks("p4", mid, EC)
+            rows_out(3)
+            if last:
+                for n in (2, 3, 1):
+                    rows_ym(n)
+            to_front("p5", "p4", mid, EC)
+        if rnd < 2:
+            lane_constants((2, 6)[rnd])
+        if last:
             for u in range(4):
                 act(A("xf", 64 * u, 64 * u + EC), A("sm", 128, 128 + EC), AF.Relu, C(34 + u), C(38 + u))
-        for bank, (c0, c1, at) in zip(("p4", "p5", "p6"), early + late):
-            for x0, x1, s in sides(c0, c1):
-                mm(A(bank, 2 * (x0 - c0), 2 * (x1 - c0)), win("ti32", s), A(bl, 2 * x0, 2 * x1))
-            act(A("qq", 2 * (H0 + c0), 2 * (H0 + c1)), A(bank, 0, 2 * (c1 - c0)))
         mm(A("p2", 0, LC), ident, A("kc", 0, LC), True, False)
         if rnd:
             mm(A("p3", 0, 2 * LC), ident, A("kc", LC, 3 * LC), True, False)
-        else:
+        if rnd == 0:
+            lane_constants(10)
             lane_constants(3)
-        for i in range(8):
-            mm(A("p1", 0, 2 * AC), win("tq", 2 * i), A("lr", i, CAP, 8), i == 0, i == 7)
-        lanes("tn", "p0", 0)
-        lanes("ta", "p0", LC)
-        lanes("tlo", "p7", 0)
-        lanes("tih", "p2", 0, False)
+        if OPT["q"] == "dma":
+            shift("yq", bl, 2, "hq")
+            for f in range(2):
+                act(A("qq", RW * f + FB, RW * f + FB + H), A("yq", f, 2 * H, 2))
+        else:
+            if rnd and OPT["ms"] == "mid":
+                send_m(rnd, act, OPT["mc"])
+            if OPT["q"] == "mix":
+                shift("yq", bl, 2, "hq", l0, l1)
+            if OPT["q"] == "xim":
+                shift("yq", bl, 2, "hq", 0, l0, l1, H)
+                for c0, c1, at in early:
+                    for f in range(2):
+                        act(A("qq", RW * f + FB + c0, RW * f + FB + c1), A("yq", 2 * c0 + f, 2 * c1, 2))
+            for bank, (c0, c1, at) in zip(("p7", "p6", "p5"), {"pe": early + late, "mix": early, "xim": late}[OPT["q"]]):
+                for x0, x1, s in sides(c0, c1):
+                    mm(A(bank, 2 * (x0 - c0), 2 * (x1 - c0)), win("ti32", s), A(bl, 2 * x0, 2 * x1))
+                for f in range(2):
+                    act(A("qq", RW * f + FB + c0, RW * f + FB + c1), A(bank, f, 2 * (c1 - c0), 2))
+        if rnd and OPT["ms"] == "late":
+            send_m(rnd, act, OPT["mc"])
+        if rnd and OPT["m"] == "dma":
+            shift("mh", ml, 1, "hm")
         nn, aa = A("p0", 0, LC), A("p0", LC, 2 * LC)
-        ts(A("ql", 0, 2 * AC), A("p1", 0, 2 * AC), ODD, OP.add)
-        act(A("qe"), IND(Qw(rnd), A("ql", 0, 2 * AC)))
-        ts(W(0, 2), A("p0", 0, 2 * LC), 0.0, OP.max, -0.5, OP.mult)
-        ts(CO(0), A("p7", 0, LC), 127.5, OP.is_lt, 0.5, OP.subtract)
-        tt(W(2), W(1), W(0), OP.subtract)
-        ts(A("nl", 0, LC), A("p2", 0, LC), M2, OP.add, M2, OP.subtract)
-        tt(CO(1), W(2), CO(0), OP.mult)
-        tt(W(3), W(2), aa, OP.add)
-        spread(1, 4)
-        tt(W(4), W(3), nn, OP.subtract)
-        tt(CO(3), W(3), CO(1), OP.mult)
+        for x in OPT["pe"]:
+            if x == "q":
+                for i in range(8):
+                    mm(A("p1", 0, 2 * AC), win("tq", 2 * i), A("lr", i, CAP, 8), i == 0, i == 7)
+            elif x == "a":
+                lanes("tn", "p0", 0)
+                lanes("ta", "p0", LC)
+            elif x == "s":
+                lanes("tlo", "p7", 0)
+            else:
+                lanes("tih", "p2", 0, False)
+        for x in OPT["v"]:
+            if x == "q":
+                ts(A("ql", 0, 2 * AC), A("p1", 0, 2 * AC), C(16), OP.add)
+                act(A("qe"), IND(Qw(rnd), A("ql", 0, 2 * AC)))
+            elif x == "r":
+                cp(A("rl", 0, 2 * AC), A("p1", 0, 2 * AC))
+            elif x == "n":
+                ts(A("nl"), A("p2", 0, LC), M1, OP.add, M1, OP.subtract)
+                for f in range(2):
+                    act(A("qn", L * f, L * f + L), IND(A("qq", RW * f, RW * f + FB + H), A("nl")))
+            elif x == "0":
+                ts(W(0, 2), A("p0", 0, 2 * LC), 0.0, OP.max, -0.5, OP.mult)
+            elif x == "2":
+                tt(W(2), W(1), W(0), OP.subtract)
+            elif x == "s":
+                ts(CO(0), A("p7", 0, LC), 127.5, OP.is_lt, 0.5, OP.subtract)
+            elif x == "3":
+                tt(W(3), W(2), aa, OP.add)
+            elif x == "c":
+                tt(CO(1), W(2), CO(0), OP.mult)
+                spread(1)
+            elif x == "4":
+                tt(W(4), W(3), nn, OP.subtract)
         tt(CO(2), W(4), CO(1), OP.mult)
-        spread(2, 6)
-        ts(A("nl", LC, 2 * LC), A("nl", 0, LC), 1.0, OP.add)
-        act(A("qn", 0, L), IND(Qw(rnd), A("nl", 0, LC)))
+        tt(CO(3), W(3), CO(1), OP.mult)
+        q0e, q1e = A("qe", 0, 2 * CAP, 2), A("qe", 1, 2 * CAP, 2)
+        for k in range(4):
+            tt(A("ue", CAP * k, CAP * k + CAP), q0e, K(1, k), OP.mult)
+            spread(2, (k,))
+            if k == 1 and rnd:
+                ts(A("fg", 0, LC), nn, -0.5, OP.is_gt, BIGM, OP.mult)
+                ts(A("fg", LC, 2 * LC), nn, 0.5, OP.is_lt, BIGM, OP.mult)
+        spread(3)
         if rnd:
-            lanes("tn", "p1", 64)
             lanes("tid", "p3", 0, False, False)
             lanes("tow", "p3", LC, False, False)
-        for i in range(16):
-            mm(A("p2", 128, 128 + AC), win("tr", i), A("lr", i, CAP, 16), i == 0, i == 15)
-        if rnd:
-            act(A("fg", 0, LC), A("p1", 64, 64 + LC), AF.Relu, BIGM, BIGM)
-            act(A("fg", LC, 2 * LC), A("p1", 64, 64 + LC), AF.Relu, -BIGM, BIGM)
-        act(A("qn", L, 2 * L), IND(Qw(rnd), A("nl", LC, 2 * LC)))
-        if rnd:
             mm(A("p3", 0, 2 * LC), win("nti"), A("fg"), False, True)
-        spread(3, 0)
-        q0e, q1e = A("qe", 0, 2 * CAP, 2), A("qe", 1, 2 * CAP, 2)
+        if last:
+            for u in range(4):
+                mm(A("p2", 160, 160 + PC), win("tf", 4 * u), A("pz", u, V, 4), u == 0, False)
+            for u in range(4):
+                mm(A("p2", 160 + u, 160 + PC, 4), win("tac"), A("xf", 64 * u, 64 * u + EC), False, u == 3)
 
-        def side(u, x0, x1, bank, scale, sq, between):
+        def side(u, x0, x1, f, scale, sq, between):
             def X(k):
                 return A(u, CAP * k, CAP * k + CAP)
             for h in range(2):
+                for k in ((2 * h, 2 * h + 1) if x0 else ()):
+                    tt(X(k), x0(k), K(1, k), OP.mult)
                 for k in (2 * h, 2 * h + 1):
-                    tt(X(k), x0(k), K(4, k), OP.mult)
-                for k in (2 * h, 2 * h + 1):
-                    tt(K(bank, k), x1(k), K(bank, k), OP.mult)
+                    tt(K(f, k), x1(k), K(f, k), OP.mult)
                 between(h)
                 for k in (2 * h, 2 * h + 1):
-                    tt(X(k), X(k), K(bank, k), OP.add)
+                    tt(X(k), X(k), K(f, k), OP.add)
                 act(A(u, *hs[h]), A(u, *hs[h]), AF.Relu, scale)
-                act(sq(h), A(u, *hs[h]), AF.Square)
+                if x0 or not OPT["e"]:
+                    act(sq(h), A(u, *hs[h]), AF.Square)
+            if not x0 and OPT["e"]:
+                for h in range(2):
+                    act(sq(h), A(u, *hs[h]), AF.Square)
 
-        def lists(h):
-            if h == 1:
-                cp(A("rl", 0, AC), A("p2", 128, 128 + AC))
+        def memories(h):
+            if h == 0:
+                if soon:
+                    act(A("ze"), IND(Zw(rnd), A("rl", 0, 2 * AC)))
                 if rnd:
                     ts(A("il"), A("p3", 0, 2 * LC), -float(MOFF), OP.add, 0.0, OP.max)
                 if last:
-                    ts(W(0), A("p2", 0, LC), M2, OP.add, M2, OP.subtract)
-                    ts(A("nl", 2 * LC, 3 * LC), A("nl", 0, LC), 0.5, OP.mult)
-                    tt(W(0), A("p2", 0, LC), W(0), OP.subtract)
-                    act(W(1), W(0), scale=0.5)
-                spread(0, 2)
-        side("ue", lambda k: q0e, lambda k: q1e, 6, 0.125, lambda h: A("ue", *hs[h]), lists)
-        act(A("ze"), IND(Zw(rnd), A("rl", 0, AC)))
-        if rnd == 0:
-            lane_constants(4)
-        side("un", lambda k: A("qn", k, L, 4), lambda k: A("qn", L + k, 2 * L, 4), 0, -0.125, lambda h: A("p%d" % (6 + h), 0, 2 * CAP), lambda h: None)
-        for i in range(16):
-            mm(A("p0", 0, AC), win("tco", i), A("ze", i, CAP, 16), i == 0, i == 15)
+                    ts(A("fl"), A("p2", 160, 160 + PC), -float(MOFF), OP.add, 0.0, OP.max)
+            spread(0, (2 * h, 2 * h + 1))
+        soon = last or (rnd == 0 and OPT["soon0"])
+        side("ue", None, lambda k: q1e, 2, 0.125, lambda h: A("ue", *hs[h]), lambda h: None)
+        side("un", lambda k: A("qn", k, L, 4), lambda k: A("qn", L + k, 2 * L, 4), 3, -0.125, lambda h: A("p%d" % (2 + h), 0, 2 * CAP), memories)
         zu = A("zw", rec, rec + CAP)
-
-        def rows_new(bank, j0, j1, stop):
-            mm(A(bank, 0, j1 - j0), ident, A("kz", j0, j1), True, False)
-            mm(A(bank, 0, j1 - j0), win("ea", 4), A("ze", j0, j1), False, False)
-            mm(A(bank, 0, j1 - j0), win("ed"), A("ze", j0, j1), False, stop)
-        if last:
-            rows_new("p5", 0, CAP, True)
-            act(zu, A("p5", 0, CAP))
-        if rnd:
-            for x0, x1, s in sides(0, H):
-                mm(A("p4", 128 + x0, 128 + x1), win("ti32", s), A(ml, x0, x1))
-            act(A("mm", 8, 8 + 4 * H, 4), A("p4", 128, 128 + H))
-        mm(A("p1", 0, CAP), win("dts"), A("ze"))
         q0p = A("p1", CAP, 2 * CAP)
-        act(q0p, q0e)
-        act(A("rdt", 0, CAP), A("p1", 0, CAP), AF.Relu, -0.5, 1.25)
-        for h in range(2):
-            rows_new("p%d" % (4 + h), HC * h, HC * h + HC, False)
-        for h in range(2):
-            for k in (2 * h, 2 * h + 1):
-                tt(A("ss", CAP * k, CAP * k + CAP), A("ue", CAP * k, CAP * k + CAP), K(6, k), OP.add)
-            if h == 0:
-                cp(A("al", 0, AC), A("p0", 0, AC))
-                if last:
-                    for u in range(4):
-                        mm(A("p0", 128, 128 + PC), win("tf", 4 * u), A("fail", u, V, 4), u == 0, False)
-                    for u in range(4):
-                        mm(A("p0", 128 + u, 128 + PC, 4), win("tac"), A("xf", 64 * u, 64 * u + EC), False, u == 3)
-            for k in (2 * h, 2 * h + 1):
-                tt(A("ff", k, L, 4), A("ss", CAP * k, CAP * k + CAP), K(2, k), OP.mult)
-            if h == 0 and last:
-                cp(IND(Zc, A("al", 0, AC)), zu)
-                act(A("zs"), IND(Zc, A("zrl", 0, RC)))
-            if h == 1 and last:
-                ts(A("fl"), A("p0", 128, 128 + PC), -float(MOFF + MZ), OP.add, 0.0, OP.max)
-        act(A("rdt", CAP, 2 * CAP), A("rdt", 0, CAP), AF.Identity, 1.0, 0.25)
-        if last:
-            mm(A("p6", 0, H), win("nb4"), A("zs"), True, False)
-            todo = sides(0, H)
-            for n, (x0, x1, s) in enumerate(todo):
-                mm(A("p6", x0, x1), win("tb4", s), A(zl, x0, x1), False, n == len(todo) - 1)
-            rim_records()
-            put_m(rnd)
-            list_m()
-            ts(A("mk"), A("p6", 0, H), -0.5, OP.is_lt)
-            send_m(RO, lambda out, x: tt(out, x, A("mk"), OP.mult), 2)
-            act(A("zn"), IND(Zw(rnd), A("nl", 2 * LC, 3 * LC)))
-            for c0, c1 in ((0, 80), (80, 160), (160, PC)):
-                act(A("mg", L + 16 * c0, L + 16 * c1), IND(A("mm", MZ, 4 * rec - MOFF), A("fl", c0, c1)))
+
+        def rows_new(bank, at, j0, j1, stop):
+            mm(A(bank, at, at + j1 - j0), ident, A("kz", j0, j1), True, False)
+            mm(A(bank, at, at + j1 - j0), win("ea", 4), A("ze", 2 * j0, 2 * j1, 2), False, False)
+            mm(A(bank, at, at + j1 - j0), win("ed"), A("ze", 2 * j0, 2 * j1, 2), False, stop)
+
+        cols = A("p0", 0, AC)
+
+        def columns():
             for i in range(16):
-                mm(A("p0", 0, LC), win("tco", i), A("zn", i, L, 16), i == 0, i == 15)
+                mm(cols, win("tco", i), A("ze", 2 * i, 2 * CAP, 32), i == 0, i == 15)
+        if rnd and OPT["m"] == "dma":
+            act(A("mm", 4 * FB - MOFF, 4 * (FB + H) - MOFF, 4), A("mh"))
+        elif rnd:
+            for x0, x1, s in sides(0, H):
+                mm(A("p1" if last else "p0", 128 + x0, 128 + x1), win("ti32", s), A(ml, x0, x1))
+            act(A("mm", 4 * FB - MOFF, 4 * (FB + H) - MOFF, 4), A("p1" if last else "p0", 128, 128 + H))
+        if last:
+            columns()
+            rows_new("p0", 256, 0, CAP, True)
+            act(zu, A("p0", 256, 256 + CAP))
+        if not soon:
+            act(A("ze"), IND(Zw(rnd), A("rl", 0, 2 * AC)))
+        act(q0p, q0e)
+        if last:
+            act(A("mg", L, L + 16 * 40), IND(Mw(), A("fl", 0, 40)))
+        for h in range(2):
+            for k in (2 * h, 2 * h + 1):
+                tt(A("ss", CAP * k, CAP * k + CAP), A("ue", CAP * k, CAP * k + CAP), K(4, k), OP.add)
+            for k in (2 * h, 2 * h + 1):
+                tt(A("ff", 8 + k, 8 + L, 4), A("ss", CAP * k, CAP * k + CAP), K(0, k), OP.mult)
+        if last:
+            cp(A("al", 0, AC), cols)
+            cp(IND(Zc, A("al", 0, AC)), zu)
+            act(A("zs"), IND(Zc, A("zrl", 0, RC)))
+            rim_records("p3")
+            act(A("pe"), IND(A("pw"), A("al", 0, AC)))
+            act(A("mg", L + 16 * 40, L + 16 * 100), IND(Mw(), A("fl", 40, 100)))
+        for h in range(2):
+            rows_new("p%d" % (4 + h), 0, HC * h, HC * h + HC, False)
+        if not last:
+            columns()
+        mm(A("p2", 0, CAP), win("dts"), A("ze", 0, 2 * CAP, 2))
+        act(A("rdt", 0, CAP), A("p2", 0, CAP), AF.Relu, -0.5, 1.25)
+        act(A("rdt", CAP, 2 * CAP), A("rdt", 0, CAP), AF.Identity, 1.0, 0.25)
+        if rnd in (2, 3):
+            lane_constants(11 if rnd == 2 else 8)
+        if last:
+            put_m(rnd)
+            list_m(8 - 4 * rec, "p3")
+            ts(A("ms"), IND(A("ff"), A("mrl", 0, RC)), -1.0, OP.mult)
+            exchange("ms", "ml%d" % (RO % 2), B, "ma%d" % RO, "msent", 2)
+            for c0, c1 in ((100, 170), (170, PC)):
+                act(A("mg", L + 16 * c0, L + 16 * c1), IND(Mw(), A("fl", c0, c1)))
+            lanes("tpw", "p6", 0, rows="pe")
             for i in range(16):
                 mm(A("p7", 0, EC), win("tr", i), A("zw", O0 + i, H0, 16), i == 0, i == 15)
-            mm(A("p6", 0, H), win("tb2"), A("zs"))
-        src = "ff"
+        src = "mf" if rnd else "ff"
         if rnd:
-            for h in range(2):
-                tt(A("mf", *hs[h]), IND(Mw(rnd), A("il", LC // 2 * h, LC // 2 * (h + 1))), A("ff", *hs[h]), OP.add)
-            src = "mf"
+            for h, (c0, c1) in enumerate(hs):
+                tt(A("mf", 8 + c0, 8 + c1), IND(Mw(), A("il", LC // 2 * h, LC // 2 * (h + 1))), A("ff", 8 + c0, 8 + c1), OP.add)
 
         def q0n(j0, j1):
-            return A("qq", 2 * (rec + j0), 2 * (rec + j1), 2)
+            return A("qq", rec + j0, rec + j1)
         for k in range(4):
             for h in range(2):
                 j0, j1 = HC * h, HC * (h + 1)
-                tt(q0n(j0, j1) if k == 3 else A("p1", j0, j1), A("p1", j0 + (0 if k else CAP), j1 + (0 if k else CAP)), A(src, 4 * j0 + k, 4 * j1, 4), OP.add)
+                tt(q0n(j0, j1) if k == 3 else A("p1", j0, j1), A("p1", j0 + (0 if k else CAP), j1 + (0 if k else CAP)), A(src, 8 + 4 * j0 + k, 8 + 4 * j1, 4), OP.add)
+        if not last:
+            cp(A("al", 0, AC), cols)
         for h in range(2):
             j0, j1 = HC * h, HC * (h + 1)
             ts(A("cb", j0, j1), q0n(j0, j1), A("tht", 0, 1), OP.is_gt)
@@ -664,7 +807,7 @@ def rank_program(g, core, T, topo):
 
         def put_q():
             tt(A("p1", 0, CAP), q0n(0, CAP), q0p, OP.subtract)
-            tt(A("qq", 2 * rec + 1, 2 * (rec + CAP), 2), A("rdt", CAP, 2 * CAP), A("p1", 0, CAP), OP.mult)
+            tt(A("qq", RW + rec, RW + rec + CAP), A("rdt", CAP, 2 * CAP), A("p1", 0, CAP), OP.mult)
 
         if not last:
             put_z()
@@ -677,38 +820,35 @@ def rank_program(g, core, T, topo):
             gather_z(act, 110, 146)
             gather_z(cp, 146, 190)
             gather_z(cp, 190, PC)
-            if rnd == 0:
-                lane_constants(5)
             rim_records()
 
     ml = "ml%d" % (RO % 2)
-    tt(W(0), W(1), A("p0", 0, LC), OP.add)
-    ts(A("yl", 0, EC), A("p7", 0, EC), 2.0, OP.mult)
-    ts(W(0), W(0), 4.0, OP.mult, L + 1.5 - 4 * O0, OP.add)
-    ts(A("yl", EC, 2 * EC), A("p7", 0, EC), 2.0, OP.mult, 1.0, OP.add)
-    tt(W(0), W(0), A("si", 0, LC), OP.max)
-    put_q()
+    tt(W(0), A("si", 0, LC), A("p6", 0, LC), OP.max)
+    cp(A("yl"), A("p7", 0, EC))
     cp(A("il", 0, LC), W(0))
+    put_q()
+    act(A("mo"), IND(A("mg"), A("rnl", 0, RC)))
     put_z()
-    cp(IND(A("mg"), A("il", 0, LC)), A("mm", 4 * rec - MOFF, 4 * rec - MOFF + L))
-    ts(A("mk"), A("p6", 0, H), AB + AS * (RO - 1) - 0.5, OP.is_lt)
+    cp(IND(A("mg"), A("il", 0, LC)), A("un"))
     for x0, x1, s in sides(0, H):
         mm(A("p2", x0, x1), win("ti32", s), A(ml, x0, x1))
     for j, t in enumerate(("tt4", "tdt")):
         for i in range(16):
             mm(A("p7", 64 * (j + 1), 64 * (j + 1) + EC), win(t, i), A("zw", O0 + EC * i, O0 + EC * (i + 1)), i == 0, i == 15)
     for j in range(2):
-        act(A("yq", V * j, V * j + V), IND(Qw(RO), A("yl", EC * j, EC * j + EC)))
+        act(A("yq", V * j, V * j + V), IND(Qw(RO, j), A("yl")))
         dma("s", (T.y0, T.y1)[j][:], A("yq", V * j, V * j + V))
-    for j in range(2):
-        act(A("ytb", 64 * j, 64 * j + EC), A("p7", 64 * (j + 1), 64 * (j + 1) + EC))
-        dma("s", T.yt[:, V * j:V * (j + 1)], A("ytb", 64 * j, 64 * j + EC))
-    tt(A("mh"), A("mk"), A("p2", 0, H), OP.mult)
-    cp(IND(A("mg"), A("rnl", 0, RC)), A("mh"))
-    cuts = (0, 100, 200, 400, 600, 764, V)
-    for c in range(6):
+        if j == 0:
+            act(A("mh"), A("p2", 0, H))
+    tt(IND(A("mg"), A("rnl", 0, RC)), A("mo"), A("mh"), OP.add)
+    cuts = (0, 90, 180, 390, 600, 700, 800, 864, V)
+    for c in range(8):
+        if c == 7:
+            for j in range(2):
+                act(A("ytb", 64 * j, 64 * j + EC), A("p7", 64 * (j + 1), 64 * (j + 1) + EC))
+                dma("s", T.yt[:, V * j:V * (j + 1)], A("ytb", 64 * j, 64 * j + EC))
         act(A("p%d" % c, 0, cuts[c + 1] - cuts[c]), A("mg", L + 4 * cuts[c], L + 4 * cuts[c + 1], 4))
-    for c in range(0, 6, 2):
+    for c in range(0, 8, 2):
         for k in (1, 2, 3):
             for h in range(2):
                 e0, e1 = cuts[c + h], cuts[c + h + 1]

from concourse.bass import DstId, RemoteDMATransfer
from concourse.mybir import AluOpType as OP, ActivationFunctionType as AF

N, V, B, CAP, RO = 8, 928, 48, 208, 5
H = (N - 1) * B
L = 4 * CAP
O0 = 32
H0 = O0 + V
ZC = H0 + CAP
AB, AS = ZC + 16, 224
RW = AB + AS * RO
FB = 2 * RW
MOFF = 4 * AB - 8
PC, EC, AC, LC, RC, TC = V // 4, V // 16, CAP // 16, L // 16, H // 16, (V + CAP) // 16
M1, BIG, BIGM = 1.5 * 2.0 ** 23, 8192.0, 16384.0
LATE = (3, 4)
OPT = {"q": "xim", "m": "dma", "ms": "mid", "mc": 2, "pe": "aqsn", "v": "02qs3cn4r", "e": 1, "soon0": 0, "halves": 0, "afail": 1}
F, BF, I32, U16 = "float32", "bfloat16", "int32", "uint16"
MASTERS = ("x1", "x2", "x4", "x16", "ti", "tiz", "nti", "tx", "dg", "tn", "tnb", "ta", "tlo", "tid", "tih", "tow", "tq", "tr",
           "tco", "tt4", "tdt", "dz", "dz2", "ea", "es", "ed", "e4", "en", "dts", "ncb", "blk", "up", "ul", "tf", "tac", "tpw", "dzl")

_SB = {
    "qq": (RW + FB + H, F), "mm": (4 * (FB + H) - MOFF, F), "zw": (RW, BF), "td": (128, I32), "tb": (288, BF), "qr": (2 * V, BF), "gw": (4 * V, BF),
    "st": (V, BF), "fail": (V, BF), "psb": (V, BF), "pz": (V, BF), "zq": (H0, BF), "lr": (2800, BF), "hz": (H, BF), "zh": (H, BF), "kz": (CAP, BF), "ze": (2 * CAP, BF),
    "zl0": (H, BF), "zl1": (H, BF), "bl0": (2 * H, F), "bl1": (2 * H, F), "ml0": (H, F), "ml1": (H, F),
    "zs": (H, BF), "bs": (2 * H, F), "ms": (H, F), "mo": (H, F), "mh": (H, F),
    "pt": (PC, I32), "rm": (24, I32), "tht": (4, F), "xb": (PC, I32), "col": (64, F), "coli": (16, I32), "r16": (16, F), "r4": (4, F),
    "tl": (3 * 80, I32), "ti32": (160, F), "sel": (2048, BF), "tm": (640, BF), "kc": (3 * LC, BF), "kr": (24, BF),
    "si": (PC, F), "w1": (PC, I32), "w2": (PC, F), "xf": (4 * PC, BF), "nbl": (PC, U16), "kk": (EC, F),
    "ri": (24, I32), "zrl": (24, U16), "brl": (48, U16), "mrl": (24, U16), "rnl": (24, U16), "rzl": (24, U16),
    "can": (64, BF), "sm": (256, F), "ol": (EC, U16), "ql": (32, U16), "rl": (32, U16), "al": (16, U16), "nl": (LC, U16), "pw": (H0 + CAP, BF), "pe": (CAP, BF),
    "il": (2 * LC, U16), "co": (4 * LC, BF), "cw": (6 * LC, F), "fg": (2 * LC, BF), "rdt": (2 * CAP, F),
    "qe": (2 * CAP, F), "qn": (2 * L, F), "ue": (L, F), "un": (L, F), "ss": (L, F), "ff": (8 + L, F), "mf": (8 + L, F), "cb": (2 * CAP, BF),
    "fl": (PC, U16), "yl": (EC, U16), "mg": (L + 4 * V + H, F), "yo": (V, F), "yq": (2 * V, F), "ytb": (128, F),
}
for _m in MASTERS:
    _SB[_m] = (160, BF)
SCRATCH = {k: ("sbuf", [128, v[0]], v[1]) for k, v in _SB.items()}
for _i in range(8):
    SCRATCH["p%d" % _i] = ("psum", [128, 512], F)
SEMAPHORES = (["cv", "ca", "ct", "cg", "zsent", "bsent", "msent", "ltd", "hq", "hm"] + ["za%d" % i for i in range(RO)] + ["zc%d" % i for i in range(RO)]
              + ["ba%d" % i for i in range(RO)] + ["bc%d" % i for i in range(RO)] + ["ma%d" % i for i in range(1, RO + 1)] + ["d%d" % i for i in range(15)])


def rank_program(g, core, T, topo):
    r = T.rank_of(core)
    if r is None:
        return
    nhi = B * (N - 1 - r)
    Q = {"v": g.vector, "a": g.scalar, "t": g.tensor, "s": g.sync, "g": g}
    ops, acc, total, nd = [], {}, {}, [0]

    def A(name, lo=0, hi=None, st=1, rows=None):
        hi = (512 if name not in _SB else _SB[name][0]) if hi is None else hi
        m = ((1 << (hi - lo)) - 1) << lo
        if st > 1:
            m = sum(1 << c for c in range(lo, hi, st))
        ap = T[name][:, lo:hi:st] if st > 1 else T[name][:, lo:hi] if rows is None else T[name][rows::16, lo:hi]
        return (ap, [(name, m)], [])

    def IND(w, off):
        return (w[0].indirect(off[0]), w[1], off[1])

    def add(q, fn, outs, ins, tok=None):
        me = {"q": q, "fn": fn, "deps": [], "tok": tok, "need": False}
        touch = [(x, True) for a in outs for x in a[1]] + [(x, False) for a in outs for x in a[2]]
        touch += [(x, False) for a in ins if isinstance(a, tuple) for x in a[1] + a[2]]
        for (name, m), wr in touch:
            bank = name not in _SB
            for (m2, wr2, op) in acc.get(name, []):
                if op is me or (tok is not None and op["tok"] is not None and op["tok"][0] == tok[0] and tok[0] in ("ltd", "hq", "hm")):
                    continue
                if bank and op["q"] != q:
                    me["deps"].append(op)
                elif (m & m2) and (wr or wr2) and not (q == "t" and op["q"] == "t"):
                    me["deps"].append(op)
        for (name, m), wr in touch:
            bank = name not in _SB
            old = acc.get(name, [])
            if wr:
                old = [x for x in old if (x[0] & ~m) and not (bank and x[2]["q"] != q)]
            else:
                old = [x for x in old if x[1] or x[2]["q"] != q or x[2]["tok"] is not None or (x[0] & ~m)]
            acc[name] = old + [(m, wr, me)]
        ops.append(me)
        return me

    def P(a):
        return a[0] if isinstance(a, tuple) else a

    def ts(out, x, s1, op0, s2=None, op1=None):
        if op1 is None:
            return add("v", lambda: g.vector.tensor_scalar(out[0], x[0], P(s1), None, op0), [out], [x, s1])
        return add("v", lambda: g.vector.tensor_scalar(out[0], x[0], P(s1), P(s2), op0, op1), [out], [x, s1, s2])

    def tt(out, x, y, op):
        return add("v", lambda: g.vector.tensor_tensor(out[0], x[0], y[0], op), [out], [x, y])

    def cp(out, x):
        return add("v", lambda: g.vector.tensor_copy(out[0], x[0]), [out], [x])

    def ms(out, c):
        return add("v", lambda: g.vector.memset(out[0], c), [out], [])

    def act(out, x, fn=AF.Copy, scale=1.0, bias=0.0):
        return add("a", lambda: g.scalar.activation(out[0], x[0], fn, bias=P(bias), scale=P(scale)), [out], [x, scale, bias])

    def mm(out, lt, rhs, start=True, stop=True):
        return add("t", lambda: g.tensor.matmul(out[0], lt[0], rhs[0], start, stop), [out], [lt, rhs])

    def iota(out, pattern, base, ch, small=False):
        if small:
            return add("g", lambda: g.iota(out[0], pattern, base, ch, allow_small_or_imprecise_dtypes=True), [out], [])
        return add("g", lambda: g.iota(out[0], pattern, base, ch), [out], [])

    def dma(q, out, x, sem=None):
        if sem is None:
            sem = "d%d" % nd[0]
            nd[0] += 1
        total[sem] = total.get(sem, 0) + 16
        tok = [sem, total[sem]]
        outs = [out] if isinstance(out, tuple) else []
        return add(q, lambda: Q[q].dma_start(P(out), P(x)).then_inc(T.sem[sem], 16), outs, [x], tok=tok)

    def plan(src, calls):
        rs = T.rank_of(src)
        peers = {d: T.cores[(rs + d) % N] for d in range(1, N)}
        far = [d for d in peers if topo.chip(peers[d]) != topo.chip(src)]
        near = [d for d in peers if d not in far]
        eng = topo.engines(src, peers[far[0]])
        res = []
        if calls == 1:
            spare, i, one = len(eng) - len(far), 0, {}
            for n, d in enumerate(far):
                k = 2 if n < spare else 1
                one[d] = eng[i:i + k]
                i += k
            res.append(one)
        else:
            for part in ([d for d in far if d not in LATE], [d for d in far if d in LATE]):
                k = len(eng) // len(part)
                res.append({d: eng[n * k:(n + 1) * k] for n, d in enumerate(part)})
        for n, d in enumerate(near):
            rest = [e for e in topo.engines(src, peers[d]) if e not in eng]
            k = len(rest) // len(near)
            res[0][d] = rest[n * k:(n + 1) * k]
        return res

    def exchange(src, dst, w, sem0, lsem, calls, sem1=None):
        sent, sems = [], (sem0, sem1 or sem0)
        for n, part in enumerate(plan(core, calls)):
            tr = []
            for d, es in part.items():
                rid, pid, _ = topo.addr(T.cores[(r + d) % N])
                tr.append(RemoteDMATransfer(dst_ids=[DstId(rid=rid, pnc=pid)], dma_engine_mask=sum(1 << e for e in es), remote_sem=T.sem[sems[n]],
                                            src=T[src][:, (d - 1) * w:d * w], dst=T[dst][:, (N - d - 1) * w:(N - d) * w]))
            total[lsem] = total.get(lsem, 0) + sum(len(x) for x in part.values())
            sent.append(add("g", lambda tr=tr: g.remote_dma_fused(tr, local_sem=T.sem[lsem]), [], [A(src, (d - 1) * w, d * w) for d in part], tok=[lsem, 0]))
        for x in sent:
            x["tok"][1] = total[lsem]
        came = [(sems[n], d, len(part[N - d])) for n in range(calls) for d in range(1, N)
                for part in [plan(T.cores[(r + d) % N], calls)[n]] if N - d in part]
        acc[dst] = []
        for sem in dict.fromkeys(sems):
            total[sem] = sum(x[2] for x in came if x[0] == sem)
            add(None, None, [A(dst, w * (x[1] - 1), w * x[1]) for x in came if x[0] == sem], [], tok=[sem, total[sem]])

    def C(i):
        return A("col", i, i + 1)

    def R(i):
        return A("r16", i, i + 1)

    def R4(i):
        return A("r4", i, i + 1)

    def win(name, s=0):
        return A(name, 16 - s, 144 - s)

    ident = win("ti")
    own = (O0, O0 + V)
    s0, s1 = B * (min(LATE) - 1), B * max(LATE)
    l0, l1 = B * (N - 1 - max(LATE)), B * (N - min(LATE))
    early = ((0, l0, 0), (l1, H, l0))
    late = ((l0, l1, H - (l1 - l0)),)

    def sides(c0, c1):
        return [x for x in ((c0, min(c1, nhi), -16), (max(c0, nhi), c1, 16)) if x[0] < x[1]]

    def shift(out, land, w, sem, c0=0, c1=H, c2=0, c3=0):
        moves = []
        for x0, x1, s in sides(c0, c1) + sides(c2, c3):
            for p0, p1 in ((0, 112), (112, 128)) if s < 0 else ((16, 128), (0, 16)):
                q0 = (p0 - s) % 128
                to, fro = A(out, w * x0, w * x1), A(land, w * x0, w * x1)
                moves.append(dma("s", (T[out][p0:p1, w * x0:w * x1],) + to[1:], (T[land][q0:q0 + p1 - p0, w * x0:w * x1],) + fro[1:], sem))
        for x in moves:
            x["tok"][1] = total[sem]

    def Zw(rnd):
        return A("zw", 0, AB + AS * rnd)

    def Qw(rnd, f=None):
        return A("qq", RW * (f or 0), RW * (1 if f is None else f) + AB + AS * rnd)

    def Mw(rnd=None):
        return A("mm") if rnd is None else A("mm", 0, 4 * (AB + AS * rnd) - MOFF)

    Zc = A("zw", 0, ZC)

    def send_z(rnd, eng, w):
        eng[0](A("zs", 0, s0), IND(w, A("zrl", 0, s0 // 16)))
        eng[1](A("zs", s1, H), IND(w, A("zrl", s1 // 16, RC)))
        eng[0](A("zs", s0, s1), IND(w, A("zrl", s0 // 16, s1 // 16)))
        exchange("zs", "zl%d" % (rnd % 2), B, "za%d" % rnd, "zsent", 2, "zc%d" % rnd)

    def list_q():
        for i in range(8):
            mm(A("p6", 0, 2 * RC), win("tq", 2 * i), A("zs", i, H, 8), i == 0, i == 7)
        ts(A("brl", 0, 2 * RC), A("p6", 0, 2 * RC), C(16), OP.add)

    def send_q(rnd, eng):
        eng(A("bs"), IND(Qw(rnd), A("brl", 0, 2 * RC)))
        exchange("bs", "bl%d" % (rnd % 2), 2 * B, "ba%d" % rnd, "bsent", 2, "bc%d" % rnd)

    def rim_records(bank="p7"):
        mm(A(bank, 0, RC), ident, A("kr", 0, RC), True, False)
        for i in range(16):
            mm(A(bank, 0, RC), win("tr", i), A("zs", i, H, 16), False, i == 15)

    def list_m(off=-MOFF, bank="p7"):
        ts(A("sm", 192, 192 + RC), A(bank, 0, RC), 4.0, OP.mult, float(off), OP.add)
        ts(A("mrl", 0, RC), A("sm", 192, 192 + RC), 0.0, OP.max)

    def send_m(rnd, eng, calls=1):
        eng(A("ms"), IND(Mw(rnd), A("mrl", 0, RC)))
        exchange("ms", "ml%d" % (rnd % 2), B, "ma%d" % rnd, "msent", calls)

    def gather_z(eng, c0, c1):
        eng(A("gw", 16 * c0, 16 * c1), IND(Zc, A("nbl", c0, c1)))

    parts = (("p0", 0, 320), ("p1", 320, 480), ("p2", 480, 784), ("p3", 784, V))
    if not OPT["halves"]:
        parts = (("p0", 0, 320), ("p1", 320, 640), ("p2", 640, 832), ("p3", 832, V))

    def rows_own(dz):
        for bank, e0, e1 in parts:
            mm(A(bank, 0, e1 - e0), ident, A("st", e0, e1), True, False)
            mm(A(bank, 0, e1 - e0), win(dz), A("zw", O0 + e0, O0 + e1), False, False)

    def rows_near(bank, e0, e1, ports=range(4)):
        for k in ports:
            mm(A(bank, 0, e1 - e0), win("dg", k), A("gw", 4 * e0 + k, 4 * e1, 4), False, k == 3)

    def msum(out, names, bank):
        for n, x in enumerate(names):
            mm(A(bank, 0, 160), ident, A(x), n == 0, n == len(names) - 1)
        act(A(out), A(bank, 0, 160))

    def eq(out, x, c, k=None):
        return ts(A(out), A(x), c, OP.is_equal) if k is None else ts(A(out), A(x), c, OP.is_equal, k, OP.mult)

    def cyclic(out, x, c, n):
        for lo, hi, s in ((16, 144, 0.0), (0, 16, n), (144, 160, -n)):
            ts(A(out, lo, hi), A(x, lo, hi), s, OP.add, c, OP.is_equal)

    PP, P16, PK, ODD, G16, G16K, G4, G41, G2, G1, MR, DT, KT, MC = (C(i) for i in range(14))

    ms(A("zw", O0, ZC), 0.0)
    dma("s", A("td", 0, EC), T.t0[:])
    dma("a", A("td", 64, 64 + EC), T.d0[:])
    dma("s", A("rm", 0, RC), T.rim[:])
    dma("a", A("pt"), T.port[:])
    iota(A("coli", 0, 2), [[0, 2]], 0, 1)
    iota(A("xb"), [[1, PC]], 0, 0)
    iota(A("x1"), [[1, 160]], -16, 0, True)
    iota(A("x2"), [[1, 80], [0, 2]], -8, 0, True)
    iota(A("x4"), [[1, 40], [0, 4]], -4, 0, True)
    iota(A("x16"), [[1, 10], [0, 16]], -1, 0, True)
    ms(A("zw", 0, O0), -100.0)
    for i, m in enumerate((15, 3, 1, 112)):
        ts(A("coli", 2 + 2 * i, 3 + 2 * i), A("coli", 0, 1), m, OP.bitwise_and)
    ts(C(14), A("coli", 2, 3), float(TC), OP.mult, float(O0), OP.add)
    cp(A("col", 0, 5), A("coli", 0, 10, 2))
    ts(A("tl", 0, TC), A("xb", 0, TC), C(14), OP.add)
    ts(A("r16"), A("xb", 0, 16), P16, OP.is_equal)
    ts(A("tl", 80, 80 + TC), A("tl", 0, TC), 4064, OP.bitwise_and)
    ts(A("tl", 160, 160 + TC), A("tl", 0, TC), 31, OP.bitwise_and)
    cp(A("tb", 0, TC), A("tl", 80, 80 + TC))
    cp(A("tb", 80, 80 + TC), A("tl", 160, 160 + TC))
    ltd = [dma("s", A("zw", O0, ZC, rows=row), A("tb", at, at + TC), "ltd") for row, at in ((2, 0), (3, 80), (8, 0), (12, 80))]
    cyclic("ti", "x1", PP, 128.0)
    cp(A("tb", 160, 160 + EC), A("td", 0, EC))
    cp(A("tb", 224, 224 + EC), A("td", 64, 64 + EC))
    ltd += [dma("s", A("zw", *own, rows=row), A("tb", at, at + EC), "ltd") for row, at in ((4, 160), (1, 224))]
    for x in ltd:
        x["tok"][1] = total["ltd"]
    dma("s", A("qr", 0, V), T.q0[:])
    dma("s", A("qr", V, 2 * V), T.q1[:])
    dma("s", A("tht", 0, 1), T.th[:])

    def aff(out, x, scale, bias=0.0):
        return act(out, x, AF.Identity, scale, bias)
    aff(C(15), PK, -1.0, P16)
    aff(MR, R(2), 1.0, R(3))
    aff(DT, R(0), 2.0, R(1))
    aff(MC, R(8), 1.0, R(12))
    aff(G2, G16, 0.5)
    aff(C(16), ODD, float(RW))
    aff(KT, DT, 1.0, R(4))
    aff(G1, G16, 0.0625)
    aff(C(17), R(2), 8.0, G16)
    aff(C(18), R(3), 4.0, R(2))
    aff(G4, G16, 0.25)
    aff(C(17), R(3), 12.0, C(17))
    aff(C(18), R(4), -1.0, C(18))
    aff(G41, G16, 0.25, 1.0)
    aff(C(17), R(4), 4.0, C(17))
    aff(C(20), KT, -1.0)
    aff(G16K, G16, 1.0, PK)
    ts(A("ri", 0, RC), A("rm", 0, RC), 2, OP.arith_shift_right)
    ts(A("r4"), A("xb", 0, 16, 4), C(15), OP.is_equal)
    ts(A("zrl", 0, RC), A("ri", 0, RC), float(O0), OP.add)
    ts(A("w1"), A("pt"), 2, OP.arith_shift_right)
    ts(A("p4", 0, PC), A("pt"), 4 * V - 0.5, OP.is_ge, -BIG, OP.mult)
    ts(A("si"), A("xb"), 16.0, OP.mult, P16, OP.add)
    ts(A("p5", 0, PC), A("pt"), 4 * V + nhi - 0.5, OP.is_ge, BIG, OP.mult)
    tt(A("w2"), A("w1"), A("p4", 0, PC), OP.add)
    for u in range(4):
        act(A("tm", 160 * u, 160 * u + 160), A("ti"), scale=R4(u))
    eq("tq", "x2", G2, MR)
    eq("blk", "x16", G1)
    send_z(0, (act, act), Zc)
    for out, step, ch, op in (("up", -1, 1, OP.is_gt), ("ul", 1, -1, OP.is_ge)):
        add("g", lambda out=out, step=step, ch=ch, op=op: g.affine_select(win(out)[0], win("blk")[0], [[step, 128]], op, 0.0, 0, ch), [win(out)], [win("blk")])
    ts(A("w1"), A("pt"), 3, OP.bitwise_and)
    ts(A("nbl"), A("w2"), float(O0), OP.add, 0.0, OP.max)
    tt(A("p5", 0, PC), A("si"), A("p5", 0, PC), OP.add)
    tt(A("xf", 3 * PC, 4 * PC), A("w1"), A("p4", 0, PC), OP.add)
    tt(A("xf", 0, PC), A("pt"), A("p5", 0, PC), OP.is_gt)
    list_q()
    act(A("qq", 0, 2 * RW, RW), A("r16", 0, 2), scale=0.0)
    aff(C(44), R(2), float(FB - O0))
    act(A("qq", O0, H0), A("qr", 0, V))
    act(A("qq", RW + O0, RW + H0), A("qr", V, 2 * V))
    send_q(0, act)
    ts(A("xf", 3 * PC, 4 * PC), A("xf", 3 * PC, 4 * PC), 0.0, OP.max)
    ts(A("xf", PC, 2 * PC), A("xf", 0, PC), -32.0, OP.mult)
    ts(A("p5", 0, PC), A("xf", 0, PC), 128.0, OP.mult)
    tt(A("xf", 2 * PC, 3 * PC), A("xf", 3 * PC, 4 * PC), A("p5", 0, PC), OP.add)

    def static_rows(j):
        for u in range(4):
            for f, row in enumerate((0, 8, 12)):
                s = 160 * u + 16 - (row - 4 * u)
                mm(A("p%d" % (2 + j), u, 2 * PC, 4), A("tm", s, s + 128), A("xf", f * PC + j * PC // 2, f * PC + (j + 1) * PC // 2), f == 0, f == 2)
    static_rows(0)
    static_rows(1)
    gather_z(act, 0, 50)
    ts(C(19), KT, 1.0, OP.min)
    ts(C(21), MC, R(4), OP.add, -1.0, OP.mult)
    eq("e4", "x4", G4, C(20))
    eq("dz2", "x4", G41, R(4))
    ts(A("en"), A("ti"), C(21), OP.mult)
    eq("ea", "x1", G16, KT)
    eq("es", "x1", C(17), C(18))
    ts(A("tiz"), A("ti"), C(19), OP.mult)
    ts(C(22), R4(0), BIG, OP.mult)
    ts(C(23), R4(0), -1.0, OP.mult, 1.0, OP.add)
    ts(C(24), R4(1), -8.0, OP.mult, R(1), OP.add)
    for c0, c1, at in early + late:
        ts(A("hz", at, at + c1 - c0), A("zw", O0 + c0, O0 + c1), MR, OP.mult, C(44), OP.add)
        i = at // 16 + (c0 == l0)
        cp(A("rzl", i, i + (c1 - c0) // 16), A("rm", c0 // 16, c1 // 16))
    cp(A("st", 0, 2 * PC), A("p2", 0, 2 * PC))
    gather_z(cp, 104, 170)
    cp(A("st", 2 * PC, V), A("p3", 0, 2 * PC))
    msum("dz", ("e4", "dz2", "en"), "p5")
    msum("dg", ("ea", "es"), "p4")
    gather_z(act, 50, 104)
    gather_z(cp, 170, PC)

    def lane_constants(part):
        if part == 0:
            act(A("lr", 0, CAP), A("zw", H0, H0 + CAP), AF.Identity, MR, C(24))
            act(A("ti32"), A("ti"))
            for f in range(2):
                act(A("qq", RW * f + H0, RW * f + ZC), A("qr", 0, CAP), scale=0.0)
            for i in range(6):
                act(A("sel", 128 * i, 128 * i + 128), win("blk"), scale=R(i))
            eq("tx", "x1", G16, C(22))
            ts(A("kk"), A("si", 0, EC), float(V), OP.add)
            ms(A("can", 0, 2), 0.0)
            ms(A("sm", 0, 2), 0.0)
            eq("tn", "x1", G16K, R4(1))
            ts(C(26), R4(3), 0.25, OP.mult, R4(2), OP.add)
            eq("e4", "x4", G4, DT)
            eq("tlo", "x1", G16K, R4(3))
            eq("tih", "x1", G16K, C(26))
            ms(A("kc", 0, LC), -0.375)
        elif part == 1:
            ts(C(27), R(0), 6.0, OP.mult)
            tt(C(28), R(0), R(1), OP.add)
            eq("tr", "x1", G16, MR)
            ts(C(27), R(1), 11.0, OP.mult, C(27), OP.add)
            ts(C(29), C(28), BIG, OP.mult, -BIG, OP.add)
            ts(C(30), C(28), 3.0 - BIG, OP.mult, BIG, OP.add)
            ts(C(27), R(2), float(AB - H0), OP.mult, C(27), OP.add)
            tt(C(29), C(29), R(1), OP.add)
            tt(C(30), C(30), DT, OP.subtract)
            for i in range(6, 12):
                ts(A("sel", 128 * i, 128 * i + 128), win("blk"), R(i), OP.mult)
        elif part == 2:
            msum("ta", ("tn", "e4"), "p0")
            for i in range(12, 16):
                act(A("sel", 128 * i, 128 * i + 128), win("blk"), scale=R(i))
        elif part == 10:
            lane_constants(4)
        elif part == 3:
            eq("tco", "x1", G16, MC)
            eq("ncb", "x2", G2, -1.0)
            ts(A("ri", 0, RC), A("rm", 0, RC), 3, OP.bitwise_and)
            ts(C(33), R(2), float(AS), OP.mult)
            ts(A("kr", 0, RC), A("ri", 0, RC), 0.25, OP.mult)
        elif part == 4:
            act(A("kz"), A("zw", H0, H0 + CAP), AF.Identity, MR, C(27))
            act(A("ed"), A("ti"), scale=MC)
            act(A("dts"), A("blk"), scale=DT)
            act(C(31), A("tht", 0, 1), scale=-1.0)
            act(A("mm", 0, 8), A("r16", 0, 8), scale=0.0)
        elif part == 5:
            ts(C(32), MR, 4.0, OP.mult)
            ms(A("kc", LC, 2 * LC), 0.0)
            eq("tow", "x4", G4, C(32))
            ts(A("kc", 2 * LC, 3 * LC), A("kc", LC, 2 * LC), PK, OP.add)
            ts(A("w1"), A("pt"), 4064, OP.bitwise_and)
        elif part == 9:
            ts(A("w1"), A("pt"), 31, OP.bitwise_and)
            tt(C(43), R4(0), R4(1), OP.add)
            cp(A("xf", PC, 2 * PC), A("w1"))
            eq("tpw", "x1", G16K, C(43))
            ms(A("pw", H0, H0 + CAP), -100.0)
        elif part == 6:
            act(A("tid"), A("tih"), scale=4.0)
            act(A("nti"), A("ti"), scale=-1.0)
            act(A("tnb"), A("tn"), scale=-BIGM)
            act(A("col", 34, 38), A("r4"), scale=-1.0)
            act(A("col", 38, 42), A("r4"), scale=CAP - 0.5)
            act(A("en"), A("en"), scale=-1.0)
        elif part == 11:
            msum("tf", ("tid", "tnb"), "p6")
            msum("dzl", ("dz", "en"), "p7")
        elif part == 7:
            eq("tt4", "x1", G16, R(4))
            eq("tdt", "x1", G16, DT)
            ts(A("rnl", 0, RC), A("rm", 0, RC), float(L), OP.add)
            tt(C(42), G4, PK, OP.add)
            ms(A("ff", 0, 8), 0.0)
            eq("tac", "x4", C(42), -4 * BIGM)
            ts(A("xf", 0, PC), A("w1"), float(L), OP.add)
        else:
            for j in range(2):
                for u in range(4):
                    for f in range(2):
                        s = 160 * u + 16 - 4 * (f - u)
                        mm(A("p%d" % (6 + j), u, 2 * PC, 4), A("tm", s, s + 128), A("xf", f * PC + j * PC // 2, f * PC + (j + 1) * PC // 2), f == 0, f == 1)
                act(A("pw", O0 + 2 * PC * j, O0 + 2 * PC * (j + 1)), A("p%d" % (6 + j), 0, 2 * PC))


    def W(i, n=1):
        return A("cw", LC * i, LC * (i + n))

    def CO(i):
        return A("co", LC * i, LC * (i + 1))

    def K(i, k, u=0, st=1):
        bank, at = ((4 + k, 0), (4 + k, 0), (4 + k, CAP), (k // 2, CAP * (k % 2)), (2 + k // 2, CAP * (k % 2)))[i]
        return A("p%d" % bank, at + u, at + CAP, st)

    def spread(i, ports=range(4)):
        for k in ports:
            for u in range(4):
                s = 128 * (4 * u + k)
                mm(K(i, k, u, 4), A("sel", s, s + 128), CO(i))

    def lanes(t, bank, at, start=True, stop=True, rows="lr"):
        for u in range(4):
            mm(A(bank, at, at + LC), win(t, 4 * u), A(rows, u, CAP, 4), start and u == 0, stop and u == 3)

    def put_m(rnd, c0=0, c1=LC):
        at = 4 * (AB + AS * rnd) - MOFF
        to, f = A("mm", at + 16 * c0, at + 16 * c1) if rnd < RO - 1 else A("un"), A("ff", 8 + 16 * c0, 8 + 16 * c1)
        if rnd:
            tt(to, IND(Mw(rnd), A("il", LC + c0, LC + c1)), f, OP.subtract)
        else:
            ts(to, f, -1.0, OP.mult)

    HC = CAP // 2
    hs = [(2 * CAP * h, 2 * CAP * (h + 1)) for h in range(2)]
    for rnd in range(RO):
        last = rnd == RO - 1
        zl, bl, ml = ("%s%d" % (x, rnd % 2) for x in ("zl", "bl", "ml"))
        rec = AB + AS * rnd
        rows_own("dzl" if last else "dz")
        ins = []
        for bank, pieces in (("p4", early), ("p5", late)):
            a0, a1 = pieces[0][2], pieces[-1][2] + pieces[-1][1] - pieces[-1][0]
            mm(A(bank, 0, a1 - a0), ident, A("hz", a0, a1), True, False)
            ins.append((bank, a0, a1, [(x0, x1, at + x0 - c0 - a0, s) for c0, c1, at in pieces for x0, x1, s in sides(c0, c1)]))
        for bank, a0, a1, todo in ins:
            for n, (x0, x1, at, s) in enumerate(todo):
                mm(A(bank, at, at + x1 - x0), win("tiz", s), A(zl, x0, x1), False, n == len(todo) - 1)
            (cp if a0 else act)(A("zh", a0, a1), A(bank, 0, a1 - a0))
            cp(IND(A("gw"), A("rzl", a0 // 16 + (a0 > 0), a1 // 16 + (a0 > 0))), A("zh", a0, a1))
        if rnd == 0:
            lane_constants(0)
        else:
            act(A("lr", 0, CAP), A("zw", H0, H0 + CAP), AF.Identity, MR, C(24))
            act(A("kz"), A("kz"), AF.Identity, 1.0, C(33))
            put_m(rnd - 1)
            list_m()
        if last:
            act(A("zq", *own), A("zw", *own), scale=R4(0))

        def failing(n):
            bank, e0, e1 = parts[n]
            act(A("fail", e0, e1), A(bank, 0, e1 - e0), AF.Relu, -1.0, 1.0)

        def rows_out(n):
            bank, e0, e1 = parts[n]
            act(A("psb", e0, e1), A(bank, 0, e1 - e0), AF.Copy, C(23))

        def rows_ym(n):
            bank, e0, e1 = parts[n]
            act(A("pz", e0, e1), A(bank, 0, e1 - e0), AF.Relu, 1.0, R4(1))

        def count(bank, c0, c1):
            for i in range(16):
                mm(A(bank, c0, c1), win("tx", i), A("fail", 16 * c0 + i, 16 * c1, 16), i == 0, i == 15)

        def ranks(bank, c0, c1):
            mm(A(bank, c0, c1), win("ul"), A("can", 1 + c0, 1 + c1), True, False)
            mm(A(bank, c0, c1), win("up"), A("can", c0, c1), False, True)

        def to_front(cnt, bank, c0, c1):
            tt(A("sm", 1 + c0, 1 + c1), A(cnt, c0, c1), A("kk", c0, c1), OP.min)
            tt(A("sm", 64 + c0, 64 + c1), A("sm", 1 + c0, 1 + c1), A("sm", c0, c1), OP.subtract)
            out, d0, d1, ini = A("sm", 128 + c0, 128 + c1), A("sm", 64 + c0, 64 + c1), A(bank, c0, c1), A("sm", 127 + c0, 128 + c0) if c0 else -1.0
            add("v", lambda: g.vector.tensor_tensor_scan(out[0], d0[0], d1[0], P(ini), OP.add, OP.add), [out], [d0, d1, ini])
            cp(A("ol", c0, c1), out)
            tt(IND(A("lr"), A("ol", c0, c1)), A("psb", 16 * c0, 16 * c1), A("zq" if last else "zw", O0 + 16 * c0, O0 + 16 * c1), OP.add)
        mid = parts[2][1] // 16
        if not OPT["halves"]:
            for n in range(4):
                rows_near(*parts[n])
                if OPT["afail"] and n != 2:
                    failing(n)
                else:
                    ts(A("fail", *parts[n][1:]), A(parts[n][0], 0, parts[n][2] - parts[n][1]), 0.5, OP.is_lt)
                if n == 0 or not OPT["afail"]:
                    rows_out(n)
            for n in range(1, 4):
                if OPT["afail"]:
                    rows_out(n)
            count("p6", 0, EC)
            if not last:
                lane_constants((1, 5, 7, 9)[rnd])
            ts(A("can", 1, 1 + EC), A("p6", 0, EC), 0.5, OP.is_lt)
            ranks("p7", 0, EC)
            to_front("p6", "p7", 0, EC)
            if last:
                for n in (2, 3, 0, 1):
                    rows_ym(n)
        else:
            for n in range(2):
                rows_near(*parts[n])
                failing(n)
            rows_near(*parts[2], ports=(0,))
            rows_out(0)
            rows_out(1)
            if rnd and OPT["ms"] == "early":
                send_m(rnd, act, OPT["mc"])
            count("p6", 0, mid)
            rows_near(*parts[2], ports=(1,))
            if not last:
                lane_constants((1, 5, 7, 9)[rnd])
            ts(A("can", 1, 1 + mid), A("p6", 0, mid), 0.5, OP.is_lt)
            ranks("p7", 0, mid)
            rows_near(*parts[2], ports=(2, 3))
            failing(2)
            rows_near(*parts[3])
            failing(3)
            to_front("p6", "p7", 0, mid)
            count("p5", mid, EC)
            rows_out(2)
            if last:
                rows_ym(0)
            act(A("can", 1 + mid, 1 + EC), A("p5", mid, EC), AF.Relu, -1.0, 1.0)
            ranks("p4", mid, EC)
            rows_out(3)
            if last:
                for n in (2, 3, 1):
                    rows_ym(n)
            to_front("p5", "p4", mid, EC)
        if rnd < 2:
            lane_constants((2, 6)[rnd])
        if last:
            for u in range(4):
                act(A("xf", 64 * u, 64 * u + EC), A("sm", 128, 128 + EC), AF.Relu, C(34 + u), C(38 + u))
        mm(A("p2", 0, LC), ident, A("kc", 0, LC), True, False)
        if rnd:
            mm(A("p3", 0, 2 * LC), ident, A("kc", LC, 3 * LC), True, False)
        if rnd == 0:
            lane_constants(10)
            lane_constants(3)
        if OPT["q"] == "dma":
            shift("yq", bl, 2, "hq")
            for f in range(2):
                act(A("qq", RW * f + FB, RW * f + FB + H), A("yq", f, 2 * H, 2))
        else:
            if rnd and OPT["ms"] == "mid":
                send_m(rnd, act, OPT["mc"])
            if OPT["q"] == "mix":
                shift("yq", bl, 2, "hq", l0, l1)
            if OPT["q"] == "xim":
                shift("yq", bl, 2, "hq", 0, l0, l1, H)
                for c0, c1, at in early:
                    for f in range(2):
                        act(A("qq", RW * f + FB + c0, RW * f + FB + c1), A("yq", 2 * c0 + f, 2 * c1, 2))
            for bank, (c0, c1, at) in zip(("p7", "p6", "p5"), {"pe": early + late, "mix": early, "xim": late}[OPT["q"]]):
                for x0, x1, s in sides(c0, c1):
                    mm(A(bank, 2 * (x0 - c0), 2 * (x1 - c0)), win("ti32", s), A(bl, 2 * x0, 2 * x1))
                for f in range(2):
                    act(A("qq", RW * f + FB + c0, RW * f + FB + c1), A(bank, f, 2 * (c1 - c0), 2))
        if rnd and OPT["ms"] == "late":
            send_m(rnd, act, OPT["mc"])
        if rnd and OPT["m"] == "dma":
            shift("mh", ml, 1, "hm")
        nn, aa = A("p0", 0, LC), A("p0", LC, 2 * LC)
        for x in OPT["pe"]:
            if x == "q":
                for i in range(8):
                    mm(A("p1", 0, 2 * AC), win("tq", 2 * i), A("lr", i, CAP, 8), i == 0, i == 7)
            elif x == "a":
                lanes("tn", "p0", 0)
                lanes("ta", "p0", LC)
            elif x == "s":
                lanes("tlo", "p7", 0)
            else:
                lanes("tih", "p2", 0, False)
        for x in OPT["v"]:
            if x == "q":
                ts(A("ql", 0, 2 * AC), A("p1", 0, 2 * AC), C(16), OP.add)
                act(A("qe"), IND(Qw(rnd), A("ql", 0, 2 * AC)))
            elif x == "r":
                cp(A("rl", 0, 2 * AC), A("p1", 0, 2 * AC))
            elif x == "n":
                ts(A("nl"), A("p2", 0, LC), M1, OP.add, M1, OP.subtract)
                for f in range(2):
                    act(A("qn", L * f, L * f + L), IND(A("qq", RW * f, RW * f + FB + H), A("nl")))
            elif x == "0":
                ts(W(0, 2), A("p0", 0, 2 * LC), 0.0, OP.max, -0.5, OP.mult)
            elif x == "2":
                tt(W(2), W(1), W(0), OP.subtract)
            elif x == "s":
                ts(CO(0), A("p7", 0, LC), 127.5, OP.is_lt, 0.5, OP.subtract)
            elif x == "3":
                tt(W(3), W(2), aa, OP.add)
            elif x == "c":
                tt(CO(1), W(2), CO(0), OP.mult)
                spread(1)
            elif x == "4":
                tt(W(4), W(3), nn, OP.subtract)
        tt(CO(2), W(4), CO(1), OP.mult)
        tt(CO(3), W(3), CO(1), OP.mult)
        q0e, q1e = A("qe", 0, 2 * CAP, 2), A("qe", 1, 2 * CAP, 2)
        for k in range(4):
            tt(A("ue", CAP * k, CAP * k + CAP), q0e, K(1, k), OP.mult)
            spread(2, (k,))
            if k == 1 and rnd:
                ts(A("fg", 0, LC), nn, -0.5, OP.is_gt, BIGM, OP.mult)
                ts(A("fg", LC, 2 * LC), nn, 0.5, OP.is_lt, BIGM, OP.mult)
        spread(3)
        if rnd:
            lanes("tid", "p3", 0, False, False)
            lanes("tow", "p3", LC, False, False)
            mm(A("p3", 0, 2 * LC), win("nti"), A("fg"), False, True)
        if last:
            for u in range(4):
                mm(A("p2", 160, 160 + PC), win("tf", 4 * u), A("pz", u, V, 4), u == 0, False)
            for u in range(4):
                mm(A("p2", 160 + u, 160 + PC, 4), win("tac"), A("xf", 64 * u, 64 * u + EC), False, u == 3)

        def side(u, x0, x1, f, scale, sq, between):
            def X(k):
                return A(u, CAP * k, CAP * k + CAP)
            for h in range(2):
                for k in ((2 * h, 2 * h + 1) if x0 else ()):
                    tt(X(k), x0(k), K(1, k), OP.mult)
                for k in (2 * h, 2 * h + 1):
                    tt(K(f, k), x1(k), K(f, k), OP.mult)
                between(h)
                for k in (2 * h, 2 * h + 1):
                    tt(X(k), X(k), K(f, k), OP.add)
                act(A(u, *hs[h]), A(u, *hs[h]), AF.Relu, scale)
                if x0 or not OPT["e"]:
                    act(sq(h), A(u, *hs[h]), AF.Square)
            if not x0 and OPT["e"]:
                for h in range(2):
                    act(sq(h), A(u, *hs[h]), AF.Square)

        def memories(h):
            if h == 0:
                if soon:
                    act(A("ze"), IND(Zw(rnd), A("rl", 0, 2 * AC)))
                if rnd:
                    ts(A("il"), A("p3", 0, 2 * LC), -float(MOFF), OP.add, 0.0, OP.max)
                if last:
                    ts(A("fl"), A("p2", 160, 160 + PC), -float(MOFF), OP.add, 0.0, OP.max)
            spread(0, (2 * h, 2 * h + 1))
        soon = last or (rnd == 0 and OPT["soon0"])
        side("ue", None, lambda k: q1e, 2, 0.125, lambda h: A("ue", *hs[h]), lambda h: None)
        side("un", lambda k: A("qn", k, L, 4), lambda k: A("qn", L + k, 2 * L, 4), 3, -0.125, lambda h: A("p%d" % (2 + h), 0, 2 * CAP), memories)
        zu = A("zw", rec, rec + CAP)
        q0p = A("p1", CAP, 2 * CAP)

        def rows_new(bank, at, j0, j1, stop):
            mm(A(bank, at, at + j1 - j0), ident, A("kz", j0, j1), True, False)
            mm(A(bank, at, at + j1 - j0), win("ea", 4), A("ze", 2 * j0, 2 * j1, 2), False, False)
            mm(A(bank, at, at + j1 - j0), win("ed"), A("ze", 2 * j0, 2 * j1, 2), False, stop)

        cols = A("p0", 0, AC)

        def columns():
            for i in range(16):
                mm(cols, win("tco", i), A("ze", 2 * i, 2 * CAP, 32), i == 0, i == 15)
        if rnd and OPT["m"] == "dma":
            act(A("mm", 4 * FB - MOFF, 4 * (FB + H) - MOFF, 4), A("mh"))
        elif rnd:
            for x0, x1, s in sides(0, H):
                mm(A("p1" if last else "p0", 128 + x0, 128 + x1), win("ti32", s), A(ml, x0, x1))
            act(A("mm", 4 * FB - MOFF, 4 * (FB + H) - MOFF, 4), A("p1" if last else "p0", 128, 128 + H))
        if last:
            columns()
            rows_new("p0", 256, 0, CAP, True)
            act(zu, A("p0", 256, 256 + CAP))
        if not soon:
            act(A("ze"), IND(Zw(rnd), A("rl", 0, 2 * AC)))
        act(q0p, q0e)
        if last:
            act(A("mg", L, L + 16 * 40), IND(Mw(), A("fl", 0, 40)))
        for h in range(2):
            for k in (2 * h, 2 * h + 1):
                tt(A("ss", CAP * k, CAP * k + CAP), A("ue", CAP * k, CAP * k + CAP), K(4, k), OP.add)
            for k in (2 * h, 2 * h + 1):
                tt(A("ff", 8 + k, 8 + L, 4), A("ss", CAP * k, CAP * k + CAP), K(0, k), OP.mult)
        if last:
            cp(A("al", 0, AC), cols)
            cp(IND(Zc, A("al", 0, AC)), zu)
            act(A("zs"), IND(Zc, A("zrl", 0, RC)))
            rim_records("p3")
            act(A("pe"), IND(A("pw"), A("al", 0, AC)))
            act(A("mg", L + 16 * 40, L + 16 * 100), IND(Mw(), A("fl", 40, 100)))
        for h in range(2):
            rows_new("p%d" % (4 + h), 0, HC * h, HC * h + HC, False)
        if not last:
            columns()
        mm(A("p2", 0, CAP), win("dts"), A("ze", 0, 2 * CAP, 2))
        act(A("rdt", 0, CAP), A("p2", 0, CAP), AF.Relu, -0.5, 1.25)
        act(A("rdt", CAP, 2 * CAP), A("rdt", 0, CAP), AF.Identity, 1.0, 0.25)
        if rnd in (2, 3):
            lane_constants(11 if rnd == 2 else 8)
        if last:
            put_m(rnd)
            list_m(8 - 4 * rec, "p3")
            ts(A("ms"), IND(A("ff"), A("mrl", 0, RC)), -1.0, OP.mult)
            exchange("ms", "ml%d" % (RO % 2), B, "ma%d" % RO, "msent", 2)
            for c0, c1 in ((100, 170), (170, PC)):
                act(A("mg", L + 16 * c0, L + 16 * c1), IND(Mw(), A("fl", c0, c1)))
            lanes("tpw", "p6", 0, rows="pe")
            for i in range(16):
                mm(A("p7", 0, EC), win("tr", i), A("zw", O0 + i, H0, 16), i == 0, i == 15)
        src = "mf" if rnd else "ff"
        if rnd:
            for h, (c0, c1) in enumerate(hs):
                tt(A("mf", 8 + c0, 8 + c1), IND(Mw(), A("il", LC // 2 * h, LC // 2 * (h + 1))), A("ff", 8 + c0, 8 + c1), OP.add)

        def q0n(j0, j1):
            return A("qq", rec + j0, rec + j1)
        for k in range(4):
            for h in range(2):
                j0, j1 = HC * h, HC * (h + 1)
                tt(q0n(j0, j1) if k == 3 else A("p1", j0, j1), A("p1", j0 + (0 if k else CAP), j1 + (0 if k else CAP)), A(src, 8 + 4 * j0 + k, 8 + 4 * j1, 4), OP.add)
        if not last:
            cp(A("al", 0, AC), cols)
        for h in range(2):
            j0, j1 = HC * h, HC * (h + 1)
            ts(A("cb", j0, j1), q0n(j0, j1), A("tht", 0, 1), OP.is_gt)
            ts(A("cb", CAP + j0, CAP + j1), q0n(j0, j1), C(31), OP.is_lt)
            mm(A("p%d" % (4 + h), 0, HC), win("ncb"), A("cb", j0, j1), False, False)
            mm(A("p%d" % (4 + h), 0, HC), win("ncb"), A("cb", CAP + j0, CAP + j1), False, True)

        def put_z():
            for h in range(2):
                ts(A("zw", rec + HC * h, rec + HC * h + HC), A("p%d" % (4 + h), 0, HC), C(29), OP.max, C(30), OP.min)
            cp(IND(Zc, A("al", 0, AC)), zu)

        def put_q():
            tt(A("p1", 0, CAP), q0n(0, CAP), q0p, OP.subtract)
            tt(A("qq", RW + rec, RW + rec + CAP), A("rdt", CAP, 2 * CAP), A("p1", 0, CAP), OP.mult)

        if not last:
            put_z()
            send_z(rnd + 1, (act, cp), Zc)
            gather_z(act, 0, 60)
            put_q()
            list_q()
            send_q(rnd + 1, cp)
            gather_z(act, 60, 110)
            gather_z(act, 110, 146)
            gather_z(cp, 146, 190)
            gather_z(cp, 190, PC)
            rim_records()

    ml = "ml%d" % (RO % 2)
    tt(W(0), A("si", 0, LC), A("p6", 0, LC), OP.max)
    cp(A("yl"), A("p7", 0, EC))
    cp(A("il", 0, LC), W(0))
    put_q()
    act(A("mo"), IND(A("mg"), A("rnl", 0, RC)))
    put_z()
    cp(IND(A("mg"), A("il", 0, LC)), A("un"))
    for x0, x1, s in sides(0, H):
        mm(A("p2", x0, x1), win("ti32", s), A(ml, x0, x1))
    for j, t in enumerate(("tt4", "tdt")):
        for i in range(16):
            mm(A("p7", 64 * (j + 1), 64 * (j + 1) + EC), win(t, i), A("zw", O0 + EC * i, O0 + EC * (i + 1)), i == 0, i == 15)
    for j in range(2):
        act(A("yq", V * j, V * j + V), IND(Qw(RO, j), A("yl")))
        dma("s", (T.y0, T.y1)[j][:], A("yq", V * j, V * j + V))
        if j == 0:
            act(A("mh"), A("p2", 0, H))
    tt(IND(A("mg"), A("rnl", 0, RC)), A("mo"), A("mh"), OP.add)
    cuts = (0, 90, 180, 390, 600, 700, 800, 864, V)
    for c in range(8):
        if c == 7:
            for j in range(2):
                act(A("ytb", 64 * j, 64 * j + EC), A("p7", 64 * (j + 1), 64 * (j + 1) + EC))
                dma("s", T.yt[:, V * j:V * (j + 1)], A("ytb", 64 * j, 64 * j + EC))
        act(A("p%d" % c, 0, cuts[c + 1] - cuts[c]), A("mg", L + 4 * cuts[c], L + 4 * cuts[c + 1], 4))
    for c in range(0, 8, 2):
        for k in (1, 2, 3):
            for h in range(2):
                e0, e1 = cuts[c + h], cuts[c + h + 1]
                y = A("p%d" % (c + h), 0, e1 - e0)
                tt(A("yo", e0, e1) if k == 3 else y, y, A("mg", L + 4 * e0 + k, L + 4 * e1, 4), OP.add)
        dma("sa"[c // 2 % 2], T.ym[:, cuts[c]:cuts[c + 2]], A("yo", cuts[c], cuts[c + 2]))

    for op in ops:
        for d in op["deps"]:
            d["need"] = True
    cnt = {}
    for op in ops:
        if op["tok"] is None and op["need"]:
            s = "c" + op["q"]
            cnt[s] = cnt.get(s, 0) + 1
            op["tok"] = [s, cnt[s]]
            op["inc"] = True
    seen = {q: {} for q in Q}
    for op in ops:
        q = op["q"]
        if q is None:
            continue
        want = {}
        for d in op["deps"]:
            s, v = d["tok"]
            want[s] = max(want.get(s, 0), v)
        for s, v in want.items():
            if seen[q].get(s, 0) < v:
                Q[q].wait_ge(T.sem[s], v)
                seen[q][s] = v
        ins = op["fn"]()
        if op.get("inc"):
            ins.then_inc(T.sem[op["tok"][0]], 1)
    total.update(cnt)
    for s, v in total.items():
        if seen["g"].get(s, 0) < v:
            g.wait_ge(T.sem[s], v)
